import numpy as np, ml_dtypes
CORES = [8,136,40,168]
N = 4
BF = ml_dtypes.bfloat16
def gentries(a):
    return np.ascontiguousarray(a.reshape(8, 16, -1).transpose(0, 2, 1)).reshape(8, -1)
def gtable(e):
    e = np.asarray(e); return np.ascontiguousarray(e.reshape(8, -1, 16).transpose(0, 2, 1)).reshape(128, -1).astype(np.int32)
V, H, RO, SQ, K = 1536, 256, 4, 4, 64
W = V + 2 * H; Z = 8 * N
def ring(a):
    return np.ascontiguousarray(np.swapaxes(a, 0, 1)).reshape((Z,) + a.shape[2:])
def unring(a):
    return np.ascontiguousarray(np.swapaxes(a.reshape((8, N) + a.shape[1:]), 0, 1))
def tiles(a):
    return np.ascontiguousarray(unring(a).transpose(0, 1, 3, 2)).reshape(N, 128, V)
def pack(x, lf, rt):
    return {"x0": (tiles(x).astype(np.float32) * np.float32(0.015625)).astype(BF), "lf": np.stack([gtable(a) for a in unring(lf)]), "rt": np.stack([gtable(a) for a in unring(rt)])}
def loose(rng):
    v = np.arange(H, H + V)
    return (rng.random((Z, V)) * v).astype(np.int64), v + 1 + (rng.random((Z, V)) * (W - 1 - v)).astype(np.int64)
def textures(rng, lf, rt, scale):
    B = V // 4; i = np.arange(4)
    prof = (rng.integers(0, 257, (K, 4, 16)) * scale).astype(np.int64); good = rng.integers(0, 5, K); amp = rng.choice(np.array([2, 8, 20, 40]), (K, 1, 1))
    lab = np.minimum((K * rng.random((Z, B)) ** 2).astype(np.int64), K - 1)
    x = prof[lab] + np.rint((2 * rng.random((Z, B, 4, 16)) - 1) * amp[lab]).astype(np.int64)
    for z in range(Z):
        o = np.argsort(lab[z], kind="stable"); a, b = o[:-1], o[1:]; s = lab[z][a] == lab[z][b]; a, b = a[s], b[s]
        g = good[lab[z][a]][:, None]; on = (g == i) | (g == 4); u = rng.random((a.size, 1))
        pa = 4 * a[:, None] + i; pb = 4 * b[:, None] + i
        m = on & (u > 0.04); rt[z, pa[m]] = H + pb[m]
        m = on & (u < 0.96); lf[z, pb[m]] = H + pa[m]
        y = (z + 1) % Z
        last = np.full(K, -1); last[lab[z]] = np.arange(B); first = np.full(K, B); first[lab[y][::-1]] = np.arange(B)[::-1]
        k = np.nonzero((last >= (V - H) // 4) & (first < H // 4))[0]
        g = good[k][:, None]; on = (g == i) | (g == 4); pa = 4 * last[k][:, None] + i; pb = 4 * first[k][:, None] + i
        rt[z, pa[on]] = H + V + pb[on]; lf[y, pb[on]] = H - V + pa[on]
    return np.clip(x, 0, 256).reshape(Z, V, 16)
def setup_inputs(rng):
    lf, rt = loose(rng); x = textures(rng, lf, rt, 1)
    return pack(x, lf, rt)
def setup_inputs_spread(rng):
    v = np.arange(H, H + V)
    lf = v - np.floor(np.power(1.0 * v, rng.random((Z, V)))).astype(np.int64)
    rt = v + np.floor(np.power(1.0 * (W - 1 - v), rng.random((Z, V)))).astype(np.int64)
    x = textures(rng, lf, rt, rng.choice(np.array([1.0, 0.5, 0.25]), (K, 1, 16), p=[0.5, 0.25, 0.25]))
    return pack(x * (rng.random((Z, V, 1)) > 0.03), lf, rt)
def setup_inputs_ends(rng):
    v = np.arange(H, H + V); near = np.zeros((Z, V), bool); n = V // 2 + 40
    for z in range(Z):
        runs = np.stack([rng.integers(1, 21, n), rng.integers(1, 51, n)], axis=1).reshape(-1); o = rng.integers(0, 40)
        near[z] = np.repeat(np.arange(2 * n) % 2 == 0, runs)[o:o + V]
        g = z // N
        if g % 2 == 0 or g == 7: near[z, 0] = True
        if g % 2 == 1: near[z, V - 1] = True
    near[Z - 1, V - 30:] = True
    arch = rng.integers(0, 2, 16); flip = rng.random((Z, V, 16)) < rng.choice(np.array([0.0, 0.1, 0.4]), (Z, V, 1))
    x = 256 * ((arch + rng.integers(0, 2, (Z, V, 1)) + flip) % 2)
    x = np.where(rng.random((Z, V, 1)) < 0.28, rng.integers(0, 257, (Z, V, 16)), x)
    return pack(x, np.where(near, v - 1, 0), np.where(near, v + 1, W - 1))
def setup_inputs_corners(rng):
    lf, rt = loose(rng); x = np.zeros((Z, V, 16), np.int64); T = 2 ** SQ
    sizes = [[1], [1, 2, 3], [3, 4, 5], [T - 1, T, T + 1, T + 2], [3 * T], [V], [1, 2, 3, 4, T, T + 1, 2 * T], [4]]
    for z in range(Z):
        k = np.array(sizes[(z // N + z % N) % 8]); n = rng.choice(k, V // int(k.min()) + 1)
        lab = np.empty(V, np.int64); lab[rng.permutation(V)] = np.repeat(np.arange(n.size), n)[:V]
        o = np.argsort(lab, kind="stable"); a, b = o[:-1], o[1:]; s = lab[a] == lab[b]; a, b = a[s], b[s]
        rt[z, a] = H + b; lf[z, b] = H + a
        amp = 40 if k[0] == V else 3
        x[z] = rng.integers(0, 257, (V, 16))[lab] + rng.integers(-amp, amp + 1, (V, 16))
    for z in range(Z):
        y = (z + 1) % Z
        if (z // N) % 2 == 0: rt[z, V - 1] = H + V; lf[y, 0] = H - 1
        else: rt[z, V - H] = W - 1; lf[y, H - 1] = 0
    return pack(np.clip(x, 0, 256), lf, rt)
def setup_inputs_crowd(rng):
    lf, rt = loose(rng); x = textures(rng, lf, rt, 1); v = np.arange(H, H + V); kind = rng.permutation(8)
    for z in range(Z):
        k = kind[z // N]
        if k < 2:
            j = rng.integers(0, V); a, b = lf[z, j], rt[z, j]; lf[z] = 0; rt[z] = W - 1
            if k == 1: lf[z, j] = a; rt[z, j] = b
        elif k == 2:
            rt[z] = np.where(v < H + V - 1, H + V - 1, W - 1); lf[z] = np.where(v > H, H, 0)
        elif k == 3:
            h = np.sort(H + rng.permutation(V)[:5])
            rt[z] = np.concatenate([h, [W - 1]])[np.searchsorted(h, v, side="right")]
            lf[z] = np.concatenate([[0], h])[np.searchsorted(h, v, side="left")]
    return pack(x, lf, rt)
def setup_inputs_calm(rng):
    lf, rt = loose(rng); x = textures(rng, lf, rt, 1); kind = rng.permutation(8)
    for z in range(Z):
        k = kind[z // N] % 4
        if k < 3: x[z] = (0, 253, 192)[k] + rng.integers(0, 4, (V, 16))
    return pack(x, lf, rt)
def check_ranges(d):
    bad = []; v = np.arange(H, H + V)
    x = np.asarray(d["x0"]).astype(np.float64)
    if not np.all((x >= 0) & (x <= 4)): bad.append("range of x0")
    elif np.any(x * 64 != np.floor(x * 64)): bad.append("x0 holds a number that is no multiple of 2**-6")
    elif np.min(np.mean(x.reshape(N, -1), axis=1)) < 1: bad.append("the mean of a rank's x0 is under 1")
    a = np.stack([gentries(e) for e in np.asarray(d["lf"])]).astype(np.int64); b = np.stack([gentries(e) for e in np.asarray(d["rt"])]).astype(np.int64)
    if np.min(a) < 0 or np.max(a) > H + V - 2: bad.append("range of lf")
    if np.any(a >= v): bad.append("an entry of lf isn't under its place")
    if np.min(b) < H + 1 or np.max(b) > W - 1: bad.append("range of rt")
    if np.any(b <= v): bad.append("an entry of rt isn't over its place")
    return bad
def pick(w, i):
    return w.reshape(-1, 16)[i + w.shape[1] * np.arange(Z)[:, None]]
def better(w, x, c, cur):
    c = np.where((c >= 0) & (c < W), c, cur)
    near = np.abs(pick(w, c) - x) < np.abs(pick(w, cur) - x)
    return np.where(np.add.reduce(near.astype(np.int64), axis=2) >= 9, c, cur)
def reference(x0, lf, rt):
    x = ring(np.asarray(x0).astype(np.float32).reshape(N, 8, 16, V).transpose(0, 1, 3, 2))
    l = ring(np.stack([gentries(a) for a in lf]).astype(np.int64)); r = ring(np.stack([gentries(a) for a in rt]).astype(np.int64))
    y = np.zeros((Z, V, 16)); own = np.arange(H, H + V)
    for t in range(RO):
        w = np.concatenate([np.roll(x, 1, axis=0)[:, V - H:], x, np.roll(x, -1, axis=0)[:, :H]], axis=1)
        if t % 2 == 0:
            cl = np.concatenate([np.roll(l, 1, axis=0)[:, V - 1:] - V, l[:, :V - 1]], axis=1) + 1
            cr = np.concatenate([np.roll(r, 1, axis=0)[:, V - 1:] - V, r[:, :V - 1]], axis=1) + 1
        else:
            cl = np.concatenate([l[:, 1:], np.roll(l, -1, axis=0)[:, :1] + V], axis=1) - 1
            cr = np.concatenate([r[:, 1:], np.roll(r, -1, axis=0)[:, :1] + V], axis=1) - 1
        l = better(w, x, cl, l); r = better(w, x, cr, r)
        rw = np.concatenate([np.roll(r, 1, axis=0)[:, V - H:] - V, r], axis=1)
        lw = np.concatenate([l, np.roll(l, -1, axis=0)[:, :H] + V], axis=1)
        back = np.where(np.take_along_axis(rw, l, 1) == own, l, own)
        end = np.take_along_axis(lw, r - H, 1) != own
        a = np.concatenate([np.tile(np.arange(H), (Z, 1)), back], axis=1); n = (a != np.arange(H + V)).astype(np.int64); m = np.ascontiguousarray(w[:, :H + V])
        for k in range(SQ):
            m = np.maximum(m, pick(m, a)); n = n + np.take_along_axis(n, a, 1); a = np.take_along_axis(a, a, 1)
        y = y + m[:, H:].astype(np.float64) * np.exp(-np.abs(x - pick(w, r)).astype(np.float64))
        go = end & (n[:, H:] >= 3)
        moved = np.minimum(np.maximum(x + np.float32(0.125) * (x - pick(w, a[:, H:])), np.float32(0)), np.float32(4))
        x = np.where(go[:, :, None], moved, x)
    return {"xe": tiles(x).astype(np.float32), "ye": tiles(y).astype(np.float32)}

def check_inputs(d):
    bad = list(check_ranges(d))
    if not bad:
        for name, y in reference(**d).items():
            for q in range(N):
                v = np.abs(np.asarray(y[q], np.float64)); s = np.sqrt(np.mean(v * v))
                if v.max() > 5 * s or s < 2.0 ** -1: bad.append('%s of rank %d is uneven or too small' % (name, q))
    return bad

@@ -1,0 +1,685 @@
+import math
+import numpy as np
+from concourse.bass import DstId, RemoteDMATransfer
+from concourse.mybir import AluOpType, AxisListType, ActivationFunctionType
+
+AL = AluOpType
+AF = ActivationFunctionType
+V, H, W, RO = 1536, 256, 2048, 4
+ZO = 1808
+ZW = 3872
+F, B, I, U = "float32", "bfloat16", "int32", "uint16"
+SCRATCH = {
+    "xb": ("sbuf", [128, V], B), "xr": ("sbuf", [128, H], B), "xl": ("sbuf", [128, 2 * H], B),
+    "lw": ("sbuf", [128, 192], I), "gs": ("sbuf", [128, 4], I), "gl": ("sbuf", [128, 4], I),
+    "wp": ("sbuf", [128, 400], B),
+    "ones": ("sbuf", [128, 256], B), "onef": ("sbuf", [128, 256], F), "rot": ("sbuf", [128, 256], F),
+    "ident": ("sbuf", [128, 128], B), "gsel": ("sbuf", [128, 16], B), "btmp": ("sbuf", [128, 144], B),
+    "bm": ("sbuf", [128, 2304], B), "cs": ("sbuf", [128, 912], B),
+    "ki": ("sbuf", [128, 8], I), "col": ("sbuf", [128, 8], F),
+    "v2": ("sbuf", [128, 416], F), "vw": ("sbuf", [128, 288], F), "sm": ("sbuf", [128, 672], F),
+    "pb": ("sbuf", [128, V], B), "pa": ("sbuf", [128, 1792], B), "tt": ("sbuf", [128, W], B),
+    "g1": ("sbuf", [128, V], B), "g2": ("sbuf", [128, V], B),
+    "a1": ("sbuf", [128, 1792], B), "a2": ("sbuf", [128, 1792], B), "a4": ("sbuf", [128, 1792], B), "a8": ("sbuf", [128, V], B),
+    "nl": ("sbuf", [128, V], B), "nr": ("sbuf", [128, V], B),
+    "lu": ("sbuf", [128, 5 * 960], U),
+    "dl": ("sbuf", [128, 2 * V], F), "ds": ("sbuf", [128, V], F), "ww": ("sbuf", [128, V], F),
+    "tm": ("sbuf", [128, V], F), "zc": ("sbuf", [128, V], F), "xs": ("sbuf", [128, H], F), "mf": ("sbuf", [128, V], F),
+    "pt": ("psum", [128, 2048], B),
+}
+for _k in range(4):
+    SCRATCH["z%d" % _k] = ("sbuf", [128, ZW], F)
+    SCRATCH["ll%d" % _k] = ("sbuf", [128, 272], B)
+    SCRATCH["lr%d" % _k] = ("sbuf", [128, 272], B)
+for _k in range(2):
+    SCRATCH["u%d" % _k] = ("sbuf", [128, 1792], F)
+    SCRATCH["dr%d" % _k] = ("sbuf", [128, 2 * V], F)
+    SCRATCH["m" + "ab"[_k]] = ("sbuf", [128, 1792], F)
+    SCRATCH["mc%d" % _k] = ("sbuf", [128, V], F)
+for _k in range(6):
+    SCRATCH["ps%d" % _k] = ("psum", [128, 512], F)
+SEMAPHORES = ["ev", "es", "ep", "eg"] + ["d%d" % k for k in range(110)] + ["%s%d" % (a, k) for a in ("a", "sn") for k in range(17)]
+
+SLOT = [0, 1, 10, 11, 2, 3, 4, 5, 6, 7, 8, 9]
+EL, ER, ED, EA, SR, SC, SP, SN, SD, EN, QQ = 0, 144, 288, 432, 576, 608, 640, 672, 704, 720, 864
+LL, LR, LD, LCL, LCR, LA1, LA2, LA4, LA8, LS = [96 * k for k in range(10)]
+TCOPY, ACOPY, CURCOPY = "s", "v", "s"
+TRIES, FB = 700, 32
+PLANS = {}
+P = {"g1": 256, "g2": 0, "a2": 0, "a4": 0, "a8": 0, "z8": 0, "de": "ss", "dr": "ss", "mc": 3,
+     "t0": "v", "t1": "v", "t2": "v", "t3": "v", "c0": "v", "c1": "v"}
+
+
+def models():
+    out = []
+    for ga, f, pe, lat, rem in ((1.56, 1.25, 0.55, 0.12, 3.5), (1.1, 1.1, 0.45, 0.08, 2.8), (2.0, 1.4, 0.9, 0.2, 4.5)):
+        out.append({"g": ga, "c": 0.00083 * f, "pe": 0.001 * pe, "lat": lat, "rem": rem})
+    return out
+
+
+def build(core, T, topo):
+    rank = T.rank_of(core)
+    n = len(T.cores)
+    left, right = T.cores[(rank - 1) % n], T.cores[(rank + 1) % n]
+    rotr, rotl = rank == n - 1, rank == 0
+    ops = []
+    nd, nx = [0], [0]
+
+    def R(name, a=0, b=None, s=1):
+        if b is None:
+            b = SCRATCH[name][1][1] if name in SCRATCH else V
+        return (name, a, b, s)
+
+    def A(r):
+        return T[r[0]][:, r[1]:r[2]:r[3]] if r[3] != 1 else T[r[0]][:, r[1]:r[2]]
+
+    def cnt(r):
+        return len(range(r[1], r[2], r[3]))
+
+    def X(x):
+        return A(x) if isinstance(x, tuple) else x
+
+    def op(eng, cost, fn, rd, wr, kind="c", sem=None, val=0, after=()):
+        ops.append({"e": eng, "cost": cost, "fn": fn, "rd": [r for r in rd if isinstance(r, tuple)], "wr": list(wr), "k": kind,
+                    "sem": sem, "val": val, "after": list(after)})
+        return len(ops) - 1
+
+    def two(*rs):
+        return all(SCRATCH[r[0]][2] in (B, U) for r in rs)
+
+    def ts(out, a, s1, s2, o0, o1=None):
+        def fn(q):
+            if o1 is None:
+                return [q.tensor_scalar(A(out), A(a), X(s1), None, o0)]
+            return [q.tensor_scalar(A(out), A(a), X(s1), X(s2), o0, o1)]
+        return op("v", ("e", cnt(a) * (0.5 if two(out, a) else 1)), fn, [a, s1, s2], [out])
+
+    def tt(out, a, b, o):
+        both = SCRATCH[a[0]][0] == "sbuf" and SCRATCH[b[0]][0] == "sbuf"
+        return op("v", ("e", cnt(a) * (2 if both else 1)), lambda q: [q.tensor_tensor(A(out), A(a), A(b), o)], [a, b], [out])
+
+    def cp(eng, out, a, bias=None):
+        if eng == "v":
+            if bias is not None:
+                return ts(out, a, bias, None, AL.add)
+            return op("v", ("e", cnt(a) * (0.5 if two(out, a) else 1)), lambda q: [q.tensor_copy(A(out), A(a))], [a], [out])
+        if bias is not None:
+            return act(out, a, AF.Identity, bias=bias)
+        return act(out, a, AF.Copy)
+
+    def act(out, a, f, bias=None, scale=None, off=None):
+        def fn(q):
+            kw = {}
+            if bias is not None:
+                kw["bias"] = X(bias)
+            if scale is not None:
+                kw["scale"] = scale
+            return [q.activation(A(out), A(a).indirect(A(off)) if off else A(a), f, **kw)]
+        return op("s", ("g" if off else "e", cnt(out)), fn, [a, bias, off], [out])
+
+    def gtt(out, win, off, b, o):
+        return op("v", ("g", cnt(out)), lambda q: [q.tensor_tensor(A(out), A(win).indirect(A(off)), A(b), o)], [win, off, b], [out])
+
+    def gcp(out, win, off, x):
+        o1, f1 = (out[0], out[1], out[1] + x, 1), (off[0], off[1], off[1] + x // 16, 1)
+        if x:
+            op("v", ("g", x), lambda q: [q.tensor_copy(A(o1), A(win).indirect(A(f1)))], [win, f1], [o1])
+        if x < cnt(out):
+            act((out[0], out[1] + x, out[2], 1), win, AF.Copy, off=(off[0], off[1] + x // 16, off[2], 1))
+
+    def ms(out, c):
+        return op("v", ("e", cnt(out) * (0.5 if two(out) else 1)), lambda q: [q.memset(A(out), c)], [], [out])
+
+    def red(out, a):
+        return op("v", ("e", cnt(a)), lambda q: [q.tensor_reduce(A(out), A(a), AxisListType.X, AL.add)], [a], [out])
+
+    def iota(out, pat, base, cm):
+        kw = {} if SCRATCH[out[0]][2] == I else {"allow_small_or_imprecise_dtypes": True}
+        return op("g", ("q", cnt(out)), lambda q: [q.iota(A(out), pat, base, cm, **kw)], [], [out])
+
+    def sel(out, a, pat, cmpop, base, cm):
+        return op("g", ("q", cnt(out)), lambda q: [q.affine_select(A(out), A(a), pat, cmpop, 0.0, base, cm)], [a], [out])
+
+    def mm(groups):
+        def fn(q):
+            last = []
+            for out, terms in groups:
+                for k, (l, r) in enumerate(terms):
+                    ins = q.matmul(A(out), A(l), A(r), k == 0, k == len(terms) - 1)
+                last.append(ins)
+            return last
+        c = sum(max(64, cnt(r)) * (4 if SCRATCH[r[0]][2] == F else 1) for out, terms in groups for l, r in terms)
+        return op("p", ("p", c), fn, [x for out, terms in groups for t in terms for x in t], [out for out, terms in groups], val=len(groups))
+
+    def tr(pairs):
+        return op("p", ("p", 128 * len(pairs)), lambda q: [q.transpose(A(o), A(a), A(R("ident"))) for o, a in pairs],
+                  [a for o, a in pairs] + [R("ident")], [o for o, a in pairs], val=len(pairs))
+
+    def dma(eng, pairs, rd, wr, nbytes, add=False):
+        s = "d%d" % nd[0]
+        nd[0] += 1
+
+        def fn(q):
+            if add:
+                return [q.dma_start(o, a, accum_op=AL.add) for o, a in pairs]
+            return [q.dma_start(o, a) for o, a in pairs]
+        return op(eng, ("d", len(pairs), nbytes * (2 if add else 1)), fn, rd, wr, kind="d", sem=s, val=16 * len(pairs))
+
+    def twin(dst, src):
+        return dma("y", [(A(dst), A(src))], [src], [dst], 512 * cnt(src))
+
+    def exchange(sides, nbytes):
+        k = nx[0]
+        nx[0] += len(sides)
+        eng = [topo.engines(core, x[0]) for x in sides]
+        m = len(eng[0]) // len(sides)
+
+        def fn(q):
+            trs = []
+            for j, (d, src, there, here) in enumerate(sides):
+                rid, pid = topo.addr(d, core)
+                mask = sum(1 << e for e in eng[j][j * m:(j + 1) * m])
+                trs.append(RemoteDMATransfer(dst_ids=[DstId(rid=rid, pnc=pid)], dma_engine_mask=mask, remote_sem=T.sem["a%d" % (k + j)], src=A(src), dst=A(there)))
+            q.remote_dma_fused(trs, local_sem=T.sem["sn%d" % k])
+            return []
+        o = op("g", ("r", nbytes), fn, [x[1] for x in sides], [], kind="s", sem="sn%d" % k, val=m * len(sides))
+        for j, x in enumerate(sides):
+            op(None, ("a",), None, [], [x[3]], kind="a", sem="a%d" % (k + j), val=m, after=[o])
+
+    def terms(e, tab, first, c0=0, c1=96):
+        return [(R("cs", e + 16 - i, e + 144 - i), R(tab, first + 16 * c0 + i, first + 16 * c1 + i - 15, 16)) for i in range(16)]
+
+    def ext(out, e, tab, first, c0=0, c1=96):
+        return mm([(out, terms(e, tab, first, c0, c1))])
+    bank, bank2 = ("ps5", "ps4"), ("ps2", "ps3")
+
+    def lst(t, c, a=0, b=96):
+        return R("lu", 960 * (t + 1) + c + a, 960 * (t + 1) + c + b)
+
+    def rot_pairs(dst, src, up):
+        if up:
+            return [(dst[16:128], src[0:112]), (dst[0:16], src[112:128])]
+        return [(dst[0:112], src[16:128]), (dst[112:128], src[0:16])]
+
+    dma("y", [(T.xb[:], T.x0[:])], [], [R("xb")], 393216)
+    srcl, srcr = R("xb", 0, H), R("xb", V - H, V)
+    if rotr:
+        dma("y", [(T.xr[16:128, :], T.x0[0:112, V - H:V]), (T.xr[0:16, :], T.x0[112:128, V - H:V])], [], [R("xr")], 65536)
+        srcr = R("xr")
+    if rotl:
+        dma("y", [(T.xr[0:112, :], T.x0[16:128, 0:H]), (T.xr[112:128, :], T.x0[0:16, 0:H])], [], [R("xr")], 65536)
+        srcl = R("xr")
+    dma("s", [(T.lw[:, 0:96], T.lf[:]), (T.lw[:, 96:192], T.rt[:])], [], [R("lw")], 98304)
+    if rotr:
+        pr = [(T.gs[16:128, 0:2], T.lf[0:112, 94:96]), (T.gs[0:16, 0:2], T.lf[112:128, 94:96]),
+              (T.gs[16:128, 2:4], T.rt[0:112, 94:96]), (T.gs[0:16, 2:4], T.rt[112:128, 94:96])]
+    else:
+        pr = [(T.gs[:, 0:2], T.lf[:, 94:96]), (T.gs[:, 2:4], T.rt[:, 94:96])]
+    dma("y", pr, [], [R("gs")], 65536)
+    exchange([(left, srcl, R("xl", H, 2 * H), R("xl", H, 2 * H)), (right, srcr, R("xl", 0, H), R("xl", 0, H))], 131072)
+    exchange([(right, R("gs"), R("gl"), R("gl"))], 16384)
+
+    ms(R("ones"), 1.0)
+    sel(R("ident"), R("ones", 0, 128), [[-1, 128]], AL.is_equal, 0, 1)
+    sel(R("btmp"), R("ones", 0, 144), [[-1, 16], [-16, 9]], AL.is_equal, 16, 1)
+    ms(R("bm"), 0.0)
+    cp("s", R("bm", 0, 2304, 16), R("btmp"))
+    ms(R("cs"), 0.0)
+    sel(R("gsel", 0, 8), R("ones", 0, 8), [[-16, 8]], AL.is_ge, 0, 1)
+    sel(R("gsel", 8, 16), R("gsel", 0, 8), [[16, 8]], AL.is_ge, 15, -1)
+    cp("s", R("cs", EA + 16, EA + 144, 16), R("gsel", 8, 16))
+    for j in (2, 3):
+        cp("s", R("cs", QQ + j, QQ + 34, 4), R("gsel", 8, 16))
+
+    def idn(a, s):
+        return R("ident", a, 128, s)
+
+    def c_(base, a, s, w=32):
+        return R("cs", base + a, base + w, s)
+    tt(c_(SC, 0, 1), idn(0, 4), idn(1, 4), AL.add)
+    tt(R("cs", EL + 16, EL + 144, 16), c_(SC, 0, 4), c_(SC, 1, 4), AL.add)
+    tt(R("cs", ER + 16, ER + 144, 16), c_(SC, 2, 4), c_(SC, 3, 4), AL.add)
+    for base, o_ in ((SP, AL.add), (SN, AL.subtract)):
+        act(c_(base, 0, 1), c_(SC, 0, 1), AF.Copy, scale=-1.0)
+        for j in (1, 3):
+            tt(c_(base, j, 4), c_(base, j, 4), idn(11, 16), o_)
+    tt(c_(SD, 0, 2, 16), c_(SC, 0, 4), idn(3, 16), AL.subtract)
+    tt(c_(SD, 1, 2, 16), c_(SC, 1, 4), idn(7, 16), AL.subtract)
+    ed = R("cs", ED + 16, ED + 144, 16)
+    act(R("gsel", 0, 8), idn(10, 16), AF.Copy, scale=1536.0)
+    act(R("btmp", 0, 8), idn(11, 16), AF.Copy, scale=-272.0)
+    tt(ed, idn(3, 16), idn(7, 16), AL.add)
+    tt(ed, ed, R("gsel", 0, 8), AL.add)
+    tt(R("cs", EN + 16, EN + 144, 16), R("cs", ER + 16, ER + 144, 16), R("btmp", 0, 8), AL.add)
+    KK, ONE, HI, BM, BP = [R("col", k, k + 1) for k in range(5)]
+    iota(R("ki", 0, 1), [[0, 1]], 0, 1)
+    ts(R("ki", 4, 5), R("ki", 0, 1), 15, None, AL.bitwise_and)
+    cp("v", KK, R("ki", 4, 5))
+    red(ONE, idn(11, 16))
+    red(HI, idn(0, 8))
+    act(BM, HI, AF.Copy, scale=-1536.0)
+    act(BP, HI, AF.Copy, scale=1536.0)
+    iota(R("v2", 0, 32), [[1280, 2], [128, 2], [0, 8]], 256, 1)
+    iota(R("v2", 32, 96), [[128, 8], [0, 8]], 512, 1)
+    iota(R("v2", 112, 208), [[128, 12], [0, 8]], 256, 1)
+    iota(R("v2", 208, 224), [[128, 2], [0, 8]], 0, 1)
+    iota(R("v2", 224, 416), [[128, 12], [0, 16]], 256, 1)
+    for j in range(2):
+        cp("s", c_(SR, j, 2, 16), R("cs", ER + 16, ER + 144, 16))
+    iota(R("vw", 192, 288), [[16, 96]], 256, 0)
+    act(R("vw", 0, 96), R("vw", 192, 288), AF.Identity, bias=KK)
+    ts(R("vw", 96, 192), R("vw", 192, 288), KK, float(ZO), AL.add, AL.add)
+    ms(R("pb"), 0.0)
+    ms(R("pa"), 0.0)
+    ms(R("pb", 11, V, 16), 1.0)
+    ts(R("pb", 3, V, 16), R("v2", 0, 96), KK, None, AL.subtract)
+    act(R("pb", 7, V, 16), R("v2", 0, 96), AF.Identity, bias=KK, scale=0.0)
+    ts(R("pa", 1, 1792, 16), R("v2", 112, 224), KK, None, AL.subtract)
+    act(R("pa", 2, 1792, 16), R("v2", 112, 224), AF.Identity, bias=KK, scale=0.0)
+    tr([(R("pt", 128 * b, 128 * b + 128), R("pa", V + 128 * b, V + 128 * b + 128)) for b in range(2)])
+    for a in ("a1", "a2", "a4"):
+        cp("s", R(a, 0, H), R("pt", 0, H))
+    if rotr or rotl:
+        ms(R("onef"), 1.0)
+        sel(R("rot"), R("onef"), [[0, 2], [-1, 128]], AL.is_equal, 0, 1)
+    for k in range(RO):
+        ms(R("z%d" % k, ZO - 16, ZO), 64.0)
+        ms(R("z%d" % k, ZO + W, ZW), 64.0)
+
+    s0 = 8.0 ** -RO
+    act(R("zc"), R("xb"), AF.Copy, scale=s0)
+    ts(R("z0", ZO + H, ZO + H + V), R("xb"), s0, None, AL.mult)
+    act(R("z0", ZO, ZO + H), R("xl", 0, H), AF.Copy, scale=s0)
+    ts(R("z0", ZO + H + V, ZO + W), R("xl", H, 2 * H), s0, None, AL.mult)
+    cp("v", lst(-1, LL), R("lw", 0, 96))
+    ts(lst(-1, LR), R("lw", 96, 192), -float(H), None, AL.add)
+    big = 1.5 * 2.0 ** 27
+    ts(R("wp", 0, 192), R("lw"), big, big, AL.add, AL.subtract)
+    tt(R("wp", 192, 384), R("lw"), R("wp", 0, 192), AL.subtract)
+    ts(R("wp", 384, 388), R("gl"), big, big, AL.add, AL.subtract)
+    tt(R("wp", 388, 392), R("gl"), R("wp", 384, 388), AL.subtract)
+    parts = [(0, 0), (4, 192), (8, 96), (12, 288)]
+
+    def bv(i, kk):
+        return R("bm", 144 * i + 16 - kk, 144 * i + 144 - kk)
+    for k in range(4):
+        p = "ps%d" % k
+        mm([(R(p, 96 * j, 96 * j + 96), [(bv(4 * k + j, kk), R("wp", c, c + 96)) for kk, c in parts]) for j in range(4)])
+        for j in range(4):
+            cp("s", R("tt", H + 4 * k + j, H + V, 16), R(p, 96 * j, 96 * j + 96), bias=ONE)
+    mm([(R("ps5", 0, 1), [(bv(15, kk), R("wp", c, c + 1)) for kk, c in ((0, 385), (4, 389), (8, 387), (12, 391))])])
+    act(R("col", 5, 6), HI, AF.Identity, bias=ONE, scale=-1536.0)
+    cp("s", R("tt", H - 1, H), R("ps5", 0, 1), bias=R("col", 5, 6))
+
+    def blk(tab, s, first=0):
+        return R(tab, first + 128 * SLOT[s], first + 128 * SLOT[s] + 128)
+
+    def prepare(t):
+        d = 1 if t % 2 == 0 else -1
+        ext(R("ps4", 144, 240), EL, "tt", H - d)
+        ext(R("ps4", 240, 336), EN, "tt", H - d)
+        ts(lst(t - 1, LCL, 0, 192), R("ps4", 144, 336), float(16 + d), float(H + V + 15), AL.add, AL.min)
+        mm([(R("ps3", 32 * s, 32 * s + 32), [(blk("tt", s, H), c_(SC, 0, 1))]) for s in range(12)])
+        cp(CURCOPY, R("pb", 0, V, 4), R("ps3", 0, 384))
+        mm([(R("ps2", 32 * s, 32 * s + 32), [(blk("tt", s, H - d), c_(SC, 0, 1)), (blk("tt", s, H), c_(SP if d > 0 else SN, 0, 1))]) for s in range(12)])
+
+    thirds = [(0, 512), (512, 1024), (1024, V)]
+
+    def ypart(t):
+        sc, tm = 8.0 ** (t - RO), "tm"
+        for ci, (a, b) in enumerate(thirds):
+            p = R("ps%d" % (ci % 2))
+            act(R("ds", a, b), R("dr%d" % (t % 2)), AF.Abs, off=lst(t, LD, a // 16, b // 16))
+            act(p, R("ds", a, b), AF.Exp, bias=-math.log(sc * (9.0 if t % 2 else 1.0)), scale=-1.0 / sc)
+            tt(R(tm, a, b), p, R("mf", a, b), AL.mult)
+            if t == RO - 1:
+                dma("g", [(T.ye[:, a:b], A(R(tm, a, b)))], [R(tm, a, b)], [R("ye", a, b)], 262144, add=True)
+        if t == 0:
+            dma("y", [(T.ye[:], A(R(tm)))], [R(tm)], [R("ye")], 786432)
+        elif t < RO - 1:
+            dma("g", [(T.ye[:], A(R(tm)))], [R(tm)], [R("ye")], 786432, add=True)
+
+    prepare(0)
+    chunks = [(0, H), (V - H, V), (H, 768), (768, V - H)]
+    for t in range(RO):
+        z, u, dr, ma, mb = "z%d" % t, "u%d" % (t % 2), "dr%d" % (t % 2), "ma", "mb"
+        zw = R(z, ZO, ZO + H + V)
+
+        def own(a=0, b=V):
+            return R("zc", a, b)
+        for a, b in ((0, 768), (768, V)):
+            act(R(u, H + a, H + b), R(z, ZO + H + a, ZO + H + b), AF.Copy, scale=-9.0)
+        if t % 2 == 0:
+            tab, t0 = z, ZO
+        else:
+            act(R(u, 0, H), R(z, ZO, ZO + H), AF.Copy, scale=-9.0)
+            tab, t0 = u, 0
+        wins = {LL: zw, LR: R(z, ZO + H, ZO + W), LCL: R(z, ZO - 16, ZO + H + V), LCR: R(z, ZO + H, ZW)}
+        for d_, lc, x in (("dl", LL, P["de"]), (dr, LR, P["dr"])):
+            for ci, (a, b) in enumerate([(V - H, V), (0, H)] + ([(H, V - H)] if x in ("vv", "ss") else chunks[2:])):
+                if x[max(ci - 2, 0)] == "s" and ci > 1:
+                    act(R(d_, a, b), wins[lc], AF.Copy, scale=-1.0, off=lst(t - 1, lc, a // 16, b // 16))
+                    dma("g", [(A(R(d_, a, b)), A(own(a, b)))], [own(a, b), R(d_, a, b)], [R(d_, a, b)], 512 * (b - a), add=True)
+                else:
+                    gtt(R(d_, a, b), wins[lc], lst(t - 1, lc, a // 16, b // 16), own(a, b), AL.subtract)
+                act(R(d_, a, b), R(d_, a, b), AF.Abs)
+        pk = [0]
+        ll, lr = "ll%d" % t, "lr%d" % t
+        for ci in (1, 0, 2, 3):
+            a, b = chunks[ci]
+            for d_, lc, nn in ((dr, LCR, "nr"), ("dl", LCL, "nl")):
+                p = R("ps%d" % (pk[0] % 2), 0, b - a)
+                pk[0] += 1
+                gtt(R(d_, V + a, V + b), wins[lc], lst(t - 1, lc, a // 16, b // 16), own(a, b), AL.subtract)
+                act(p, R(d_, V + a, V + b), AF.Abs)
+                tt(R(nn, a, b), p, R(d_, a, b), AL.is_lt)
+            a, b = ((0, 2), (2, 4), (4, 8), (8, 12))[ci]
+            mm([(R("ps3", 32 * s, 32 * s + 32), [(blk("nl", s), R("cs", QQ + 2, QQ + 34)), (blk("nr", s), R("cs", QQ, QQ + 32))]) for s in range(a, b)])
+            dec = R("pb", 128 * a + 2, 128 * b, 4)
+            ts(dec, R("ps3", 32 * a, 32 * b), 8.5, None, AL.is_gt)
+            tt(R("pb", 128 * a + 1, 128 * b, 4), R("ps2", 32 * a, 32 * b), dec, AL.mult)
+            if ci == 1:
+                exchange([(right, R("pb", H, 2 * H), R(ll, 16 * rotr, 16 * rotr + H), R(ll, 16 * rotl, 16 * rotl + H))], 65536)
+            if ci == 0:
+                exchange([(left, R("pb", 0, H), R(lr, 0, H), R(lr, 0, H))], 65536)
+        if rotl:
+            sel(R(ll, 0, 16), R(ll, 128, 144), [[0, 16]], AL.is_gt, 1, 0)
+            sel(R(ll, 128, 144), R(ll, 256, 272), [[0, 16]], AL.is_gt, 1, 0)
+        if rotr:
+            sel(R(lr, 256, 272), R(lr, 128, 144), [[0, 16]], AL.is_gt, 1, 0)
+            sel(R(lr, 128, 144), R(lr, 0, 16), [[0, 16]], AL.is_gt, 1, 0)
+        if t:
+            ypart(t - 1)
+        o = 16 * rotr
+        inv = {b: s for s, b in enumerate(SLOT)}
+        tr([(R("pt", H + 128 * b, H + 128 * b + 128), R("pb", 128 * inv[b], 128 * inv[b] + 128)) for b in range(6)])
+        cp(P["t0"], R("tt", H, 1024), R("pt", H, 1024))
+        tr([(R("pt", H + 128 * b, H + 128 * b + 128), R("pb", 128 * inv[b], 128 * inv[b] + 128)) for b in (10, 11)])
+        tr([(R("pt", 128 * b, 128 * b + 128), R(ll, 128 * b, 128 * b + 128)) for b in range(2)])
+        tr([(R("pt", H + V + 128 * b, H + V + 128 * b + 128), R(lr, o + 128 * b, o + 128 * b + 128)) for b in range(2)])
+        cp(P["t1"], R("tt", 0, H), R("pt", 0, H), bias=BM)
+        cp(P["t2"], R("tt", H + V, W), R("pt", H + V, W), bias=BP)
+        tr([(R("pt", H + 128 * b, H + 128 * b + 128), R("pb", 128 * inv[b], 128 * inv[b] + 128)) for b in range(6, 10)])
+        cp(P["t3"], R("tt", 1024, H + V), R("pt", 1024, H + V))
+        for h in range(2):
+            ext(R(bank[h], 96, 144), EL, "tt", H, 48 * h, 48 * h + 48)
+            cp("v", lst(t, LL, 48 * h, 48 * h + 48), R(bank[h], 96, 144))
+            mm([(R(bank2[h], 16 * b, 16 * b + 16), [(R("tt", H + 768 * h + 128 * b, H + 768 * h + 128 * b + 128), c_(SD, 0, 1, 16))]) for b in range(6)])
+        ext(R("ps5", 240, 336), ER, "tt", H)
+        ext(R("ps5", 336, 432), ED, "tt", H)
+        ts(lst(t, LR, 0, 192), R("ps5", 240, 432), -float(H), None, AL.add)
+        for h in range(2):
+            c0 = 768 * h
+            gcp(R("g1", c0, c0 + 768), R("tt", 0, H + V), lst(t, LL, 48 * h, 48 * h + 48), P["g1"])
+            mm([(R(bank2[h], 384 + 16 * b, 400 + 16 * b), [(R("g1", c0 + 128 * b, c0 + 128 * b + 128), c_(SR, 0, 1, 16))]) for b in range(6)])
+            mut = R("sm", 96 * h, 96 * h + 96)
+            tt(mut, R(bank2[h], 384, 480), R("v2", 224 + 96 * h, 320 + 96 * h), AL.is_equal)
+            tt(R("pa", c0, c0 + 768, 8), R(bank2[h], 0, 96), mut, AL.mult)
+            tr([(R("pt", H + c0 + 128 * b, H + c0 + 128 * b + 128), R("pa", c0 + 128 * b, c0 + 128 * b + 128)) for b in range(6)])
+            cp(P["c%d" % h], R("a1", H + c0, H + c0 + 768), R("pt", H + c0, H + c0 + 768))
+        for h in range(2):
+            gcp(R("g2", 768 * h, 768 * h + 768), R("tt", H, W), lst(t, LR, 48 * h, 48 * h + 48), P["g2"])
+        twin(R(z, 0, H), R(z, ZO, ZO + H))
+        dma("y", [(A(R(ma, 0, H)), A(R(tab, t0, t0 + H))), (A(R(mb, 0, H)), A(R(tab, t0, t0 + H)))], [R(tab, t0, t0 + H)], [R(ma, 0, H), R(mb, 0, H)], 262144)
+        if t % 2:
+            twin(R("mc0"), R(u, H, H + V))
+        halves = [(V // P["mc"] * j, V // P["mc"] * (j + 1)) for j in range(P["mc"])]
+        src = [(tab, t0), (ma, 0), (mb, 0), (ma, 0)]
+        dst = [(ma, H), (mb, H), (ma, H), ("mf", 0)]
+        tabs = ["a1", "a2", "a4", "a8"]
+        for k in range(4):
+            for h in range(2):
+                pa_ = R(bank[h], 48 * (k % 2), 48 * (k % 2) + 48)
+                ext(pa_, EA, tabs[k], H if k < 3 else 0, 48 * h, 48 * h + 48)
+                cp("v", lst(t, LA1 + 96 * k, 48 * h, 48 * h + 48), pa_)
+                if k == 1:
+                    cp("s", R("sm", 576 + 48 * h, 624 + 48 * h), pa_)
+                if k == 2:
+                    tt(R("sm", 288 + 48 * h, 336 + 48 * h), pa_, R("sm", 576 + 48 * h, 624 + 48 * h), AL.is_equal)
+                if k == 3:
+                    tt(R("sm", 480 + 48 * h, 528 + 48 * h), pa_, R("sm", 384 + 48 * h, 432 + 48 * h), AL.max)
+            for h in range(2):
+                c0 = 768 * h + (H if k != 2 else 0)
+                gcp(R(tabs[k + 1] if k < 3 else z, c0, c0 + 768), R(tabs[k]) if k < 3 else zw, lst(t, LA1 + 96 * k, 48 * h, 48 * h + 48), P[tabs[k + 1] if k < 3 else "z8"])
+            if k == 1:
+                ext(R("ps5", 144, 240), EL, "g2", 0)
+                tt(R("sm", 192, 288), R("ps5", 144, 240), R("vw", 0, 96), AL.is_equal)
+            if k == 2:
+                tt(R("sm", 288, 384), R("sm", 288, 384), R("sm", 192, 288), AL.max)
+                tt(R("sm", 384, 480), R("sm", 288, 384), R("vw", 96, 192), AL.mult)
+            if k == 3:
+                cp("v", lst(t, LS), R("sm", 480, 576))
+            sn, s_ = src[k]
+            dn, d_ = dst[k]
+            cn = "zc" if k == 0 and t % 2 == 0 else "mc%d" % (k % 2)
+            for a, b in halves:
+                gtt(R(dn, d_ + a, d_ + b), R(sn, s_, s_ + H + V), lst(t, LA1 + 96 * k, a // 16, b // 16), R(cn, a, b), AL.max)
+                if k < 3:
+                    twin(R("mc%d" % (1 - k % 2), a, b), R(dn, d_ + a, d_ + b))
+        if t < RO - 1:
+            prepare(t + 1)
+        top = 4.0 * 8.0 ** (t + 1 - RO)
+        lo, hi = (-top, 0.0) if t % 2 == 0 else (0.0, top)
+        nz = "z%d" % (t + 1)
+        for ci, (a, b) in enumerate(thirds if t == RO - 1 else chunks):
+            gtt(R("ww", a, b), R(z, 0, ZO + H + V), lst(t, LS, a // 16, b // 16), R(u, H + a, H + b), AL.add)
+            if t == RO - 1:
+                ts(R("z0", a, b), R("ww", a, b), lo, hi, AL.max, AL.min)
+                dma("y", [(T.xe[:, a:b], A(R("z0", a, b)))], [R("z0", a, b)], [R("xe", a, b)], 262144)
+                continue
+            ts(R(nz, ZO + H + a, ZO + H + b), R("ww", a, b), lo, hi, AL.max, AL.min)
+            twin(R("zc", a, b), R(nz, ZO + H + a, ZO + H + b))
+            if (ci == 0 and rotl) or (ci == 1 and rotr):
+                mm([(R("ps3", 0, H), [(R("rot", 112, 240) if rotr else R("rot", 16, 144), R("ww", a, b))])])
+                ts(R("xs"), R("ps3", 0, H), lo, hi, AL.max, AL.min)
+            gl_, gr_ = R(nz, ZO, ZO + H), R(nz, ZO + H + V, ZO + W)
+            if ci == 0:
+                exchange([(left, R("xs") if rotl else R(nz, ZO + H, ZO + 2 * H), gr_, gr_)], 131072)
+            if ci == 1:
+                exchange([(right, R("xs") if rotr else R(nz, ZO + V, ZO + V + H), gl_, gl_)], 131072)
+    ypart(RO - 1)
+    return ops
+
+
+def bits(r):
+    m = np.zeros(4864, np.uint8)
+    m[r[1]:r[2]:r[3]] = 1
+    return int.from_bytes(np.packbits(m).tobytes(), "big")
+
+
+def banks(o):
+    s = set()
+    for r in o["rd"] + o["wr"]:
+        if r[0] == "pt":
+            s.update(("pt", k) for k in range(r[1] // 1024, (r[2] - 1) // 1024 + 1))
+        elif r[0][:2] == "ps":
+            s.add((r[0], 0))
+    return s
+
+
+def depend(ops):
+    hist = {}
+    memo = {}
+    deps = []
+    for i, o in enumerate(ops):
+        d = set(o["after"])
+        new = []
+        for lst_, w in ((o["rd"], False), (o["wr"], True)):
+            for r in lst_:
+                if r not in memo:
+                    memo[r] = bits(r)
+                m = memo[r]
+                for j, wj, mj in hist.get(r[0], ()):
+                    if (w or wj) and (m & mj):
+                        d.add(j)
+                new.append((r[0], w, m))
+        for name, w, m in new:
+            h = hist.setdefault(name, [])
+            if w:
+                h[:] = [(j, wj, mj & ~m) for j, wj, mj in h if mj & ~m]
+            h.append((i, w, m))
+        d.discard(i)
+        deps.append(sorted(d))
+    return deps
+
+
+def times(o, m):
+    c = o["cost"]
+    if c[0] == "e":
+        x = 0.06 + max(64, c[1]) * m["c"]
+    elif c[0] == "g":
+        x = 0.06 + c[1] * m["g"] * m["c"]
+    elif c[0] == "q":
+        x = 0.17 + 2 * c[1] * m["c"]
+    elif c[0] == "p":
+        x = 0.05 + c[1] * m["pe"]
+    elif c[0] == "d":
+        i = c[1] * (1.0 if o["e"] == "g" else 0.1)
+        return i, i + 2.0 + c[2] / 400000.0
+    elif c[0] == "r":
+        return 0.6, 0.6 + m["rem"] * 0.5 + c[1] / 150000.0
+    else:
+        return 0.0, m["rem"] * 0.5
+    return x, x
+
+
+def plan(ops, deps, m, pr, slack, back=False):
+    n = len(ops)
+    tm_ = [times(o, m) for o in ops]
+    succ = [[] for o in ops]
+    for i, d in enumerate(deps):
+        for j in d:
+            succ[j].append(i)
+    if back:
+        deps, succ = succ, deps
+    bk = [o["bk"] for o in ops]
+    left = [len(d) for d in deps]
+    ready = {i: 0.0 for i in range(n) if not left[i]}
+    free = {}
+    last = {}
+    fin = [0.0] * n
+    order = []
+    extra = [[] for o in ops]
+    while ready:
+        est = {}
+        for i, r in ready.items():
+            e = ops[i]["e"]
+            s = max(r, free.get(e, 0.0) - (tm_[i][1] - tm_[i][0] if back else 0.0)) if e else r
+            for b in bk[i]:
+                for e2, j in last.get(b, {}).items():
+                    if e2 != e:
+                        s = max(s, fin[j] + m["lat"])
+            est[i] = s
+        i0 = min(est, key=lambda i: (est[i], -pr[i]))
+        i = max((j for j in est if ops[j]["e"] == ops[i0]["e"] and est[j] <= est[i0] + slack[i0]), key=lambda j: pr[j]) if ops[i0]["e"] else i0
+        e = ops[i]["e"]
+        for b in bk[i]:
+            extra[i] += [j for e2, j in last.get(b, {}).items() if e2 != e]
+            last.setdefault(b, {})[e] = i
+        if e:
+            free[e] = est[i] + tm_[i][1 if back else 0]
+        fin[i] = est[i] + tm_[i][1]
+        order.append(i)
+        del ready[i]
+        for j in succ[i]:
+            left[j] -= 1
+            if not left[j]:
+                ready[j] = max(fin[k] for k in deps[j]) + m["lat"]
+    return order, extra, fin
+
+
+def replay(ops, deps, extra, order, m):
+    free = {}
+    fin = {}
+    for i in order:
+        e = ops[i]["e"]
+        s = max([fin[j] + m["lat"] for j in deps[i] + extra[i]] + [free.get(e, 0.0) if e else 0.0])
+        a, b = times(ops[i], m)
+        if e:
+            free[e] = s + a
+        fin[i] = s + b
+    return max(fin.values())
+
+
+def arrange(ops):
+    deps = depend(ops)
+    ms_ = models()
+    rng = np.random.default_rng(7)
+    best = None
+    n = len(ops)
+    for o in ops:
+        o["bk"] = banks(o)
+    level = [0.0] * n
+    for i in range(n - 1, -1, -1):
+        level[i] += times(ops[i], ms_[0])[1] + ms_[0]["lat"]
+        for j in deps[i]:
+            level[j] = max(level[j], level[i])
+    fin = None
+    for k in range(TRIES):
+        if k < FB:
+            slack = np.full(n, [0.1, 0.2, 0.35, 0.5][(k // 8) % 4])
+            noise = np.array(level if k % 8 == 0 else plan(ops, deps, ms_[0], fin, slack.tolist(), True)[2])
+        else:
+            noise, slack = best[4].copy(), best[5].copy()
+            a = int(rng.integers(0, n))
+            pick = (rng.random(n) < 0.3) & (np.abs(np.arange(n) - a) < int(rng.choice([10, 40, 120])))
+            noise[pick] += rng.normal(0.0, float(rng.choice([0.3, 1.0, 3.0])), n)[pick]
+            slack[pick] = rng.choice([0.05, 0.2, 0.5, 1.0], n)[pick]
+        order, extra, fin = plan(ops, deps, ms_[0], noise.tolist(), slack.tolist())
+        ts_ = [replay(ops, deps, extra, order, m) for m in ms_]
+        score = ts_[0] / 1.0 + ts_[1] / 0.75 + ts_[2] / 1.4
+        if best is None or score <= best[0]:
+            best = (score, order, extra, ts_, noise, slack)
+    return deps, best
+
+
+def rank_program(g, core, T, topo):
+    if T.rank_of(core) is None:
+        return
+    ops = build(core, T, topo)
+    key = tuple((o["e"], o["cost"], tuple(o["wr"])) for o in ops)
+    if key not in PLANS:
+        PLANS[key] = arrange(ops)
+    deps, best = PLANS[key]
+    order, extra = best[1], best[2]
+    Q = {"v": g.vector, "s": g.scalar, "p": g.tensor, "g": g, "y": g.sync}
+    known = {e: {} for e in Q}
+    total = {}
+    tok = {}
+    clock = {}
+    for i in order:
+        o = ops[i]
+        e = o["e"]
+        if o["k"] == "a":
+            tok[i] = (o["sem"], o["val"])
+            total[o["sem"]] = o["val"]
+            clock[i] = {o["sem"]: o["val"]}
+            continue
+        kn = known[e]
+        need = {}
+        for j in sorted(set(deps[i] + extra[i]), key=lambda j: -len(clock[j])):
+            s, v = tok[j]
+            if kn.get(s, 0) < v:
+                need[s] = max(need.get(s, 0), v)
+                for s2, v2 in clock[j].items():
+                    if kn.get(s2, 0) < v2:
+                        kn[s2] = v2
+        for s, v in need.items():
+            Q[e].wait_ge(T.sem[s], v)
+        ins = o["fn"](Q[e])
+        if o["k"] == "c":
+            s = "e" + e
+            for x in ins:
+                x.then_inc(T.sem[s], 1)
+            total[s] = total.get(s, 0) + len(ins)
+            tok[i] = (s, total[s])
+        else:
+            for x in ins:
+                x.then_inc(T.sem[o["sem"]], 16)
+            total[o["sem"]] = o["val"]
+            tok[i] = (o["sem"], o["val"])
+        clock[i] = dict(kn)
+        clock[i][tok[i][0]] = tok[i][1]
+    for s, v in total.items():
+        if known["g"].get(s, 0) < v:
+            g.wait_ge(T.sem[s], v)

@@ -6,69 +6,86 @@ from concourse.mybir import AluOpType, AxisListType, ActivationFunctionType
 AL = AluOpType
 AF = ActivationFunctionType
 V, H, W, RO = 1536, 256, 2048, 4
-ZO = 1808
-ZW = 3872
+ZO, Z8, ZW = 16, 2080, 3872
 F, B, I, U = "float32", "bfloat16", "int32", "uint16"
 SCRATCH = {
-    "xb": ("sbuf", [128, V], B), "xr": ("sbuf", [128, H], B), "xl": ("sbuf", [128, 2 * H], B),
-    "lw": ("sbuf", [128, 192], I), "gs": ("sbuf", [128, 4], I), "gl": ("sbuf", [128, 4], I),
-    "wp": ("sbuf", [128, 400], B),
-    "ones": ("sbuf", [128, 256], B), "onef": ("sbuf", [128, 256], F), "rot": ("sbuf", [128, 256], F),
+    "xb": ("sbuf", [128, V], B), "xr": ("sbuf", [128, 2 * H], B),
+    "lw": ("sbuf", [128, 192], I), "gl": ("sbuf", [128, 100], I),
+    "wp": ("sbuf", [128, 400], B), "wb": ("sbuf", [128, V], B),
+    "ones": ("sbuf", [128, 256], B), "id2": ("sbuf", [128, 256], B), "mvb": ("sbuf", [128, 512], B), "mvf": ("sbuf", [128, 512], F),
     "ident": ("sbuf", [128, 128], B), "gsel": ("sbuf", [128, 16], B), "btmp": ("sbuf", [128, 144], B),
-    "bm": ("sbuf", [128, 2304], B), "cs": ("sbuf", [128, 912], B),
+    "bm": ("sbuf", [128, 2416], B), "cs": ("sbuf", [128, 912], B),
     "ki": ("sbuf", [128, 8], I), "col": ("sbuf", [128, 8], F),
     "v2": ("sbuf", [128, 416], F), "vw": ("sbuf", [128, 288], F), "sm": ("sbuf", [128, 672], F),
-    "pb": ("sbuf", [128, V], B), "pa": ("sbuf", [128, 1792], B), "tt": ("sbuf", [128, W], B),
+    "pb": ("sbuf", [128, V], B), "pa": ("sbuf", [128, 1792], B), "tt": ("sbuf", [128, W + 16], B), "gu": ("sbuf", [128, 8], U),
     "g1": ("sbuf", [128, V], B), "g2": ("sbuf", [128, V], B),
     "a1": ("sbuf", [128, 1792], B), "a2": ("sbuf", [128, 1792], B), "a4": ("sbuf", [128, 1792], B), "a8": ("sbuf", [128, V], B),
     "nl": ("sbuf", [128, V], B), "nr": ("sbuf", [128, V], B),
     "lu": ("sbuf", [128, 5 * 960], U),
     "dl": ("sbuf", [128, 2 * V], F), "ds": ("sbuf", [128, V], F), "ww": ("sbuf", [128, V], F),
-    "tm": ("sbuf", [128, V], F), "zc": ("sbuf", [128, V], F), "xs": ("sbuf", [128, H], F), "mf": ("sbuf", [128, V], F),
-    "pt": ("psum", [128, 2048], B),
+    "tm": ("sbuf", [128, V], F), "zc": ("sbuf", [128, V], F), "xs": ("sbuf", [128, 2 * H], F), "mf": ("sbuf", [128, V], F),
+    "u0": ("sbuf", [128, 1792], F), "u1": ("sbuf", [128, 1792], F),
+    "lx": ("sbuf", [128, 144], B), "vn": ("sbuf", [128, 192], B),
+    "pt": ("psum", [128, 2048], B), "ps": ("psum", [128, 3072], F),
 }
 for _k in range(4):
-    SCRATCH["z%d" % _k] = ("sbuf", [128, ZW], F)
+    SCRATCH["z%d" % _k] = ("sbuf", [128, ZW], F if _k else B)
     SCRATCH["ll%d" % _k] = ("sbuf", [128, 272], B)
     SCRATCH["lr%d" % _k] = ("sbuf", [128, 272], B)
 for _k in range(2):
-    SCRATCH["u%d" % _k] = ("sbuf", [128, 1792], F)
     SCRATCH["dr%d" % _k] = ("sbuf", [128, 2 * V], F)
     SCRATCH["m" + "ab"[_k]] = ("sbuf", [128, 1792], F)
     SCRATCH["mc%d" % _k] = ("sbuf", [128, V], F)
-for _k in range(6):
-    SCRATCH["ps%d" % _k] = ("psum", [128, 512], F)
-SEMAPHORES = ["ev", "es", "ep", "eg"] + ["d%d" % k for k in range(110)] + ["%s%d" % (a, k) for a in ("a", "sn") for k in range(17)]
+SEMAPHORES = ["ev", "es", "ep", "eg"] + ["d%d" % k for k in range(110)] + ["%s%d" % (a, k) for a in ("a", "sn") for k in range(18)]
 
-SLOT = [0, 1, 10, 11, 2, 3, 4, 5, 6, 7, 8, 9]
-EL, ER, ED, EA, SR, SC, SP, SN, SD, EN, QQ = 0, 144, 288, 432, 576, 608, 640, 672, 704, 720, 864
+EL, ER, ED, EA, SR, SC, SP, SN, SD, EN, QQ, SV = 0, 144, 288, 432, 576, 608, 640, 672, 704, 720, 864, 592
 LL, LR, LD, LCL, LCR, LA1, LA2, LA4, LA8, LS = [96 * k for k in range(10)]
-TCOPY, ACOPY, CURCOPY = "s", "v", "s"
-TRIES, FB = 700, 32
+TRIES, FB, SWAPS, HEAT = 2500, 32, 16000, 0.3
 PLANS = {}
-P = {"g1": 256, "g2": 0, "a2": 0, "a4": 0, "a8": 0, "z8": 0, "de": "ss", "dr": "ss", "mc": 3,
-     "t0": "v", "t1": "v", "t2": "v", "t3": "v", "c0": "v", "c1": "v"}
+T3 = [(1024, V), (512, 1024), (0, 512)]
+P = {
+    "split": 512,
+    "rs": 0,
+    "curR": [(0, 512, "v"), (512, 1024, "s"), (1024, V, "v")], "canR": [(0, 512, "v"), (512, 1024, "s"), (1024, V, "v")],
+    "curL": [(0, 512, "v"), (512, 1024, "p"), (1024, V, "p")], "canL": [(0, 512, "v"), (512, 1024, "s"), (1024, V, "v")],
+    "seq": "R2 R0 L0 R1 L1 L2 Y0 Y1 Y2",
+    "dec": [("R", 8, 12), ("RL", 0, 4), ("RL", 4, 8), ("L", 8, 12)],
+    "ww": [(0, 512, "p"), (1024, V, "q"), (512, 1024, "p")],
+    "wwl": [(0, 512, "v"), (512, 1024, "v"), (1024, V, "v")],
+    "wwu": [(0, 512, "v"), (1280, V, "v"), (512, 1024, "v"), (1024, 1280, "v")],
+    "scale": [1.0, -8.0 ** -3, 8.0 ** -2, -8.0 ** -1, 1.0],
+    "twin": "yyyy", "twl": "yyy",
+    "g1e": 1, "g2": [(0, 512, "s"), (512, 1280, "s"), (1280, V, "s")],
+    "g1.0": (0, 512), "a2.0": (0, 512), "a4.0": (0, 512), "a8.0": (0, 512), "z8.0": (0, 512),
+    "g1": (0, 0), "a2": (0, 0), "a4": (0, 0), "a8": (0, 0), "z8": (0, 0),
+    "mc": T3[::-1], "ds": T3[::-1], "u": [(0, 768), (768, V)],
+    "ld": 1, "mut": 0, "y3": 0, "ls": 2, "mcl": T3[::-1], "t": "vvvv", "c": "vv", "cur": "s",
+}
+
+
+def of(key, t):
+    return P.get("%s.%d" % (key, t), P[key])
 
 
 def models():
     out = []
-    for ga, f, pe, lat, rem in ((1.56, 1.25, 0.55, 0.12, 3.5), (1.1, 1.1, 0.45, 0.08, 2.8), (2.0, 1.4, 0.9, 0.2, 4.5)):
-        out.append({"g": ga, "c": 0.00083 * f, "pe": 0.001 * pe, "lat": lat, "rem": rem})
+    for ga, f, pe, lat, rem, row, w in ((1.56, 1.0, 0.55, 0.07, 2.8, 0.03, 1.0), (1.15, 1.05, 0.43, 0.07, 2.5, 0.02, 0.92),
+                                        (1.85, 1.3, 0.55, 0.12, 3.5, 0.05, 1.33), (1.4, 1.15, 0.92, 0.09, 3.0, 0.03, 1.2)):
+        out.append({"g": ga, "c": 0.00083 * f, "pe": 0.001 * pe, "lat": lat, "rem": rem, "row": row, "w": w})
     return out
 
 
-def build(core, T, topo):
-    rank = T.rank_of(core)
-    n = len(T.cores)
+def build(core, T, topo, both=False):
+    rank, n = T.rank_of(core), len(T.cores)
     left, right = T.cores[(rank - 1) % n], T.cores[(rank + 1) % n]
-    rotr, rotl = rank == n - 1, rank == 0
+    rotr, rotl = both or rank == n - 1, both or rank == 0
     ops = []
-    nd, nx = [0], [0]
+    nd, nx, sent = [0], [0], []
 
     def R(name, a=0, b=None, s=1):
         if b is None:
             b = SCRATCH[name][1][1] if name in SCRATCH else V
-        return (name, a, b, s)
+        return (name, a + 16, b + 16, s) if name == "tt" else (name, a, b, s)
 
     def A(r):
         return T[r[0]][:, r[1]:r[2]:r[3]] if r[3] != 1 else T[r[0]][:, r[1]:r[2]]
@@ -140,12 +157,12 @@ def build(core, T, topo):
     def sel(out, a, pat, cmpop, base, cm):
         return op("g", ("q", cnt(out)), lambda q: [q.affine_select(A(out), A(a), pat, cmpop, 0.0, base, cm)], [a], [out])
 
-    def mm(groups):
+    def mm(groups, start=True, stop=True):
         def fn(q):
             last = []
             for out, terms in groups:
                 for k, (l, r) in enumerate(terms):
-                    ins = q.matmul(A(out), A(l), A(r), k == 0, k == len(terms) - 1)
+                    ins = q.matmul(A(out), A(l), A(r), start and k == 0, stop and k == len(terms) - 1)
                 last.append(ins)
             return last
         c = sum(max(64, cnt(r)) * (4 if SCRATCH[r[0]][2] == F else 1) for out, terms in groups for l, r in terms)
@@ -183,6 +200,8 @@ def build(core, T, topo):
             q.remote_dma_fused(trs, local_sem=T.sem["sn%d" % k])
             return []
         o = op("g", ("r", nbytes), fn, [x[1] for x in sides], [], kind="s", sem="sn%d" % k, val=m * len(sides))
+        ops[o]["behind"] = sent[-1:]
+        sent.append(o)
         for j, x in enumerate(sides):
             op(None, ("a",), None, [], [x[3]], kind="a", sem="a%d" % (k + j), val=m, after=[o])
 
@@ -191,33 +210,26 @@ def build(core, T, topo):
 
     def ext(out, e, tab, first, c0=0, c1=96):
         return mm([(out, terms(e, tab, first, c0, c1))])
-    bank, bank2 = ("ps5", "ps4"), ("ps2", "ps3")
+
+    def ps(bank, a, b, s=1):
+        return R("ps", 512 * bank + a, 512 * bank + b, s)
 
     def lst(t, c, a=0, b=96):
         return R("lu", 960 * (t + 1) + c + a, 960 * (t + 1) + c + b)
 
-    def rot_pairs(dst, src, up):
-        if up:
-            return [(dst[16:128], src[0:112]), (dst[0:16], src[112:128])]
-        return [(dst[0:112], src[16:128]), (dst[112:128], src[0:16])]
-
-    dma("y", [(T.xb[:], T.x0[:])], [], [R("xb")], 393216)
-    srcl, srcr = R("xb", 0, H), R("xb", V - H, V)
-    if rotr:
-        dma("y", [(T.xr[16:128, :], T.x0[0:112, V - H:V]), (T.xr[0:16, :], T.x0[112:128, V - H:V])], [], [R("xr")], 65536)
-        srcr = R("xr")
-    if rotl:
-        dma("y", [(T.xr[0:112, :], T.x0[16:128, 0:H]), (T.xr[112:128, :], T.x0[0:16, 0:H])], [], [R("xr")], 65536)
-        srcl = R("xr")
-    dma("s", [(T.lw[:, 0:96], T.lf[:]), (T.lw[:, 96:192], T.rt[:])], [], [R("lw")], 98304)
-    if rotr:
-        pr = [(T.gs[16:128, 0:2], T.lf[0:112, 94:96]), (T.gs[0:16, 0:2], T.lf[112:128, 94:96]),
-              (T.gs[16:128, 2:4], T.rt[0:112, 94:96]), (T.gs[0:16, 2:4], T.rt[112:128, 94:96])]
-    else:
-        pr = [(T.gs[:, 0:2], T.lf[:, 94:96]), (T.gs[:, 2:4], T.rt[:, 94:96])]
-    dma("y", pr, [], [R("gs")], 65536)
-    exchange([(left, srcl, R("xl", H, 2 * H), R("xl", H, 2 * H)), (right, srcr, R("xl", 0, H), R("xl", 0, H))], 131072)
-    exchange([(right, R("gs"), R("gl"), R("gl"))], 16384)
+    srcl, srcr = R("xr", 0, H), R("xr", H, 2 * H)
+    pr = [(T.xr[16:128, H:], T.x0[0:112, V - H:V]), (T.xr[0:16, H:], T.x0[112:128, V - H:V])] if rotr else [(T.xr[:, H:], T.x0[:, V - H:V])]
+    loads = [dma("y", pr, [], [srcr], 65536)]
+    pr = [(T.xr[0:112, :H], T.x0[16:128, 0:H]), (T.xr[112:128, :H], T.x0[0:16, 0:H])] if rotl else [(T.xr[:, :H], T.x0[:, 0:H])]
+    loads.append(dma("s", pr, [], [srcl], 65536))
+    loads.append(dma("s", [(T.lw[:, 0:96], T.lf[:]), (T.lw[:, 96:192], T.rt[:])], [], [R("lw")], 98304))
+    loads.append(dma("y", [(T.z0[:, ZO + H:ZO + H + V], T.x0[:])], [], [R("z0", ZO + H, ZO + H + V)], 393216))
+    loads.append(dma("y", [(T.xb[:], T.x0[:])], [], [R("xb")], 393216))
+    for a, b in zip(loads, loads[1:]):
+        ops[b]["behind"] = [a]
+    gl_, gr_ = R("z0", ZO, ZO + H), R("z0", ZO + H + V, ZO + W)
+    exchange([(left, srcl, gr_, gr_), (right, srcr, gl_, gl_)], 131072)
+    exchange([(right, R("lw", 92, 192), R("gl"), R("gl"))], 51200)
 
     ms(R("ones"), 1.0)
     sel(R("ident"), R("ones", 0, 128), [[-1, 128]], AL.is_equal, 0, 1)
@@ -228,8 +240,8 @@ def build(core, T, topo):
     sel(R("gsel", 0, 8), R("ones", 0, 8), [[-16, 8]], AL.is_ge, 0, 1)
     sel(R("gsel", 8, 16), R("gsel", 0, 8), [[16, 8]], AL.is_ge, 15, -1)
     cp("s", R("cs", EA + 16, EA + 144, 16), R("gsel", 8, 16))
-    for j in (2, 3):
-        cp("s", R("cs", QQ + j, QQ + 34, 4), R("gsel", 8, 16))
+    for j in (1, 3):
+        cp("s", R("cs", QQ + j, QQ + 33, 4), R("gsel", 8, 16))
 
     def idn(a, s):
         return R("ident", a, 128, s)
@@ -237,16 +249,16 @@ def build(core, T, topo):
     def c_(base, a, s, w=32):
         return R("cs", base + a, base + w, s)
     tt(c_(SC, 0, 1), idn(0, 4), idn(1, 4), AL.add)
-    tt(R("cs", EL + 16, EL + 144, 16), c_(SC, 0, 4), c_(SC, 1, 4), AL.add)
-    tt(R("cs", ER + 16, ER + 144, 16), c_(SC, 2, 4), c_(SC, 3, 4), AL.add)
+    tt(R("cs", EL + 16, EL + 144, 16), c_(SC, 0, 4), c_(SC, 2, 4), AL.add)
+    tt(R("cs", ER + 16, ER + 144, 16), c_(SC, 1, 4), c_(SC, 3, 4), AL.add)
     for base, o_ in ((SP, AL.add), (SN, AL.subtract)):
         act(c_(base, 0, 1), c_(SC, 0, 1), AF.Copy, scale=-1.0)
-        for j in (1, 3):
+        for j in (2, 3):
             tt(c_(base, j, 4), c_(base, j, 4), idn(11, 16), o_)
     tt(c_(SD, 0, 2, 16), c_(SC, 0, 4), idn(3, 16), AL.subtract)
-    tt(c_(SD, 1, 2, 16), c_(SC, 1, 4), idn(7, 16), AL.subtract)
+    tt(c_(SD, 1, 2, 16), c_(SC, 2, 4), idn(7, 16), AL.subtract)
     ed = R("cs", ED + 16, ED + 144, 16)
-    act(R("gsel", 0, 8), idn(10, 16), AF.Copy, scale=1536.0)
+    act(R("gsel", 0, 8), idn(6, 16), AF.Copy, scale=1536.0)
     act(R("btmp", 0, 8), idn(11, 16), AF.Copy, scale=-272.0)
     tt(ed, idn(3, 16), idn(7, 16), AL.add)
     tt(ed, ed, R("gsel", 0, 8), AL.add)
@@ -256,131 +268,190 @@ def build(core, T, topo):
     ts(R("ki", 4, 5), R("ki", 0, 1), 15, None, AL.bitwise_and)
     cp("v", KK, R("ki", 4, 5))
     red(ONE, idn(11, 16))
-    red(HI, idn(0, 8))
+    tt(R("btmp", 8, 16), idn(0, 16), idn(4, 16), AL.add)
+    red(HI, R("btmp", 8, 16))
     act(BM, HI, AF.Copy, scale=-1536.0)
     act(BP, HI, AF.Copy, scale=1536.0)
-    iota(R("v2", 0, 32), [[1280, 2], [128, 2], [0, 8]], 256, 1)
-    iota(R("v2", 32, 96), [[128, 8], [0, 8]], 512, 1)
+    KQ = R("col", 6, 7)
+    act(KQ, KK, AF.Copy, scale=-4096.0)
     iota(R("v2", 112, 208), [[128, 12], [0, 8]], 256, 1)
     iota(R("v2", 208, 224), [[128, 2], [0, 8]], 0, 1)
-    iota(R("v2", 224, 416), [[128, 12], [0, 16]], 256, 1)
+    if P["mut"]:
+        tt(R("btmp", 16, 24), idn(3, 16), idn(7, 16), AL.add)
+    else:
+        iota(R("v2", 224, 416), [[128, 12], [0, 16]], 256, 1)
     for j in range(2):
-        cp("s", c_(SR, j, 2, 16), R("cs", ER + 16, ER + 144, 16))
+        act(c_(SR, j, 2, 16), R("cs", ER + 16, ER + 144, 16), AF.Copy, scale=4096.0 - 8192.0 * j if P["mut"] else 1.0)
+        if P["mut"]:
+            act(c_(SV, j, 2, 16), R("btmp", 16, 24), AF.Copy, scale=8192.0 * j - 4096.0)
     iota(R("vw", 192, 288), [[16, 96]], 256, 0)
-    act(R("vw", 0, 96), R("vw", 192, 288), AF.Identity, bias=KK)
-    ts(R("vw", 96, 192), R("vw", 192, 288), KK, float(ZO), AL.add, AL.add)
+    act(R("vn", 0, 96), R("vw", 192, 288), AF.Copy, scale=-1.0)
+    ts(R("vw", 96, 192), R("vw", 192, 288), KK, float(ZO - Z8), AL.add, AL.add)
+    RS = P["rs"]
+    if RS:
+        ms(R("vn", 96, 96 + RS // 16), 0.0)
+        ms(R("vn", 96 + RS // 16, 192), -float(RS))
     ms(R("pb"), 0.0)
-    ms(R("pa"), 0.0)
+    dma("y", [(A(R("pa", 0, V)), A(R("pb"))), (A(R("pa", V, V + H)), A(R("pb", 0, H)))], [R("pb")], [R("pa")], 458752)
     ms(R("pb", 11, V, 16), 1.0)
-    ts(R("pb", 3, V, 16), R("v2", 0, 96), KK, None, AL.subtract)
-    act(R("pb", 7, V, 16), R("v2", 0, 96), AF.Identity, bias=KK, scale=0.0)
+    ts(R("pb", 3, V, 16), R("v2", 112, 208), KK, None, AL.subtract)
+    act(R("pb", 7, V, 16), R("v2", 112, 208), AF.Identity, bias=KK, scale=0.0)
     ts(R("pa", 1, 1792, 16), R("v2", 112, 224), KK, None, AL.subtract)
     act(R("pa", 2, 1792, 16), R("v2", 112, 224), AF.Identity, bias=KK, scale=0.0)
     tr([(R("pt", 128 * b, 128 * b + 128), R("pa", V + 128 * b, V + 128 * b + 128)) for b in range(2)])
-    for a in ("a1", "a2", "a4"):
-        cp("s", R(a, 0, H), R("pt", 0, H))
-    if rotr or rotl:
-        ms(R("onef"), 1.0)
-        sel(R("rot"), R("onef"), [[0, 2], [-1, 128]], AL.is_equal, 0, 1)
+    cp("s", R("a1", 0, H), R("pt", 0, H))
+    dma("y", [(A(R(a, 0, H)), A(R("a1", 0, H))) for a in ("a2", "a4")], [R("a1", 0, H)], [R("a2", 0, H), R("a4", 0, H)], 131072)
+    mw = 256
+    sel(R("id2", 0, mw), R("ones", 0, mw), [[0, mw // 128], [-1, 128]], AL.is_equal, 0, 1)
+    SCALE = P["scale"]
+    for t, m_ in enumerate(("mvb", "mvf")):
+        for c, x in ((0, 1.125), (256, -0.125)):
+            act(R(m_, c, c + mw), R("id2", 0, mw), AF.Copy, scale=x * SCALE[t + 1] / SCALE[t])
+    iota(R("tt", -16, H - 1), [[0, H + 15]], 0, 0)
+    iota(R("tt", H + V, W), [[0, H]], 0, 0)
     for k in range(RO):
-        ms(R("z%d" % k, ZO - 16, ZO), 64.0)
-        ms(R("z%d" % k, ZO + W, ZW), 64.0)
+        for c in (0, ZO + W):
+            iota(R("z%d" % k, c, c + 16), [[0, 16]], 4096, 0)
 
-    s0 = 8.0 ** -RO
-    act(R("zc"), R("xb"), AF.Copy, scale=s0)
-    ts(R("z0", ZO + H, ZO + H + V), R("xb"), s0, None, AL.mult)
-    act(R("z0", ZO, ZO + H), R("xl", 0, H), AF.Copy, scale=s0)
-    ts(R("z0", ZO + H + V, ZO + W), R("xl", H, 2 * H), s0, None, AL.mult)
-    cp("v", lst(-1, LL), R("lw", 0, 96))
-    ts(lst(-1, LR), R("lw", 96, 192), -float(H), None, AL.add)
+    cp("v", lst(-1, LL), R("lw", 0, 96), bias=16.0)
+    for a, b in ((0, RS), (RS, V)):
+        if b:
+            ts(lst(-1, LR, a // 16, b // 16), R("lw", 96 + a // 16, 96 + b // 16), -float(H + a), None, AL.add)
     big = 1.5 * 2.0 ** 27
     ts(R("wp", 0, 192), R("lw"), big, big, AL.add, AL.subtract)
     tt(R("wp", 192, 384), R("lw"), R("wp", 0, 192), AL.subtract)
-    ts(R("wp", 384, 388), R("gl"), big, big, AL.add, AL.subtract)
-    tt(R("wp", 388, 392), R("gl"), R("wp", 384, 388), AL.subtract)
-    parts = [(0, 0), (4, 192), (8, 96), (12, 288)]
+    ts(R("wp", 384, 386), R("gl", 3, 100, 96), big, big, AL.add, AL.subtract)
+    tt(R("wp", 386, 388), R("gl", 3, 100, 96), R("wp", 384, 386), AL.subtract)
+    parts = [(0, 0), (4, 96), (8, 192), (12, 288)]
 
     def bv(i, kk):
         return R("bm", 144 * i + 16 - kk, 144 * i + 144 - kk)
     for k in range(4):
-        p = "ps%d" % k
-        mm([(R(p, 96 * j, 96 * j + 96), [(bv(4 * k + j, kk), R("wp", c, c + 96)) for kk, c in parts]) for j in range(4)])
+        mm([(ps(k, 96 * j, 96 * j + 96), [(bv(4 * k + j, kk), R("wp", c, c + 96)) for kk, c in parts]) for j in range(4)])
         for j in range(4):
-            cp("s", R("tt", H + 4 * k + j, H + V, 16), R(p, 96 * j, 96 * j + 96), bias=ONE)
-    mm([(R("ps5", 0, 1), [(bv(15, kk), R("wp", c, c + 1)) for kk, c in ((0, 385), (4, 389), (8, 387), (12, 391))])])
+            cp("s", R("tt", H + 4 * k + j, H + V, 16), ps(k, 96 * j, 96 * j + 96), bias=ONE)
+    mm([(ps(5, 0, 1), [(bv(15, 4 * j + turn), R("wp", 384 + j, 385 + j)) for j in range(4) for turn in ((16, -112) if rotl else (0,))])])
     act(R("col", 5, 6), HI, AF.Identity, bias=ONE, scale=-1536.0)
-    cp("s", R("tt", H - 1, H), R("ps5", 0, 1), bias=R("col", 5, 6))
+    cp("s", R("tt", H - 1, H), ps(5, 0, 1), bias=R("col", 5, 6))
 
     def blk(tab, s, first=0):
-        return R(tab, first + 128 * SLOT[s], first + 128 * SLOT[s] + 128)
+        return R(tab, first + 128 * s, first + 128 * s + 128)
+    S = P["split"]
+    HV = [(0, S), (S, V)]
+    rebase = [(R("ident"), R("vn", 96, 192))] if RS else []
+
+    def pair(bank, h):
+        return ps(bank, -S // 16, 0) if h == 0 else ps(bank, 0, (V - S) // 16) if h == 1 else ps(bank, -S // 16, (V - S) // 16)
+
+    def rwin(name, first, end, a):
+        return R(name, first + (RS if a >= RS else 0), end)
 
     def prepare(t):
         d = 1 if t % 2 == 0 else -1
-        ext(R("ps4", 144, 240), EL, "tt", H - d)
-        ext(R("ps4", 240, 336), EN, "tt", H - d)
-        ts(lst(t - 1, LCL, 0, 192), R("ps4", 144, 336), float(16 + d), float(H + V + 15), AL.add, AL.min)
-        mm([(R("ps3", 32 * s, 32 * s + 32), [(blk("tt", s, H), c_(SC, 0, 1))]) for s in range(12)])
-        cp(CURCOPY, R("pb", 0, V, 4), R("ps3", 0, 384))
-        mm([(R("ps2", 32 * s, 32 * s + 32), [(blk("tt", s, H - d), c_(SC, 0, 1)), (blk("tt", s, H), c_(SP if d > 0 else SN, 0, 1))]) for s in range(12)])
+        src, dst, gu = lst(t - 1, LL, 0, 192), lst(t - 1, LCL, 0, 192), R("gu", 2 * t, 2 * t + 2)
+        i, c = (0, H - 1) if d > 0 else (15, H + V)
+        mm([(ps(4, 192 + j, 193 + j), [(R("cs", e + 16 - i, e + 144 - i), R("tt", c, c + 1))]) for j, e in enumerate((EL, EN))])
+        ts(gu, ps(4, 192, 194), 16.0, float(H + V + 16), AL.add, AL.min)
+        up, dn = int(d > 0), int(d < 0)
+        dma("y", [(T.lu[a + up:b + up, dst[1]:dst[2]], T.lu[a + dn:b + dn, src[1]:src[2]]) for a, b in ((0, 112), (112, 127))], [src], [dst], 49152)
+        pr = []
+        for j in range(2):
+            d0, s0, g0 = dst[1] + 96 * j, src[1] + 96 * j, dst[1] + 96 * j + 95 * dn
+            pr += [(T.lu[i:128:16, d0 + up:d0 + up + 95], T.lu[15 - i:128:16, s0 + dn:s0 + dn + 95]), (T.lu[i:128:16, g0:g0 + 1], T.gu[i:128:16, gu[1] + j:gu[1] + j + 1])]
+        ops[dma("y", pr, [src, gu], [dst], 4096)]["cost"] = ("d", 1, 16384)
+        ts(dst, dst, float(d), None, AL.add)
+        mm([(ps(3, 32 * s, 32 * s + 32), [(blk("tt", s, H), c_(SC, 0, 1))]) for s in range(12)])
+        cp(P["cur"], R("pb", 0, V, 4), ps(3, 0, 384))
+        mm([(ps(2, 32 * s, 32 * s + 32), [(blk("tt", s, H - d), c_(SC, 0, 1)), (blk("tt", s, H), c_(SP if d > 0 else SN, 0, 1))]) for s in range(12)])
 
     thirds = [(0, 512), (512, 1024), (1024, V)]
 
-    def ypart(t):
-        sc, tm = 8.0 ** (t - RO), "tm"
-        for ci, (a, b) in enumerate(thirds):
-            p = R("ps%d" % (ci % 2))
-            act(R("ds", a, b), R("dr%d" % (t % 2)), AF.Abs, off=lst(t, LD, a // 16, b // 16))
-            act(p, R("ds", a, b), AF.Exp, bias=-math.log(sc * (9.0 if t % 2 else 1.0)), scale=-1.0 / sc)
-            tt(R(tm, a, b), p, R("mf", a, b), AL.mult)
-            if t == RO - 1:
-                dma("g", [(T.ye[:, a:b], A(R(tm, a, b)))], [R(tm, a, b)], [R("ye", a, b)], 262144, add=True)
-        if t == 0:
-            dma("y", [(T.ye[:], A(R(tm)))], [R(tm)], [R("ye")], 786432)
-        elif t < RO - 1:
-            dma("g", [(T.ye[:], A(R(tm)))], [R(tm)], [R("ye")], 786432, add=True)
+    staged, ydone = [0], [0]
+
+    def stage():
+        staged[0] += 1
+        return ps(staged[0] % 2, 0, 512)
+
+    def ypart(t, a, b):
+        tm, p = "tm", stage() if t < RO - 1 else ps(2 + ydone[0] % 2, 0, b - a)
+        sc = abs(SCALE[t])
+        act(p, R("ds", a, b), AF.Exp, bias=-math.log(sc * (9.0 if SCALE[t] < 0 else 1.0)), scale=-1.0 / sc)
+        tt(R(tm, a, b), p, R("mf", a, b), AL.mult)
+        ydone[0] += 1
+        if t == RO - 1 or P["y3"]:
+            dma("g" if t else "y", [(T.ye[:, a:b], A(R(tm, a, b)))], [R(tm, a, b)], [R("ye", a, b)], 512 * (b - a), add=t > 0)
+        elif ydone[0] % 3 == 0:
+            dma("g" if t else "y", [(T.ye[:], A(R(tm)))], [R(tm)], [R("ye")], 786432, add=t > 0)
 
     prepare(0)
-    chunks = [(0, H), (V - H, V), (H, 768), (768, V - H)]
     for t in range(RO):
-        z, u, dr, ma, mb = "z%d" % t, "u%d" % (t % 2), "dr%d" % (t % 2), "ma", "mb"
-        zw = R(z, ZO, ZO + H + V)
+        z, zc, dr, ma, mb = "z%d" % t, "zc" if t else "xb", "dr%d" % (t % 2), "ma", "mb"
 
         def own(a=0, b=V):
-            return R("zc", a, b)
-        for a, b in ((0, 768), (768, V)):
-            act(R(u, H + a, H + b), R(z, ZO + H + a, ZO + H + b), AF.Copy, scale=-9.0)
-        if t % 2 == 0:
-            tab, t0 = z, ZO
-        else:
+            return R(z, ZO + H + a, ZO + H + b)
+        u = "u%d" % (t % 2)
+        pieces = P[("ww", "wwu", "wwu", "wwl")[t]]
+        for a, b in (P["u"] if SCALE[t] < 0 else [x[:2] for x in pieces if x[2] in "vs"]):
+            act(R(u, H + a, H + b), own(a, b), AF.Copy, scale=-9.0)
+        tab, t0 = (z, ZO) if SCALE[t] > 0 else (u, 0)
+        if SCALE[t] < 0:
             act(R(u, 0, H), R(z, ZO, ZO + H), AF.Copy, scale=-9.0)
-            tab, t0 = u, 0
-        wins = {LL: zw, LR: R(z, ZO + H, ZO + W), LCL: R(z, ZO - 16, ZO + H + V), LCR: R(z, ZO + H, ZW)}
-        for d_, lc, x in (("dl", LL, P["de"]), (dr, LR, P["dr"])):
-            for ci, (a, b) in enumerate([(V - H, V), (0, H)] + ([(H, V - H)] if x in ("vv", "ss") else chunks[2:])):
-                if x[max(ci - 2, 0)] == "s" and ci > 1:
-                    act(R(d_, a, b), wins[lc], AF.Copy, scale=-1.0, off=lst(t - 1, lc, a // 16, b // 16))
-                    dma("g", [(A(R(d_, a, b)), A(own(a, b)))], [own(a, b), R(d_, a, b)], [R(d_, a, b)], 512 * (b - a), add=True)
-                else:
-                    gtt(R(d_, a, b), wins[lc], lst(t - 1, lc, a // 16, b // 16), own(a, b), AL.subtract)
-                act(R(d_, a, b), R(d_, a, b), AF.Abs)
-        pk = [0]
+        sub = {}
+        for side, d_ in (("R", dr), ("L", "dl")):
+            for what, c0 in (("cur", 0), ("can", V)):
+                lc = {"curR": LR, "curL": LL, "canR": LCR, "canL": LCL}[what + side]
+                for a, b, x in of(what + side, t):
+                    win = rwin(z, ZO + H, Z8, a) if side == "R" else R(z, 0, ZO + H + b)
+                    out = R(d_, c0 + a, c0 + b)
+                    if x == "p":
+                        got, one = (out, R("mvf", 256, 384)) if t else (R({LR: "g1", LL: "g2", LCL: "wb"}[lc], a, b), R("ident"))
+                        act(got, win, AF.Copy, scale=-1.0, off=lst(t - 1, lc, a // 16, b // 16))
+                        p = ps(4 + len(sub) % 2, 0, b - a)
+                        sub[lc, a] = p
+                        mm([(p, [(one, own(a, b))])], stop=False)
+                        mm([(p, [(one, got)])], start=False)
+                        act(out if what == "cur" else p, p, AF.Abs)
+                        if what == "can":
+                            tt(R("nl", a, b), p, R(d_, a, b), AL.is_lt)
+                        continue
+                    if x == "s":
+                        act(out, win, AF.Copy, scale=-1.0, off=lst(t - 1, lc, a // 16, b // 16))
+                        dma("g", [(A(out), A(own(a, b)))], [own(a, b), out], [out], 512 * (b - a), add=True)
+                    else:
+                        gtt(out, win, lst(t - 1, lc, a // 16, b // 16), R(zc, a, b), AL.subtract)
+                    if what == "cur":
+                        act(out, out, AF.Abs)
+        for side, ci in P["seq"].split():
+            a, b = thirds[int(ci)]
+            if side == "Y":
+                if t:
+                    ypart(t - 1, a, b)
+                continue
+            if side == "L" and (LCL, a) in sub:
+                continue
+            d_, p = dr if side == "R" else "dl", stage()
+            act(p, R(d_, V + a, V + b), AF.Abs)
+            tt(R("n" + side.lower(), a, b), p, R(d_, a, b), AL.is_lt)
         ll, lr = "ll%d" % t, "lr%d" % t
-        for ci in (1, 0, 2, 3):
-            a, b = chunks[ci]
-            for d_, lc, nn in ((dr, LCR, "nr"), ("dl", LCL, "nl")):
-                p = R("ps%d" % (pk[0] % 2), 0, b - a)
-                pk[0] += 1
-                gtt(R(d_, V + a, V + b), wins[lc], lst(t - 1, lc, a // 16, b // 16), own(a, b), AL.subtract)
-                act(p, R(d_, V + a, V + b), AF.Abs)
-                tt(R(nn, a, b), p, R(d_, a, b), AL.is_lt)
-            a, b = ((0, 2), (2, 4), (4, 8), (8, 12))[ci]
-            mm([(R("ps3", 32 * s, 32 * s + 32), [(blk("nl", s), R("cs", QQ + 2, QQ + 34)), (blk("nr", s), R("cs", QQ, QQ + 32))]) for s in range(a, b)])
-            dec = R("pb", 128 * a + 2, 128 * b, 4)
-            ts(dec, R("ps3", 32 * a, 32 * b), 8.5, None, AL.is_gt)
-            tt(R("pb", 128 * a + 1, 128 * b, 4), R("ps2", 32 * a, 32 * b), dec, AL.mult)
-            if ci == 1:
-                exchange([(right, R("pb", H, 2 * H), R(ll, 16 * rotr, 16 * rotr + H), R(ll, 16 * rotl, 16 * rotl + H))], 65536)
-            if ci == 0:
+        done = {"R": set(), "L": set()}
+        late = False
+        for sides, a, b in P["dec"]:
+            mm([(ps(3, 32 * s, 32 * s + 32), [(blk("n" + x.lower(), s), R("cs", QQ + (x == "L"), QQ + (x == "L") + 32)) for x in sides]) for s in range(a, b)])
+            j, st = int(sides == "R"), 2 // len(sides)
+            dec = R("pb", 128 * a + 4 * j + 2, 128 * b, 4 * st)
+            ts(dec, ps(3, 32 * a + j, 32 * b, st), 8.5, None, AL.is_gt)
+            tt(R("pb", 128 * a + 4 * j + 1, 128 * b, 4 * st), ps(2, 32 * a + j, 32 * b, st), dec, AL.mult)
+            before = {x: set(done[x]) for x in done}
+            for x in sides:
+                done[x].update(range(a, b))
+            if {10, 11} <= done["R"] and not {10, 11} <= before["R"]:
+                exchange([(right, R("pb", V - H, V), R(ll, 16 * rotr, 16 * rotr + H), R(ll, 16 * rotl, 16 * rotl + H))], 65536)
+                late = t == 1 and 11 not in done["L"]
+            elif late and 11 in done["L"] and 11 not in before["L"]:
+                exchange([(right, blk("pb", 11), R("lx", 16 * rotr, 16 * rotr + 128), R("lx", 16 * rotl, 16 * rotl + 128))], 32768)
+                if rotl:
+                    sel(R("lx", 0, 16), R("lx", 128, 144), [[0, 16]], AL.is_gt, 1, 0)
+            if {0, 1} <= done["R"] & done["L"] and not {0, 1} <= before["R"] & before["L"]:
                 exchange([(left, R("pb", 0, H), R(lr, 0, H), R(lr, 0, H))], 65536)
         if rotl:
             sel(R(ll, 0, 16), R(ll, 128, 144), [[0, 16]], AL.is_gt, 1, 0)
@@ -388,96 +459,149 @@ def build(core, T, topo):
         if rotr:
             sel(R(lr, 256, 272), R(lr, 128, 144), [[0, 16]], AL.is_gt, 1, 0)
             sel(R(lr, 128, 144), R(lr, 0, 16), [[0, 16]], AL.is_gt, 1, 0)
-        if t:
-            ypart(t - 1)
         o = 16 * rotr
-        inv = {b: s for s, b in enumerate(SLOT)}
-        tr([(R("pt", H + 128 * b, H + 128 * b + 128), R("pb", 128 * inv[b], 128 * inv[b] + 128)) for b in range(6)])
-        cp(P["t0"], R("tt", H, 1024), R("pt", H, 1024))
-        tr([(R("pt", H + 128 * b, H + 128 * b + 128), R("pb", 128 * inv[b], 128 * inv[b] + 128)) for b in (10, 11)])
-        tr([(R("pt", 128 * b, 128 * b + 128), R(ll, 128 * b, 128 * b + 128)) for b in range(2)])
-        tr([(R("pt", H + V + 128 * b, H + V + 128 * b + 128), R(lr, o + 128 * b, o + 128 * b + 128)) for b in range(2)])
-        cp(P["t1"], R("tt", 0, H), R("pt", 0, H), bias=BM)
-        cp(P["t2"], R("tt", H + V, W), R("pt", H + V, W), bias=BP)
-        tr([(R("pt", H + 128 * b, H + 128 * b + 128), R("pb", 128 * inv[b], 128 * inv[b] + 128)) for b in range(6, 10)])
-        cp(P["t3"], R("tt", 1024, H + V), R("pt", 1024, H + V))
-        for h in range(2):
-            ext(R(bank[h], 96, 144), EL, "tt", H, 48 * h, 48 * h + 48)
-            cp("v", lst(t, LL, 48 * h, 48 * h + 48), R(bank[h], 96, 144))
-            mm([(R(bank2[h], 16 * b, 16 * b + 16), [(R("tt", H + 768 * h + 128 * b, H + 768 * h + 128 * b + 128), c_(SD, 0, 1, 16))]) for b in range(6)])
-        ext(R("ps5", 240, 336), ER, "tt", H)
-        ext(R("ps5", 336, 432), ED, "tt", H)
-        ts(lst(t, LR, 0, 192), R("ps5", 240, 432), -float(H), None, AL.add)
-        for h in range(2):
-            c0 = 768 * h
-            gcp(R("g1", c0, c0 + 768), R("tt", 0, H + V), lst(t, LL, 48 * h, 48 * h + 48), P["g1"])
-            mm([(R(bank2[h], 384 + 16 * b, 400 + 16 * b), [(R("g1", c0 + 128 * b, c0 + 128 * b + 128), c_(SR, 0, 1, 16))]) for b in range(6)])
-            mut = R("sm", 96 * h, 96 * h + 96)
-            tt(mut, R(bank2[h], 384, 480), R("v2", 224 + 96 * h, 320 + 96 * h), AL.is_equal)
-            tt(R("pa", c0, c0 + 768, 8), R(bank2[h], 0, 96), mut, AL.mult)
-            tr([(R("pt", H + c0 + 128 * b, H + c0 + 128 * b + 128), R("pa", c0 + 128 * b, c0 + 128 * b + 128)) for b in range(6)])
-            cp(P["c%d" % h], R("a1", H + c0, H + c0 + 768), R("pt", H + c0, H + c0 + 768))
-        for h in range(2):
-            gcp(R("g2", 768 * h, 768 * h + 768), R("tt", H, W), lst(t, LR, 48 * h, 48 * h + 48), P["g2"])
-        twin(R(z, 0, H), R(z, ZO, ZO + H))
-        dma("y", [(A(R(ma, 0, H)), A(R(tab, t0, t0 + H))), (A(R(mb, 0, H)), A(R(tab, t0, t0 + H)))], [R(tab, t0, t0 + H)], [R(ma, 0, H), R(mb, 0, H)], 262144)
-        if t % 2:
+        byp = []
+        for h, (a, b) in enumerate(HV):
+            bs = range(a // 128, b // 128)
+            tr([(blk("pt", s, H), blk("pb", s)) for s in bs])
+            cp(P["t"][1 + h], R("tt", H + a, H + b), R("pt", H + a, H + b))
+            p = ps(4 + h, 128, 128 + (b - a) // 16)
+            ext(p, EL, "tt", H, a // 16, b // 16)
+            cp("v", lst(t, LL, a // 16, b // 16), p, bias=16.0)
+            byp.append((bs, 128 * h - a // 8, 384 - 384 * h - a // 8))
+            if not P["mut"]:
+                mm([(ps(2, byp[h][2] + 16 * s, byp[h][2] + 16 * s + 16), [(blk("tt", s, H), c_(SD, 0, 1, 16))]) for s in bs])
+        mm([(ps(5, 288, 384), terms(ER, "tt", H) + rebase)])
+        ext(ps(5, 384, 480), ED, "tt", H)
+        for a, b in (((0, 96), (96, 192)) if P["ld"] else ((0, 192),)):
+            ts(lst(t, LR, a, b), ps(5, 288 + a, 288 + b), -float(H), None, AL.add)
+        for a, b in P["ds"]:
+            act(R("ds", a, b), R(dr), AF.Abs, off=lst(t, LD, a // 16, b // 16))
+        for h, (a, b) in enumerate(HV):
+            bs, c2, c1 = byp[h]
+            early = H if P["g1e"] and h == 0 else a
+            if early > a:
+                gcp(R("g1", H, b), R("tt", -16, H + b), lst(t, LL, H // 16, b // 16), 0)
+            if h == 0:
+                tr([(blk("pt", s), blk(ll, s)) for s in range(2)])
+                cp(P["t"][0], R("tt", 0, H), R("pt", 0, H), bias=BM)
+            e_ = H if early > a else b
+            gcp(R("g1", a, e_), R("tt", -16, H + e_), lst(t, LL, a // 16, e_ // 16), min(of("g1", t)[h], e_ - a))
+            if P["mut"]:
+                mm([(ps(3, c2 + 16 * s, c2 + 16 * s + 16), [(blk("tt", s, H), c_(SV, 0, 1, 16)), (blk("tt", s, H), c_(SD, 0, 1, 16)), (blk("g1", s), c_(SR, 0, 1, 16))])
+                    for s in bs])
+                ts(R("pa", a, b, 8), ps(3, c2 + a // 8, c2 + b // 8), -2048.0, 2048.0, AL.max, AL.min)
+            else:
+                mm([(ps(3, c2 + 16 * s, c2 + 16 * s + 16), [(blk("g1", s), c_(SR, 0, 1, 16))]) for s in bs])
+                mut = R("sm", a // 8, b // 8)
+                tt(mut, ps(3, c2 + a // 8, c2 + b // 8), R("v2", 224 + a // 8, 224 + b // 8), AL.is_equal)
+                tt(R("pa", a, b, 8), ps(2, c1 + a // 8, c1 + b // 8), mut, AL.mult)
+            tr([(blk("pt", s, H), blk("pa", s)) for s in bs])
+            cp(P["c"][h], R("a1", H + a, H + b), R("pt", H + a, H + b))
+        ghosts = False
+        for a, b, x in of("g2", t):
+            if b > V - H and not ghosts:
+                tr([(blk("pt", s, H + V), blk(lr, s, o)) for s in range(2)])
+                cp(P["t"][3], R("tt", H + V, W), R("pt", H + V, W), bias=BP)
+                ghosts = True
+            gcp(R("g2", a, b), rwin("tt", H, W, a), lst(t, LR, a // 16, b // 16), b - a if x == "v" else 0)
+        if late:
+            tr([(blk("pt", 0), blk("lx", 0))])
+            cp("s", R("tt", H - 1, H), R("pt", 127, 128), bias=BM)
+        twin(R(z, Z8, Z8 + H), R(z, ZO, ZO + H))
+        gh = R(tab, t0, t0 + H)
+        if t:
+            dma("y", [(A(R(m_, 0, H)), A(gh)) for m_ in (ma, mb)], [gh], [R(ma, 0, H), R(mb, 0, H)], 262144)
+        else:
+            cp("s", R(ma, 0, H), gh)
+            twin(R(mb, 0, H), R(ma, 0, H))
+        if SCALE[t] < 0:
             twin(R("mc0"), R(u, H, H + V))
-        halves = [(V // P["mc"] * j, V // P["mc"] * (j + 1)) for j in range(P["mc"])]
         src = [(tab, t0), (ma, 0), (mb, 0), (ma, 0)]
         dst = [(ma, H), (mb, H), (ma, H), ("mf", 0)]
-        tabs = ["a1", "a2", "a4", "a8"]
+        tabs = [("a1", H), ("a2", H), ("a4", H), ("a8", 0), (z, Z8 + H)]
         for k in range(4):
-            for h in range(2):
-                pa_ = R(bank[h], 48 * (k % 2), 48 * (k % 2) + 48)
-                ext(pa_, EA, tabs[k], H if k < 3 else 0, 48 * h, 48 * h + 48)
-                cp("v", lst(t, LA1 + 96 * k, 48 * h, 48 * h + 48), pa_)
+            bank = (0, 5, 4, 5)[k]
+            for h, (a, b) in enumerate(HV):
+                p = pair(bank, h) if k else ps(4 + h, 64, 64 + (b - a) // 16)
+                ext(p, EA, tabs[k][0], tabs[k][1], a // 16, b // 16)
+                cp("v", lst(t, LA1 + 96 * k, a // 16, b // 16), p)
+            for h, (a, b) in enumerate(HV):
+                nn, c0 = tabs[k + 1]
+                win = R(tabs[k][0], 0, H + b) if k < 3 else R(z, ZO, ZO + H + b)
+                gcp(R(nn, c0 + a, c0 + b), win, lst(t, LA1 + 96 * k, a // 16, b // 16), of(("a2", "a4", "a8", "z8")[k], t)[h])
+            for h, (a, b) in (enumerate(HV) if P["ls"] > 1 else [(2, (0, V))]):
+                a2, qq, pp, vc = [R(nn, c0 + a // 16, c0 + b // 16) for nn, c0 in (("sm", 192), ("sm", 288), ("sm", 384), ("vw", 96))]
                 if k == 1:
-                    cp("s", R("sm", 576 + 48 * h, 624 + 48 * h), pa_)
+                    cp("s", a2, pair(bank, h))
+                    p = ps(5, 192 + a // 16, 192 + b // 16)
+                    mm([(p, terms(EL, "g2", 0, a // 16, b // 16) + [(R("ident"), R("vn", a // 16, b // 16))])])
+                    act(qq, p, AF.Abs, bias=KQ, scale=4096.0)
                 if k == 2:
-                    tt(R("sm", 288 + 48 * h, 336 + 48 * h), pa_, R("sm", 576 + 48 * h, 624 + 48 * h), AL.is_equal)
-                if k == 3:
-                    tt(R("sm", 480 + 48 * h, 528 + 48 * h), pa_, R("sm", 384 + 48 * h, 432 + 48 * h), AL.max)
-            for h in range(2):
-                c0 = 768 * h + (H if k != 2 else 0)
-                gcp(R(tabs[k + 1] if k < 3 else z, c0, c0 + 768), R(tabs[k]) if k < 3 else zw, lst(t, LA1 + 96 * k, 48 * h, 48 * h + 48), P[tabs[k + 1] if k < 3 else "z8"])
-            if k == 1:
-                ext(R("ps5", 144, 240), EL, "g2", 0)
-                tt(R("sm", 192, 288), R("ps5", 144, 240), R("vw", 0, 96), AL.is_equal)
-            if k == 2:
-                tt(R("sm", 288, 384), R("sm", 288, 384), R("sm", 192, 288), AL.max)
-                tt(R("sm", 384, 480), R("sm", 288, 384), R("vw", 96, 192), AL.mult)
+                    tt(pp, a2, pair(bank, h), AL.subtract)
+                    tt(pp, pp, qq, AL.mult)
+                    tt(pp, pp, vc, AL.add)
             if k == 3:
-                cp("v", lst(t, LS), R("sm", 480, 576))
+                for h, (a, b) in (enumerate(HV) if P["ls"] else [(2, (0, V))]):
+                    mv = R("sm", 192 + a // 16, 192 + b // 16)
+                    tt(mv, pair(bank, h), R("sm", 384 + a // 16, 384 + b // 16), AL.min)
+                    ts(lst(t, LS, a // 16, b // 16), mv, float(Z8 - ZO), None, AL.add)
             sn, s_ = src[k]
             dn, d_ = dst[k]
-            cn = "zc" if k == 0 and t % 2 == 0 else "mc%d" % (k % 2)
-            for a, b in halves:
-                gtt(R(dn, d_ + a, d_ + b), R(sn, s_, s_ + H + V), lst(t, LA1 + 96 * k, a // 16, b // 16), R(cn, a, b), AL.max)
-                if k < 3:
+            cn = zc if k == 0 and SCALE[t] > 0 else "mc%d" % (k % 2)
+            for a, b in P["mcl" if t == RO - 1 else "mc"]:
+                gtt(R(dn, d_ + a, d_ + b), R(sn, s_, s_ + H + b), lst(t, LA1 + 96 * k, a // 16, b // 16), R(cn, a, b), AL.max)
+                if k < 3 and t == RO - 1 and P["twl"][k] == "s":
+                    cp("s", R("mc%d" % (1 - k % 2), a, b), R(dn, d_ + a, d_ + b))
+                elif k < 3:
                     twin(R("mc%d" % (1 - k % 2), a, b), R(dn, d_ + a, d_ + b))
         if t < RO - 1:
             prepare(t + 1)
-        top = 4.0 * 8.0 ** (t + 1 - RO)
-        lo, hi = (-top, 0.0) if t % 2 == 0 else (0.0, top)
-        nz = "z%d" % (t + 1)
-        for ci, (a, b) in enumerate(thirds if t == RO - 1 else chunks):
-            gtt(R("ww", a, b), R(z, 0, ZO + H + V), lst(t, LS, a // 16, b // 16), R(u, H + a, H + b), AL.add)
+        nz, mv_, ww = "z%d" % (t + 1), "mvf" if t else "mvb", "ww" if t else "wb"
+
+        lo, hi = sorted((0.0, 4.0 * SCALE[t + 1]))
+
+        def move(out, a, b, turn):
+            if x in "pq":
+                p = stage()
+                p = (p[0], p[1], p[1] + b - a, 1)
+                mm([(p, [(R(mv_, turn, turn + 128), own(a, b))])], stop=False)
+                mm([(p, [(R(mv_, 256 + turn, 384 + turn), R(ww, a, b))])], start=False)
+            elif turn:
+                p = ps(3, 0, H)
+                mm([(p, [(R(mv_, 256 + turn, 384 + turn), R(ww, a, b))])])
+            else:
+                p = R(ww, a, b)
+            ts(out, p, lo, hi, AL.max, AL.min)
+        for ci, (a, b, x) in enumerate(pieces):
+            win = R(z, ZO, Z8 + H + (S if b <= S else V))
+            if x in "pq":
+                gcp(R(ww, a, b), win, lst(t, LS, a // 16, b // 16), b - a if x == "q" else 0)
+            elif x == "s":
+                gcp(R(ww, a, b), win, lst(t, LS, a // 16, b // 16), 0)
+                dma("g", [(A(R(ww, a, b)), A(R(u, H + a, H + b)))], [R(u, H + a, H + b), R(ww, a, b)], [R(ww, a, b)], 512 * (b - a), add=True)
+            else:
+                gtt(R(ww, a, b), win, lst(t, LS, a // 16, b // 16), R(u, H + a, H + b), AL.add)
             if t == RO - 1:
-                ts(R("z0", a, b), R("ww", a, b), lo, hi, AL.max, AL.min)
-                dma("y", [(T.xe[:, a:b], A(R("z0", a, b)))], [R("z0", a, b)], [R("xe", a, b)], 262144)
+                move(R("z1", a, b), a, b, 0)
+                dma("y", [(T.xe[:, a:b], A(R("z1", a, b)))], [R("z1", a, b)], [R("xe", a, b)], 512 * (b - a))
                 continue
-            ts(R(nz, ZO + H + a, ZO + H + b), R("ww", a, b), lo, hi, AL.max, AL.min)
-            twin(R("zc", a, b), R(nz, ZO + H + a, ZO + H + b))
-            if (ci == 0 and rotl) or (ci == 1 and rotr):
-                mm([(R("ps3", 0, H), [(R("rot", 112, 240) if rotr else R("rot", 16, 144), R("ww", a, b))])])
-                ts(R("xs"), R("ps3", 0, H), lo, hi, AL.max, AL.min)
+            if a == 0 and rotl:
+                move(R("xs", 0, H), 0, H, 16)
+            if b == V and rotr:
+                move(R("xs", H, 2 * H), V - H, V, 112)
+            move(R(nz, ZO + H + a, ZO + H + b), a, b, 0)
+            if P["twin"][ci] == "y":
+                twin(R("zc", a, b), R(nz, ZO + H + a, ZO + H + b))
+            else:
+                cp(P["twin"][ci], R("zc", a, b), R(nz, ZO + H + a, ZO + H + b))
             gl_, gr_ = R(nz, ZO, ZO + H), R(nz, ZO + H + V, ZO + W)
-            if ci == 0:
-                exchange([(left, R("xs") if rotl else R(nz, ZO + H, ZO + 2 * H), gr_, gr_)], 131072)
-            if ci == 1:
-                exchange([(right, R("xs") if rotr else R(nz, ZO + V, ZO + V + H), gl_, gl_)], 131072)
-    ypart(RO - 1)
+            if a == 0:
+                exchange([(left, R("xs", 0, H) if rotl else R(nz, ZO + H, ZO + 2 * H), gr_, gr_)], 131072)
+            if b == V:
+                exchange([(right, R("xs", H, 2 * H) if rotr else R(nz, ZO + V, ZO + V + H), gl_, gl_)], 131072)
+    for a, b in P["mcl"]:
+        ypart(RO - 1, a, b)
     return ops
 
 
@@ -492,8 +616,8 @@ def banks(o):
     for r in o["rd"] + o["wr"]:
         if r[0] == "pt":
             s.update(("pt", k) for k in range(r[1] // 1024, (r[2] - 1) // 1024 + 1))
-        elif r[0][:2] == "ps":
-            s.add((r[0], 0))
+        elif r[0] == "ps":
+            s.update(("ps", k) for k in range(r[1] // 512, (r[2] - 1) // 512 + 1))
     return s
 
 
@@ -535,112 +659,255 @@ def times(o, m):
         x = 0.05 + c[1] * m["pe"]
     elif c[0] == "d":
         i = c[1] * (1.0 if o["e"] == "g" else 0.1)
-        return i, i + 2.0 + c[2] / 400000.0
+        x = 8 * c[1] * m["row"] + c[2] / 610000.0
+        return i, i + 1.7 + x, x
     elif c[0] == "r":
-        return 0.6, 0.6 + m["rem"] * 0.5 + c[1] / 150000.0
+        return 0.6, 0.6 + m["rem"] * 0.5 + c[1] / 150000.0, 8 * m["row"] + c[1] / 400000.0
     else:
-        return 0.0, m["rem"] * 0.5
-    return x, x
+        return 0.0, m["rem"] * 0.5, 0.0
+    return x, x, 0.0
 
 
-def plan(ops, deps, m, pr, slack, back=False):
-    n = len(ops)
-    tm_ = [times(o, m) for o in ops]
-    succ = [[] for o in ops]
-    for i, d in enumerate(deps):
-        for j in d:
-            succ[j].append(i)
-    if back:
-        deps, succ = succ, deps
-    bk = [o["bk"] for o in ops]
-    left = [len(d) for d in deps]
-    ready = {i: 0.0 for i in range(n) if not left[i]}
-    free = {}
-    last = {}
-    fin = [0.0] * n
-    order = []
-    extra = [[] for o in ops]
-    while ready:
-        est = {}
-        for i, r in ready.items():
-            e = ops[i]["e"]
-            s = max(r, free.get(e, 0.0) - (tm_[i][1] - tm_[i][0] if back else 0.0)) if e else r
+def land(s, d, busy):
+    x = max(s + d[1] - 0.7 - d[2], busy[0]) + d[2]
+    busy[0] = x
+    return x + 0.7
+
+
+def plan(pre, pr, slack, back=False):
+    eng, bk, dur, lat, n = pre["eng"], pre["bk"], pre["dur"][0], pre["lat"][0], pre["n"]
+    succ, then, left = (pre["deps"], pre["behind"], list(pre["outs"])) if back else (pre["succ"], pre["ahead"], list(pre["ins"]))
+    ready = [[i for i in range(n) if not left[i] and eng[i] == e] for e in range(6)]
+    rdy, fin, est, free = [0.0] * n, [0.0] * n, [0.0] * n, [0.0] * 6
+    last = [[-1] * 6 for b in range(8)]
+    order, extra, busy = [], [[]] * n, [0.0]
+    for step in range(n):
+        b0, e0 = 1e9, 0
+        for e in range(6):
+            f = free[e]
+            for i in ready[e]:
+                s = rdy[i]
+                x = f - dur[i][1] + dur[i][0] if back else f
+                if x > s:
+                    s = x
+                for b in bk[i]:
+                    for j in last[b]:
+                        if j >= 0 and eng[j] != e and fin[j] + lat > s:
+                            s = fin[j] + lat
+                est[i] = s
+                if s < b0:
+                    b0, e0 = s, e
+        i, p = -1, -1e9
+        for j in ready[e0]:
+            if est[j] <= b0 + slack[j] and pr[j] > p:
+                i, p = j, pr[j]
+        if bk[i]:
+            extra[i] = [j for b in bk[i] for j in last[b] if j >= 0 and eng[j] != e0]
             for b in bk[i]:
-                for e2, j in last.get(b, {}).items():
-                    if e2 != e:
-                        s = max(s, fin[j] + m["lat"])
-            est[i] = s
-        i0 = min(est, key=lambda i: (est[i], -pr[i]))
-        i = max((j for j in est if ops[j]["e"] == ops[i0]["e"] and est[j] <= est[i0] + slack[i0]), key=lambda j: pr[j]) if ops[i0]["e"] else i0
-        e = ops[i]["e"]
-        for b in bk[i]:
-            extra[i] += [j for e2, j in last.get(b, {}).items() if e2 != e]
-            last.setdefault(b, {})[e] = i
-        if e:
-            free[e] = est[i] + tm_[i][1 if back else 0]
-        fin[i] = est[i] + tm_[i][1]
+                last[b][e0] = i
+        if e0:
+            free[e0] = est[i] + dur[i][1 if back else 0]
+        fin[i] = land(est[i], dur[i], busy) if dur[i][2] and not back else est[i] + dur[i][1]
         order.append(i)
-        del ready[i]
+        ready[e0].remove(i)
+        x = fin[i] + lat
         for j in succ[i]:
+            if x > rdy[j]:
+                rdy[j] = x
+        for j in succ[i] + then[i]:
             left[j] -= 1
             if not left[j]:
-                ready[j] = max(fin[k] for k in deps[j]) + m["lat"]
+                ready[eng[j]].append(j)
     return order, extra, fin
 
 
-def replay(ops, deps, extra, order, m):
-    free = {}
-    fin = {}
+def replay(pre, extra, order, k):
+    eng, dur, lat, deps = pre["eng"], pre["dur"][k], pre["lat"][k], pre["deps"]
+    free, fin, busy = [0.0] * 6, [0.0] * pre["n"], [0.0]
     for i in order:
-        e = ops[i]["e"]
-        s = max([fin[j] + m["lat"] for j in deps[i] + extra[i]] + [free.get(e, 0.0) if e else 0.0])
-        a, b = times(ops[i], m)
+        e = eng[i]
+        s = free[e] - lat
+        for j in deps[i] + extra[i]:
+            if fin[j] > s:
+                s = fin[j]
+        s += lat
         if e:
-            free[e] = s + a
-        fin[i] = s + b
-    return max(fin.values())
+            free[e] = s + dur[i][0]
+        fin[i] = land(s, dur[i], busy) if dur[i][2] else s + dur[i][1]
+    return max(fin)
 
 
-def arrange(ops):
-    deps = depend(ops)
-    ms_ = models()
-    rng = np.random.default_rng(7)
-    best = None
-    n = len(ops)
+def held(pre, extra, order, k):
+    eng, dur, lat, deps = pre["eng"], pre["dur"][k], pre["lat"][k], pre["deps"]
+    free, fin, last, par, busy = [0.0] * 6, [0.0] * pre["n"], [-1] * 6, [None] * pre["n"], [0.0]
+    for i in order:
+        e = eng[i]
+        s, par[i] = free[e] - lat, (last[e], True)
+        for j in deps[i] + extra[i]:
+            if fin[j] > s:
+                s, par[i] = fin[j], (j, j not in deps[i])
+        s += lat
+        if e:
+            free[e], last[e] = s + dur[i][0], i
+        fin[i] = land(s, dur[i], busy) if dur[i][2] else s + dur[i][1]
+    i, out = fin.index(max(fin)), []
+    while i >= 0:
+        if par[i][1] and par[i][0] >= 0:
+            out.append((par[i][0], i))
+        i = par[i][0]
+    return out
+
+
+def follow(pre, order):
+    last, extra, bk, eng = [{} for b in range(8)], [[]] * pre["n"], pre["bk"], pre["eng"]
+    for i in order:
+        if bk[i]:
+            extra[i] = [j for b in bk[i] for e, j in last[b].items() if e != eng[i]]
+            for b in bk[i]:
+                last[b][eng[i]] = i
+    return extra
+
+
+def kind(o):
+    r = (o["wr"] or o["rd"])[0]
+    if o["k"] == "s":
+        return (o["e"], o["cost"])
+    if o["k"] == "d" or r[2] == r[1] + 1:
+        return (o["e"], r)
+    if o["e"] == "p" and o["rd"][0][0] in ("mvb", "mvf", "ident"):
+        return (o["e"], o["cost"], o["rd"][0][1], o["rd"][1][0][0], o["rd"][1][1], max(r[1], 1024))
+    if r[0] == "ps" and r[1] < 1024:
+        r = o["rd"][0] if o["e"] == "s" else o["rd"][1]
+    return (o["e"], o["cost"], r[0].rstrip("0123") if r[0][0] in "zudl" else r[0], r[1] % 960 if r[0] == "lu" else r[1] - r[1] % 32 if o["k"] == "a" else r[1])
+
+
+def names_of(ops):
+    seen = {}
+    out = []
     for o in ops:
-        o["bk"] = banks(o)
+        k = kind(o)
+        seen[k] = seen.get(k, 0) + 1
+        out.append((k, seen[k]))
+    return out
+
+
+def arrange(ops, like=None):
+    full = depend(ops)
+    ms_ = models()
+    n = len(ops)
+    deps, above = [], []
+    for d in full:
+        far = 0
+        for j in d:
+            far |= above[j]
+        deps.append([j for j in d if not far >> j & 1])
+        above.append(far | sum(1 << j for j in d))
+    behind = [o.get("behind", []) for o in ops]
+    succ, ahead = [[] for o in ops], [[] for o in ops]
+    for i in range(n):
+        for j in deps[i]:
+            succ[j].append(i)
+        for j in behind[i]:
+            ahead[j].append(i)
+    pre = {"n": n, "deps": deps, "succ": succ, "behind": behind, "ahead": ahead,
+           "ins": [len(deps[i] + behind[i]) for i in range(n)], "outs": [len(succ[i] + ahead[i]) for i in range(n)],
+           "eng": [[None, "v", "s", "p", "g", "y"].index(o["e"]) for o in ops],
+           "bk": [[k + 6 * (a == "pt") for a, k in sorted(banks(o))] for o in ops],
+           "dur": [[times(o, m) for o in ops] for m in ms_], "lat": [m["lat"] for m in ms_]}
+    names = {}
+    kinds = np.array([names.setdefault(kind(o), len(names)) for o in ops])
+    rng = np.random.default_rng(7)
     level = [0.0] * n
     for i in range(n - 1, -1, -1):
-        level[i] += times(ops[i], ms_[0])[1] + ms_[0]["lat"]
+        level[i] += pre["dur"][0][i][1] + pre["lat"][0]
         for j in deps[i]:
             level[j] = max(level[j], level[i])
-    fin = None
+    best = fin = None
+    if like:
+        rank = [0.0] * n
+        for i, x in reversed(list(enumerate(names_of(ops)))):
+            rank[i] = max([rank[j] + 0.01 for j in succ[i] + ahead[i]] + [like.get(x, -1e6)])
+        order = sorted(range(n), key=lambda i: -rank[i])
+        extra = follow(pre, order)
+        return deps, [0, order, extra, [replay(pre, extra, order, j) for j in range(len(ms_))]]
     for k in range(TRIES):
         if k < FB:
             slack = np.full(n, [0.1, 0.2, 0.35, 0.5][(k // 8) % 4])
-            noise = np.array(level if k % 8 == 0 else plan(ops, deps, ms_[0], fin, slack.tolist(), True)[2])
+            rank = np.array(level if k % 8 == 0 else plan(pre, fin, slack.tolist(), True)[2])
         else:
-            noise, slack = best[4].copy(), best[5].copy()
-            a = int(rng.integers(0, n))
-            pick = (rng.random(n) < 0.3) & (np.abs(np.arange(n) - a) < int(rng.choice([10, 40, 120])))
-            noise[pick] += rng.normal(0.0, float(rng.choice([0.3, 1.0, 3.0])), n)[pick]
-            slack[pick] = rng.choice([0.05, 0.2, 0.5, 1.0], n)[pick]
-        order, extra, fin = plan(ops, deps, ms_[0], noise.tolist(), slack.tolist())
-        ts_ = [replay(ops, deps, extra, order, m) for m in ms_]
-        score = ts_[0] / 1.0 + ts_[1] / 0.75 + ts_[2] / 1.4
+            rank, slack = best[4].copy(), best[5].copy()
+            if k % 2:
+                if best[6] is None:
+                    best[6] = [held(pre, best[2], best[1], j) for j in range(len(ms_))]
+                links = best[6][int(rng.integers(len(ms_)))]
+                j, i = links[int(rng.integers(len(links)))]
+                gap = max(rank[j] - rank[i], 0.0) + float(rng.choice([0.05, 0.3, 1.0]))
+                up = rng.random() < 0.5
+                who = i if up else j
+                pick = (kinds == kinds[who]) if rng.random() < 0.6 else (np.arange(n) == who)
+                shift = np.full(n, gap if up else -gap)
+                sl = slack.copy()
+                for x in np.nonzero((kinds == kinds[i]) if pick.sum() > 1 else (np.arange(n) == i))[0]:
+                    slack[x] = max(slack[x], float(rng.choice([0.2, 0.5, 1.0])))
+                sl = slack
+            elif k % 3:
+                pick = np.isin(kinds, rng.choice(kinds[n // 3:], int(rng.choice([1, 2, 4]))))
+                shift = rng.normal(0.0, float(rng.choice([0.5, 1.5, 4.0])), len(names))[kinds]
+                sl = rng.choice([0.05, 0.2, 0.5, 1.0], len(names))[kinds]
+            else:
+                pick = (rng.random(n) < 0.3) & (np.abs(np.arange(n) - int(rng.integers(0, n))) < int(rng.choice([5, 20, 60])))
+                shift = rng.normal(0.0, float(rng.choice([0.3, 1.0, 3.0])), n)
+                sl = rng.choice([0.05, 0.2, 0.5, 1.0], n)
+            rank[pick] += shift[pick]
+            slack[pick] = sl[pick]
+        order, extra, fin = plan(pre, rank.tolist(), slack.tolist())
+        ts_ = [max(fin)]
+        if best and ts_[0] > best[3][0] + 2.5:
+            continue
+        ts_ += [replay(pre, extra, order, j) for j in range(1, len(ms_))]
+        score = sum(t / m["w"] for t, m in zip(ts_, ms_))
         if best is None or score <= best[0]:
-            best = (score, order, extra, ts_, noise, slack)
+            best = [score, order, extra, ts_, rank, slack, None]
+    anc = []
+    for i in range(n):
+        a = 0
+        for j in deps[i] + behind[i]:
+            a |= anc[j] | 1 << j
+        anc.append(a)
+    cur = best[:6] + [None]
+    for k in range(SWAPS):
+        if cur[6] is None:
+            cur[6] = [x for j in range(len(ms_)) for x in held(pre, cur[2], cur[1], j)]
+        j, i = cur[6][int(rng.integers(len(cur[6])))]
+        if anc[i] >> j & 1:
+            continue
+        order = cur[1]
+        a, b = order.index(j), order.index(i) + 1
+        if k % 2:
+            go = [x for x in order[a:b] if x == i or anc[i] >> x & 1]
+            order = order[:a] + go + [x for x in order[a:b] if x not in go] + order[b:]
+        else:
+            go = [x for x in order[a:b] if x == j or anc[x] >> j & 1]
+            order = order[:a] + [x for x in order[a:b] if x not in go] + go + order[b:]
+        extra = follow(pre, order)
+        ts_ = [replay(pre, extra, order, x) for x in range(len(ms_))]
+        score = sum(t / m["w"] for t, m in zip(ts_, ms_))
+        if score <= cur[0] + HEAT * (1.0 - k / SWAPS) * rng.exponential():
+            cur = [score, order, extra, ts_, None, None, None]
+            if score < best[0]:
+                best = cur
     return deps, best
 
 
 def rank_program(g, core, T, topo):
     if T.rank_of(core) is None:
         return
+    if not PLANS:
+        first = build(core, T, topo, True)
+        names = names_of(first)
+        PLANS.update((names[i], -float(k)) for k, i in enumerate(arrange(first)[1][1]))
     ops = build(core, T, topo)
-    key = tuple((o["e"], o["cost"], tuple(o["wr"])) for o in ops)
-    if key not in PLANS:
-        PLANS[key] = arrange(ops)
-    deps, best = PLANS[key]
+    deps, best = arrange(ops, PLANS)
     order, extra = best[1], best[2]
     Q = {"v": g.vector, "s": g.scalar, "p": g.tensor, "g": g, "y": g.sync}
     known = {e: {} for e in Q}

@@ -7,26 +7,30 @@ AL = AluOpType
 AF = ActivationFunctionType
 V, H, W, RO = 1536, 256, 2048, 4
 ZO, Z8, ZW = 16, 2080, 3872
-F, B, I, U = "float32", "bfloat16", "int32", "uint16"
+F, B, G, I, U = "float32", "bfloat16", "float16", "int32", "uint16"
+NF, NB = 6, 2
 SCRATCH = {
     "xb": ("sbuf", [128, V], B), "xr": ("sbuf", [128, 2 * H], B),
     "lw": ("sbuf", [128, 192], I), "gl": ("sbuf", [128, 100], I),
     "wp": ("sbuf", [128, 400], B), "wb": ("sbuf", [128, V], B),
-    "ones": ("sbuf", [128, 256], B), "id2": ("sbuf", [128, 256], B), "mvb": ("sbuf", [128, 512], B), "mvf": ("sbuf", [128, 512], F),
+    "ones": ("sbuf", [128, 256], B), "mv0": ("sbuf", [128, 256], B), "mvf": ("sbuf", [128, 384], F),
+    "mv1": ("sbuf", [128, 256], F), "mv2": ("sbuf", [128, 256], F), "mv3": ("sbuf", [128, 256], F),
     "ident": ("sbuf", [128, 128], B), "gsel": ("sbuf", [128, 16], B), "btmp": ("sbuf", [128, 144], B),
-    "bm": ("sbuf", [128, 2416], B), "cs": ("sbuf", [128, 912], B),
-    "ki": ("sbuf", [128, 8], I), "col": ("sbuf", [128, 8], F),
-    "v2": ("sbuf", [128, 416], F), "vw": ("sbuf", [128, 288], F), "sm": ("sbuf", [128, 672], F),
-    "pb": ("sbuf", [128, V], B), "pa": ("sbuf", [128, 1792], B), "tt": ("sbuf", [128, W + 16], B), "gu": ("sbuf", [128, 8], U),
+    "bk": ("sbuf", [128, 128], B), "hk": ("sbuf", [128, 384], G), "hg": ("sbuf", [128, V], G), "hc": ("sbuf", [128, V], G),
+    "sh": ("sbuf", [128, 128], B), "wk": ("sbuf", [128, 256], B),
+    "bm": ("sbuf", [128, 2 * V], B), "cs": ("sbuf", [128, 912], B),
+    "ki": ("sbuf", [128, 8], I), "col": ("sbuf", [128, 12], F),
+    "v2": ("sbuf", [128, 96], F), "vw": ("sbuf", [128, 192], F), "sm": ("sbuf", [128, 288], F),
+    "pb": ("sbuf", [128, V], B), "tt": ("sbuf", [128, W + 16], B), "gu": ("sbuf", [128, 8], U),
     "g1": ("sbuf", [128, V], B), "g2": ("sbuf", [128, V], B),
     "a1": ("sbuf", [128, 1792], B), "a2": ("sbuf", [128, 1792], B), "a4": ("sbuf", [128, 1792], B), "a8": ("sbuf", [128, V], B),
     "nl": ("sbuf", [128, V], B), "nr": ("sbuf", [128, V], B),
     "lu": ("sbuf", [128, 5 * 960], U),
     "dl": ("sbuf", [128, 2 * V], F), "ds": ("sbuf", [128, V], F), "ww": ("sbuf", [128, V], F),
-    "tm": ("sbuf", [128, V], F), "zc": ("sbuf", [128, V], F), "xs": ("sbuf", [128, 2 * H], F), "mf": ("sbuf", [128, V], F),
+    "zc": ("sbuf", [128, V], F), "xs": ("sbuf", [128, 2 * H], F), "mf": ("sbuf", [128, V], F),
     "u0": ("sbuf", [128, 1792], F), "u1": ("sbuf", [128, 1792], F),
-    "lx": ("sbuf", [128, 144], B), "vn": ("sbuf", [128, 192], B),
-    "pt": ("psum", [128, 2048], B), "ps": ("psum", [128, 3072], F),
+    "lx": ("sbuf", [128, 144], B), "vn": ("sbuf", [128, 96], B),
+    "pt": ("psum", [128, 1024 * NB], B), "ps": ("psum", [128, 512 * NF], F),
 }
 for _k in range(4):
     SCRATCH["z%d" % _k] = ("sbuf", [128, ZW], F if _k else B)
@@ -40,26 +44,34 @@ SEMAPHORES = ["ev", "es", "ep", "eg"] + ["d%d" % k for k in range(110)] + ["%s%d
 
 EL, ER, ED, EA, SR, SC, SP, SN, SD, EN, QQ, SV = 0, 144, 288, 432, 576, 608, 640, 672, 704, 720, 864, 592
 LL, LR, LD, LCL, LCR, LA1, LA2, LA4, LA8, LS = [96 * k for k in range(10)]
-TRIES, FB, SWAPS, HEAT = 2500, 32, 16000, 0.3
+TRIES, SWAPS, HEAT, HOPE, SEED = 300, 100000, 0.3, 0.3, 4
+NEAR, FAR, REACH, EASE, SOON, LAZY, FLIP = 0.3, 0.4, 25, 0.003, 0.001, 4, 0.08
+QUEUES = [None, "v", "s", "p", "g", "y"]
+MODELS = ((1.7, 1.15, 0.55, 0.07, 2.8, 0.03, 1.15), (2.0, 1.4, 0.6, 0.1, 3.2, 0.04, 1.3), (1.25, 1.05, 0.45, 0.06, 2.5, 0.02, 0.95),
+          (1.4, 1.15, 0.85, 0.13, 4.4, 0.05, 1.3))
 PLANS = {}
-T3 = [(1024, V), (512, 1024), (0, 512)]
+
+
+def cut(ways, *ends):
+    ends = ends or (512, 1024, V)
+    return [(a, b, x) for a, b, x in zip((0,) + ends, ends, ways)]
+
+
 P = {
-    "split": 512,
-    "rs": 0,
-    "curR": [(0, 512, "v"), (512, 1024, "s"), (1024, V, "v")], "canR": [(0, 512, "v"), (512, 1024, "s"), (1024, V, "v")],
-    "curL": [(0, 512, "v"), (512, 1024, "p"), (1024, V, "p")], "canL": [(0, 512, "v"), (512, 1024, "s"), (1024, V, "v")],
-    "seq": "R2 R0 L0 R1 L1 L2 Y0 Y1 Y2",
+    "curR": cut("ssv"), "canR": cut("vsv"), "curL": cut("vvp"), "canL": cut("vsv"),
+    "curR.0": cut("ppp"), "canR.0": cut("vpv"),
+    "prod": 1, "prodL": "sss", "prodL.1": "vvv", "r0": 1,
     "dec": [("R", 8, 12), ("RL", 0, 4), ("RL", 4, 8), ("L", 8, 12)],
-    "ww": [(0, 512, "p"), (1024, V, "q"), (512, 1024, "p")],
-    "wwl": [(0, 512, "v"), (512, 1024, "v"), (1024, V, "v")],
-    "wwu": [(0, 512, "v"), (1280, V, "v"), (512, 1024, "v"), (1024, 1280, "v")],
-    "scale": [1.0, -8.0 ** -3, 8.0 ** -2, -8.0 ** -1, 1.0],
-    "twin": "yyyy", "twl": "yyy",
-    "g1e": 1, "g2": [(0, 512, "s"), (512, 1280, "s"), (1280, V, "s")],
-    "g1.0": (0, 512), "a2.0": (0, 512), "a4.0": (0, 512), "a8.0": (0, 512), "z8.0": (0, 512),
-    "g1": (0, 0), "a2": (0, 0), "a4": (0, 0), "a8": (0, 0), "z8": (0, 0),
-    "mc": T3[::-1], "ds": T3[::-1], "u": [(0, 768), (768, V)],
-    "ld": 1, "mut": 0, "y3": 0, "ls": 2, "mcl": T3[::-1], "t": "vvvv", "c": "vv", "cur": "s",
+    "ww.0": [(0, 512, "p"), (1024, V, "q"), (512, 1024, "p")],
+    "ww.3": cut("vvv"),
+    "ww": [(0, 512, "v"), (1280, V, "v"), (512, 1024, "v"), (1024, 1280, "v")],
+    "pm": 1, "zd": 0, "zg": 1,
+    "hv": cut("vv", 512, V), "go": cut("vv", 512, V), "xs": "s", "far": 1, "tw": "yyy", "tw.3": "ggg", "tz": "gyyy",
+    "g1": cut("ssss", 256, 512, 1024, V), "a2": cut("sss"), "a4": cut("sss"), "a8": cut("sss"), "z8": cut("sss"),
+    "g1.0": cut("sssv", 256, 512, 1024, V), "a2.0": cut("ssv"), "a4.0": cut("ssv"), "a8.0": cut("ssv"), "z8.0": cut("ssv"),
+    "g2": cut("sss", 512, 1280, V),
+    "mc": cut("vvv"), "ds": cut("sss"), "u": cut("ss", 768, V), "yy": cut("vvv"),
+    "y3": 0, "t": "svvs", "cur": "s", "pe0": 1,
 }
 
 
@@ -69,8 +81,7 @@ def of(key, t):
 
 def models():
     out = []
-    for ga, f, pe, lat, rem, row, w in ((1.56, 1.0, 0.55, 0.07, 2.8, 0.03, 1.0), (1.15, 1.05, 0.43, 0.07, 2.5, 0.02, 0.92),
-                                        (1.85, 1.3, 0.55, 0.12, 3.5, 0.05, 1.33), (1.4, 1.15, 0.92, 0.09, 3.0, 0.03, 1.2)):
+    for ga, f, pe, lat, rem, row, w in MODELS:
         out.append({"g": ga, "c": 0.00083 * f, "pe": 0.001 * pe, "lat": lat, "rem": rem, "row": row, "w": w})
     return out
 
@@ -79,16 +90,25 @@ def build(core, T, topo, both=False):
     rank, n = T.rank_of(core), len(T.cores)
     left, right = T.cores[(rank - 1) % n], T.cores[(rank + 1) % n]
     rotr, rotl = both or rank == n - 1, both or rank == 0
-    ops = []
-    nd, nx, sent = [0], [0], []
+    ops, tiles, place = [], {}, {}
+    nd, nx, sent, only = [0], [0], [], [None]
 
     def R(name, a=0, b=None, s=1):
         if b is None:
             b = SCRATCH[name][1][1] if name in SCRATCH else V
         return (name, a + 16, b + 16, s) if name == "tt" else (name, a, b, s)
 
+    def tile(label, dt=F):
+        name = "@%d" % len(tiles)
+        tiles[name] = (label, dt)
+        return name
+
     def A(r):
-        return T[r[0]][:, r[1]:r[2]:r[3]] if r[3] != 1 else T[r[0]][:, r[1]:r[2]]
+        name, c = place[r[0]] if r[0] in tiles else (r[0], 0)
+        return T[name][:, c + r[1]:c + r[2]:r[3]] if r[3] != 1 else T[name][:, c + r[1]:c + r[2]]
+
+    def dty(r):
+        return tiles[r[0]][1] if r[0] in tiles else SCRATCH[r[0]][2]
 
     def cnt(r):
         return len(range(r[1], r[2], r[3]))
@@ -98,11 +118,18 @@ def build(core, T, topo, both=False):
 
     def op(eng, cost, fn, rd, wr, kind="c", sem=None, val=0, after=()):
         ops.append({"e": eng, "cost": cost, "fn": fn, "rd": [r for r in rd if isinstance(r, tuple)], "wr": list(wr), "k": kind,
-                    "sem": sem, "val": val, "after": list(after)})
+                    "sem": sem, "val": val, "after": list(after), "behind": [], "only": only[0], "once": 0.0, "alt": None, "first": None})
         return len(ops) - 1
 
+    def either(eng, on_v, on_s):
+        (on_s if eng == "v" else on_v)()
+        alt = ops.pop()
+        o = (on_v if eng == "v" else on_s)()
+        ops[o]["alt"] = alt
+        return o
+
     def two(*rs):
-        return all(SCRATCH[r[0]][2] in (B, U) for r in rs)
+        return all(dty(r) in (B, G, U) for r in rs)
 
     def ts(out, a, s1, s2, o0, o1=None):
         def fn(q):
@@ -112,17 +139,17 @@ def build(core, T, topo, both=False):
         return op("v", ("e", cnt(a) * (0.5 if two(out, a) else 1)), fn, [a, s1, s2], [out])
 
     def tt(out, a, b, o):
-        both = SCRATCH[a[0]][0] == "sbuf" and SCRATCH[b[0]][0] == "sbuf"
-        return op("v", ("e", cnt(a) * (2 if both else 1)), lambda q: [q.tensor_tensor(A(out), A(a), A(b), o)], [a, b], [out])
+        sb = a[0] not in tiles and b[0] not in tiles
+        return op("v", ("e", cnt(a) * (2 if sb else 1)), lambda q: [q.tensor_tensor(A(out), A(a), A(b), o)], [a, b], [out])
 
-    def cp(eng, out, a, bias=None):
-        if eng == "v":
-            if bias is not None:
-                return ts(out, a, bias, None, AL.add)
+    def cp(eng, out, a, bias=None, scale=None):
+        def on_v():
+            if bias is not None or scale is not None:
+                return ts(out, a, scale if bias is None else bias, None, AL.mult if bias is None else AL.add)
             return op("v", ("e", cnt(a) * (0.5 if two(out, a) else 1)), lambda q: [q.tensor_copy(A(out), A(a))], [a], [out])
-        if bias is not None:
-            return act(out, a, AF.Identity, bias=bias)
-        return act(out, a, AF.Copy)
+        if {dty(out), dty(a)} - {F, B}:
+            return on_v()
+        return either(eng, on_v, lambda: act(out, a, AF.Copy if bias is None else AF.Identity, bias=bias, scale=scale))
 
     def act(out, a, f, bias=None, scale=None, off=None):
         def fn(q):
@@ -130,19 +157,21 @@ def build(core, T, topo, both=False):
             if bias is not None:
                 kw["bias"] = X(bias)
             if scale is not None:
-                kw["scale"] = scale
+                kw["scale"] = X(scale)
             return [q.activation(A(out), A(a).indirect(A(off)) if off else A(a), f, **kw)]
-        return op("s", ("g" if off else "e", cnt(out)), fn, [a, bias, off], [out])
+        return op("s", ("g" if off else "e", cnt(out)), fn, [a, bias, scale, off], [out])
 
     def gtt(out, win, off, b, o):
         return op("v", ("g", cnt(out)), lambda q: [q.tensor_tensor(A(out), A(win).indirect(A(off)), A(b), o)], [win, off, b], [out])
 
-    def gcp(out, win, off, x):
-        o1, f1 = (out[0], out[1], out[1] + x, 1), (off[0], off[1], off[1] + x // 16, 1)
-        if x:
-            op("v", ("g", x), lambda q: [q.tensor_copy(A(o1), A(win).indirect(A(f1)))], [win, f1], [o1])
-        if x < cnt(out):
-            act((out[0], out[1] + x, out[2], 1), win, AF.Copy, off=(off[0], off[1] + x // 16, off[2], 1))
+    def gcp(out, win, off, eng, scale=None):
+        def on_v():
+            if scale:
+                return op("v", ("g", cnt(out)), lambda q: [q.tensor_scalar(A(out), A(win).indirect(A(off)), scale, None, AL.mult)], [win, off], [out])
+            return op("v", ("g", cnt(out)), lambda q: [q.tensor_copy(A(out), A(win).indirect(A(off)))], [win, off], [out])
+        if dty(out) == G:
+            return on_v()
+        return either(eng, on_v, lambda: act(out, win, AF.Copy, scale=scale, off=off))
 
     def ms(out, c):
         return op("v", ("e", cnt(out) * (0.5 if two(out) else 1)), lambda q: [q.memset(A(out), c)], [], [out])
@@ -151,7 +180,7 @@ def build(core, T, topo, both=False):
         return op("v", ("e", cnt(a)), lambda q: [q.tensor_reduce(A(out), A(a), AxisListType.X, AL.add)], [a], [out])
 
     def iota(out, pat, base, cm):
-        kw = {} if SCRATCH[out[0]][2] == I else {"allow_small_or_imprecise_dtypes": True}
+        kw = {} if dty(out) == I else {"allow_small_or_imprecise_dtypes": True}
         return op("g", ("q", cnt(out)), lambda q: [q.iota(A(out), pat, base, cm, **kw)], [], [out])
 
     def sel(out, a, pat, cmpop, base, cm):
@@ -165,12 +194,20 @@ def build(core, T, topo, both=False):
                     ins = q.matmul(A(out), A(l), A(r), start and k == 0, stop and k == len(terms) - 1)
                 last.append(ins)
             return last
-        c = sum(max(64, cnt(r)) * (4 if SCRATCH[r[0]][2] == F else 1) for out, terms in groups for l, r in terms)
+        c = sum(max(64, cnt(r)) * (4 if dty(r) == F else 1) for out, terms in groups for l, r in terms)
         return op("p", ("p", c), fn, [x for out, terms in groups for t in terms for x in t], [out for out, terms in groups], val=len(groups))
+
+    def sums(p, *terms, ahead=None):
+        for k, x in enumerate(terms):
+            o = mm([(p, [x])], start=k == 0, stop=k == len(terms) - 1)
+            if k == 0 and ahead is not None:
+                ops[o]["behind"].append(ahead)
 
     def tr(pairs):
         return op("p", ("p", 128 * len(pairs)), lambda q: [q.transpose(A(o), A(a), A(R("ident"))) for o, a in pairs],
                   [a for o, a in pairs] + [R("ident")], [o for o, a in pairs], val=len(pairs))
+
+    gd = []
 
     def dma(eng, pairs, rd, wr, nbytes, add=False):
         s = "d%d" % nd[0]
@@ -180,12 +217,21 @@ def build(core, T, topo, both=False):
             if add:
                 return [q.dma_start(o, a, accum_op=AL.add) for o, a in pairs]
             return [q.dma_start(o, a) for o, a in pairs]
-        return op(eng, ("d", len(pairs), nbytes * (2 if add else 1)), fn, rd, wr, kind="d", sem=s, val=16 * len(pairs))
+        o = op(eng, ("d", len(pairs), nbytes * (2 if add else 1)), fn, rd, wr, kind="d", sem=s, val=16 * len(pairs))
+        if eng == "g":
+            ops[o]["behind"] += gd[:1]
+            ops[o]["once"] = 0.0 if gd else 1.0
+            gd.append(o)
+        return o
 
-    def twin(dst, src):
+    def twin(dst, src, eng="y"):
+        if eng == "g":
+            return sel(dst, src, [[0, cnt(src)]], AL.is_gt, 1, 0)
+        if eng == "s":
+            return cp(eng, dst, src)
         return dma("y", [(A(dst), A(src))], [src], [dst], 512 * cnt(src))
 
-    def exchange(sides, nbytes):
+    def exchange(sides, nbytes, also=()):
         k = nx[0]
         nx[0] += len(sides)
         eng = [topo.engines(core, x[0]) for x in sides]
@@ -199,8 +245,9 @@ def build(core, T, topo, both=False):
                 trs.append(RemoteDMATransfer(dst_ids=[DstId(rid=rid, pnc=pid)], dma_engine_mask=mask, remote_sem=T.sem["a%d" % (k + j)], src=A(src), dst=A(there)))
             q.remote_dma_fused(trs, local_sem=T.sem["sn%d" % k])
             return []
-        o = op("g", ("r", nbytes), fn, [x[1] for x in sides], [], kind="s", sem="sn%d" % k, val=m * len(sides))
-        ops[o]["behind"] = sent[-1:]
+        o = op("g", ("r", nbytes), fn, [x[1] for x in sides] + list(also), [], kind="s", sem="sn%d" % k, val=m * len(sides))
+        ops[o]["behind"] += sent[-1:]
+        ops[o]["once"] = 0.0 if sent else 1.5
         sent.append(o)
         for j, x in enumerate(sides):
             op(None, ("a",), None, [], [x[3]], kind="a", sem="a%d" % (k + j), val=m, after=[o])
@@ -208,14 +255,21 @@ def build(core, T, topo, both=False):
     def terms(e, tab, first, c0=0, c1=96):
         return [(R("cs", e + 16 - i, e + 144 - i), R(tab, first + 16 * c0 + i, first + 16 * c1 + i - 15, 16)) for i in range(16)]
 
-    def ext(out, e, tab, first, c0=0, c1=96):
-        return mm([(out, terms(e, tab, first, c0, c1))])
+    def ext(label, e, tab, first, a=0, b=V, more=()):
+        p = R(tile(label), 0, (b - a) // 16)
+        mm([(p, terms(e, tab, first, a // 16, b // 16) + list(more))])
+        return p
 
-    def ps(bank, a, b, s=1):
-        return R("ps", 512 * bank + a, 512 * bank + b, s)
+    def lst(t, c, a=0, b=V):
+        return R("lu", 960 * (t + 1) + c + a // 16, 960 * (t + 1) + c + b // 16)
 
-    def lst(t, c, a=0, b=96):
-        return R("lu", 960 * (t + 1) + c + a, 960 * (t + 1) + c + b)
+    def blk(tab, s, first=0):
+        return R(tab, first + 128 * s, first + 128 * s + 128)
+
+    def wrap(name, a, b, side):
+        only[0] = side
+        sel(R(name, a, a + 16), R(name, b, b + 16), [[0, 16]], AL.is_gt, 1, 0)
+        only[0] = None
 
     srcl, srcr = R("xr", 0, H), R("xr", H, 2 * H)
     pr = [(T.xr[16:128, H:], T.x0[0:112, V - H:V]), (T.xr[0:16, H:], T.x0[112:128, V - H:V])] if rotr else [(T.xr[:, H:], T.x0[:, V - H:V])]
@@ -226,16 +280,26 @@ def build(core, T, topo, both=False):
     loads.append(dma("y", [(T.z0[:, ZO + H:ZO + H + V], T.x0[:])], [], [R("z0", ZO + H, ZO + H + V)], 393216))
     loads.append(dma("y", [(T.xb[:], T.x0[:])], [], [R("xb")], 393216))
     for a, b in zip(loads, loads[1:]):
-        ops[b]["behind"] = [a]
+        ops[b]["behind"].append(a)
     gl_, gr_ = R("z0", ZO, ZO + H), R("z0", ZO + H + V, ZO + W)
     exchange([(left, srcl, gr_, gr_), (right, srcr, gl_, gl_)], 131072)
     exchange([(right, R("lw", 92, 192), R("gl"), R("gl"))], 51200)
 
-    ms(R("ones"), 1.0)
+    ms(R("ones", 0, 144), 1.0)
+    warm = act(R("ones", 144, 256), R("ones", 0, 112), AF.Exp, scale=0.0)
+    ops[warm]["once"] = 1.3
     sel(R("ident"), R("ones", 0, 128), [[-1, 128]], AL.is_equal, 0, 1)
     sel(R("btmp"), R("ones", 0, 144), [[-1, 16], [-16, 9]], AL.is_equal, 16, 1)
-    ms(R("bm"), 0.0)
+    ms(R("pb"), 0.0)
+    if P["zd"]:
+        o = dma("y", [(A(R("bm", a, b)), A(R("pb", 0, b - a))) for a, b in ((0, V), (V, 2416))], [R("pb")], [R("bm", 0, 2416)], 256 * 2416)
+        ops[o]["behind"].append(loads[P["zd"]])
+    else:
+        ms(R("bm", 0, 2416), 0.0)
     cp("s", R("bm", 0, 2304, 16), R("btmp"))
+
+    def zero(r):
+        return iota(r, [[0, cnt(r)]], 0, 0) if P["zg"] else ms(r, 0.0)
     ms(R("cs"), 0.0)
     sel(R("gsel", 0, 8), R("ones", 0, 8), [[-16, 8]], AL.is_ge, 0, 1)
     sel(R("gsel", 8, 16), R("gsel", 0, 8), [[16, 8]], AL.is_ge, 15, -1)
@@ -248,22 +312,21 @@ def build(core, T, topo, both=False):
 
     def c_(base, a, s, w=32):
         return R("cs", base + a, base + w, s)
+    el, er, ed = [R("cs", e + 16, e + 144, 16) for e in (EL, ER, ED)]
     tt(c_(SC, 0, 1), idn(0, 4), idn(1, 4), AL.add)
-    tt(R("cs", EL + 16, EL + 144, 16), c_(SC, 0, 4), c_(SC, 2, 4), AL.add)
-    tt(R("cs", ER + 16, ER + 144, 16), c_(SC, 1, 4), c_(SC, 3, 4), AL.add)
+    tt(el, c_(SC, 0, 4), c_(SC, 2, 4), AL.add)
+    tt(er, c_(SC, 1, 4), c_(SC, 3, 4), AL.add)
     for base, o_ in ((SP, AL.add), (SN, AL.subtract)):
         act(c_(base, 0, 1), c_(SC, 0, 1), AF.Copy, scale=-1.0)
         for j in (2, 3):
             tt(c_(base, j, 4), c_(base, j, 4), idn(11, 16), o_)
-    tt(c_(SD, 0, 2, 16), c_(SC, 0, 4), idn(3, 16), AL.subtract)
-    tt(c_(SD, 1, 2, 16), c_(SC, 2, 4), idn(7, 16), AL.subtract)
-    ed = R("cs", ED + 16, ED + 144, 16)
     act(R("gsel", 0, 8), idn(6, 16), AF.Copy, scale=1536.0)
     act(R("btmp", 0, 8), idn(11, 16), AF.Copy, scale=-272.0)
-    tt(ed, idn(3, 16), idn(7, 16), AL.add)
-    tt(ed, ed, R("gsel", 0, 8), AL.add)
-    tt(R("cs", EN + 16, EN + 144, 16), R("cs", ER + 16, ER + 144, 16), R("btmp", 0, 8), AL.add)
-    KK, ONE, HI, BM, BP = [R("col", k, k + 1) for k in range(5)]
+    vv = R("btmp", 16, 24)
+    tt(vv, idn(3, 16), idn(7, 16), AL.add)
+    tt(ed, vv, R("gsel", 0, 8), AL.add)
+    tt(R("cs", EN + 16, EN + 144, 16), er, R("btmp", 0, 8), AL.add)
+    KK, ONE, HI, BM, BP, KQ, LO, UP = [R("col", k, k + 1) for k in range(8)]
     iota(R("ki", 0, 1), [[0, 1]], 0, 1)
     ts(R("ki", 4, 5), R("ki", 0, 1), 15, None, AL.bitwise_and)
     cp("v", KK, R("ki", 4, 5))
@@ -272,175 +335,195 @@ def build(core, T, topo, both=False):
     red(HI, R("btmp", 8, 16))
     act(BM, HI, AF.Copy, scale=-1536.0)
     act(BP, HI, AF.Copy, scale=1536.0)
-    KQ = R("col", 6, 7)
     act(KQ, KK, AF.Copy, scale=-4096.0)
-    iota(R("v2", 112, 208), [[128, 12], [0, 8]], 256, 1)
-    iota(R("v2", 208, 224), [[128, 2], [0, 8]], 0, 1)
-    if P["mut"]:
-        tt(R("btmp", 16, 24), idn(3, 16), idn(7, 16), AL.add)
-    else:
-        iota(R("v2", 224, 416), [[128, 12], [0, 16]], 256, 1)
-    for j in range(2):
-        act(c_(SR, j, 2, 16), R("cs", ER + 16, ER + 144, 16), AF.Copy, scale=4096.0 - 8192.0 * j if P["mut"] else 1.0)
-        if P["mut"]:
-            act(c_(SV, j, 2, 16), R("btmp", 16, 24), AF.Copy, scale=8192.0 * j - 4096.0)
-    iota(R("vw", 192, 288), [[16, 96]], 256, 0)
-    act(R("vn", 0, 96), R("vw", 192, 288), AF.Copy, scale=-1.0)
-    ts(R("vw", 96, 192), R("vw", 192, 288), KK, float(ZO - Z8), AL.add, AL.add)
-    RS = P["rs"]
-    if RS:
-        ms(R("vn", 96, 96 + RS // 16), 0.0)
-        ms(R("vn", 96 + RS // 16, 192), -float(RS))
-    ms(R("pb"), 0.0)
-    dma("y", [(A(R("pa", 0, V)), A(R("pb"))), (A(R("pa", V, V + H)), A(R("pb", 0, H)))], [R("pb")], [R("pa")], 458752)
+    iota(R("v2"), [[128, 12], [0, 8]], 256, 1)
+
+    def w_(k, r):
+        return R("wk", 128 * k + r, 128 * k + 128, 16)
+    zero(R("wk"))
+    for r, x in enumerate((4096.0, -4096.0, -256.0, 256.0)):
+        act(w_(1, r), er, AF.Copy, scale=x)
+        act(w_(0, r), vv, AF.Copy, scale=-x)
+    for r, j, k in ((0, 0, 15), (2, 2, 7)):
+        tt(w_(0, r), w_(0, r), c_(SC, j, 4), AL.add)
+        tt(w_(0, r), w_(0, r), idn(k, 16), AL.subtract)
+    cp("s", w_(0, 4), idn(3, 16))
+    cp("s", w_(0, 5), idn(7, 16))
+    tt(R("btmp", 24, 32), idn(2, 16), idn(3, 16), AL.add)
+    red(UP, R("btmp", 24, 32))
+    ts(UP, UP, -1920.0, 2048.0, AL.mult, AL.add)
+    act(LO, UP, AF.Copy, scale=-1.0)
+    iota(R("vw", 96, 192), [[16, 96]], 256, 0)
+    act(R("vn"), R("vw", 96, 192), AF.Copy, scale=-1.0)
+    ts(R("vw", 0, 96), R("vw", 96, 192), KK, float(ZO - Z8), AL.add, AL.add)
     ms(R("pb", 11, V, 16), 1.0)
-    ts(R("pb", 3, V, 16), R("v2", 112, 208), KK, None, AL.subtract)
-    act(R("pb", 7, V, 16), R("v2", 112, 208), AF.Identity, bias=KK, scale=0.0)
-    ts(R("pa", 1, 1792, 16), R("v2", 112, 224), KK, None, AL.subtract)
-    act(R("pa", 2, 1792, 16), R("v2", 112, 224), AF.Identity, bias=KK, scale=0.0)
-    tr([(R("pt", 128 * b, 128 * b + 128), R("pa", V + 128 * b, V + 128 * b + 128)) for b in range(2)])
-    cp("s", R("a1", 0, H), R("pt", 0, H))
+    for c in (3, 15):
+        ts(R("pb", c, V, 16), R("v2"), KK, None, AL.subtract)
+    act(R("pb", 7, V, 16), R("v2"), AF.Identity, bias=KK, scale=0.0)
+    iota(R("a2", 0, H), [[1, H]], 0, 0)
+    act(R("a1", 0, H), R("a2", 0, H), AF.Copy, scale=ONE)
     dma("y", [(A(R(a, 0, H)), A(R("a1", 0, H))) for a in ("a2", "a4")], [R("a1", 0, H)], [R("a2", 0, H), R("a4", 0, H)], 131072)
-    mw = 256
-    sel(R("id2", 0, mw), R("ones", 0, mw), [[0, mw // 128], [-1, 128]], AL.is_equal, 0, 1)
-    SCALE = P["scale"]
-    for t, m_ in enumerate(("mvb", "mvf")):
-        for c, x in ((0, 1.125), (256, -0.125)):
-            act(R(m_, c, c + mw), R("id2", 0, mw), AF.Copy, scale=x * SCALE[t + 1] / SCALE[t])
-    iota(R("tt", -16, H - 1), [[0, H + 15]], 0, 0)
-    iota(R("tt", H + V, W), [[0, H]], 0, 0)
+    sel(R("mvf", 128, 384), R("ones"), [[0, 2], [-1, 128]], AL.is_equal, 0, 1)
+    PM = P["pm"]
+    SCALE = [1.0] * PM + [(-8.0) ** (t - RO) for t in range(PM, RO + 1)]
+    for t in range(PM):
+        for c, x in ((0, 1.125), (128, -0.125)):
+            act(R("mv%d" % t, c, c + 128), R("ident"), AF.Copy, scale=x * SCALE[t + 1] / SCALE[t])
+    act(R("mvf", 0, 128), R("ident"), AF.Copy, scale=-9.0)
+    if P["prod"]:
+        act(R("bk"), R("ident"), AF.Copy, scale=-0.5)
+    if P["prod"] > 1:
+        ts(R("hk", 0, 128), R("ident"), -0.5, None, AL.mult)
+        cp("v", R("hk", 128, 256), R("ident"))
+    if PM > 1:
+        ts(R("hk", 256, 384), R("ident"), -0.125 * SCALE[2], None, AL.mult)
+    zero(R("tt", -16, H - 1))
+    zero(R("tt", H + V, W))
     for k in range(RO):
         for c in (0, ZO + W):
-            iota(R("z%d" % k, c, c + 16), [[0, 16]], 4096, 0)
+            if k < P["far"]:
+                ms(R("z%d" % k, c, c + 16), 4096.0)
+            else:
+                iota(R("z%d" % k, c, c + 16), [[0, 16]], 4096, 0)
 
     cp("v", lst(-1, LL), R("lw", 0, 96), bias=16.0)
-    for a, b in ((0, RS), (RS, V)):
-        if b:
-            ts(lst(-1, LR, a // 16, b // 16), R("lw", 96 + a // 16, 96 + b // 16), -float(H + a), None, AL.add)
+    cp("v", lst(-1, LR), R("lw", 96, 192), bias=-float(H))
     big = 1.5 * 2.0 ** 27
     ts(R("wp", 0, 192), R("lw"), big, big, AL.add, AL.subtract)
     tt(R("wp", 192, 384), R("lw"), R("wp", 0, 192), AL.subtract)
-    ts(R("wp", 384, 386), R("gl", 3, 100, 96), big, big, AL.add, AL.subtract)
-    tt(R("wp", 386, 388), R("gl", 3, 100, 96), R("wp", 384, 386), AL.subtract)
+    ts(R("wp", 388, 390), R("gl", 3, 100, 96), big, big, AL.add, AL.subtract)
+    ts(R("wp", 384, 386), R("gl", 3, 100, 96), big, big + V, AL.add, AL.subtract)
+    tt(R("wp", 386, 388), R("gl", 3, 100, 96), R("wp", 388, 390), AL.subtract)
     parts = [(0, 0), (4, 96), (8, 192), (12, 288)]
 
     def bv(i, kk):
         return R("bm", 144 * i + 16 - kk, 144 * i + 144 - kk)
+    turns = (16, -112) if rotl else (0,)
+    if P["pe0"]:
+        cp("s", R("sh", 1, 128), R("ident", 0, 127))
+        ms(R("sh", 0, 128, 16), 0.0)
+        p = tile("c0")
+        mm([(R(p, 1, 192), [(R("sh"), R("wp", c + 1, c + 192)) for c in (0, 192)] + [(bv(15, 0), R("wp", c, c + 191)) for c in (0, 192)])])
+        cp("v", lst(-1, LCL, 16, V), R(p, 1, 96), bias=17.0)
+        cp("v", lst(-1, LCR, 16, V), R(p, 97, 192), bias=1.0 - H)
+        p = tile("c1")
+        mm([(R(p, 0, 2), [(R("sh"), R("wp", c, c + 192, 96)) for c in (0, 192)] + [(bv(15, k), R("wp", c, c + 2)) for c in (384, 386) for k in turns])])
+        cp("v", lst(-1, LCL, 0, 16), R(p, 0, 1), bias=17.0)
+        cp("v", lst(-1, LCR, 0, 16), R(p, 1, 2), bias=1.0 - H)
     for k in range(4):
-        mm([(ps(k, 96 * j, 96 * j + 96), [(bv(4 * k + j, kk), R("wp", c, c + 96)) for kk, c in parts]) for j in range(4)])
+        p = tile("t0")
+        mm([(R(p, 96 * j, 96 * j + 96), [(bv(4 * k + j, kk), R("wp", c, c + 96)) for kk, c in parts]) for j in range(4)])
         for j in range(4):
-            cp("s", R("tt", H + 4 * k + j, H + V, 16), ps(k, 96 * j, 96 * j + 96), bias=ONE)
-    mm([(ps(5, 0, 1), [(bv(15, 4 * j + turn), R("wp", 384 + j, 385 + j)) for j in range(4) for turn in ((16, -112) if rotl else (0,))])])
-    act(R("col", 5, 6), HI, AF.Identity, bias=ONE, scale=-1536.0)
-    cp("s", R("tt", H - 1, H), ps(5, 0, 1), bias=R("col", 5, 6))
-
-    def blk(tab, s, first=0):
-        return R(tab, first + 128 * s, first + 128 * s + 128)
-    S = P["split"]
-    HV = [(0, S), (S, V)]
-    rebase = [(R("ident"), R("vn", 96, 192))] if RS else []
-
-    def pair(bank, h):
-        return ps(bank, -S // 16, 0) if h == 0 else ps(bank, 0, (V - S) // 16) if h == 1 else ps(bank, -S // 16, (V - S) // 16)
-
-    def rwin(name, first, end, a):
-        return R(name, first + (RS if a >= RS else 0), end)
+            cp("s", R("tt", H + 4 * k + j, H + V, 16), R(p, 96 * j, 96 * j + 96), bias=ONE)
+    p = R(tile("t1"), 0, 1)
+    mm([(p, [(bv(15, 4 * j + k), R("wp", 384 + j, 385 + j)) for j in range(4) for k in turns])])
+    cp("s", R("tt", H - 1, H), p, bias=ONE)
 
     def prepare(t):
         d = 1 if t % 2 == 0 else -1
-        src, dst, gu = lst(t - 1, LL, 0, 192), lst(t - 1, LCL, 0, 192), R("gu", 2 * t, 2 * t + 2)
-        i, c = (0, H - 1) if d > 0 else (15, H + V)
-        mm([(ps(4, 192 + j, 193 + j), [(R("cs", e + 16 - i, e + 144 - i), R("tt", c, c + 1))]) for j, e in enumerate((EL, EN))])
-        ts(gu, ps(4, 192, 194), 16.0, float(H + V + 16), AL.add, AL.min)
-        up, dn = int(d > 0), int(d < 0)
-        dma("y", [(T.lu[a + up:b + up, dst[1]:dst[2]], T.lu[a + dn:b + dn, src[1]:src[2]]) for a, b in ((0, 112), (112, 127))], [src], [dst], 49152)
-        pr = []
-        for j in range(2):
-            d0, s0, g0 = dst[1] + 96 * j, src[1] + 96 * j, dst[1] + 96 * j + 95 * dn
-            pr += [(T.lu[i:128:16, d0 + up:d0 + up + 95], T.lu[15 - i:128:16, s0 + dn:s0 + dn + 95]), (T.lu[i:128:16, g0:g0 + 1], T.gu[i:128:16, gu[1] + j:gu[1] + j + 1])]
-        ops[dma("y", pr, [src, gu], [dst], 4096)]["cost"] = ("d", 1, 16384)
-        ts(dst, dst, float(d), None, AL.add)
-        mm([(ps(3, 32 * s, 32 * s + 32), [(blk("tt", s, H), c_(SC, 0, 1))]) for s in range(12)])
-        cp(P["cur"], R("pb", 0, V, 4), ps(3, 0, 384))
-        mm([(ps(2, 32 * s, 32 * s + 32), [(blk("tt", s, H - d), c_(SC, 0, 1)), (blk("tt", s, H), c_(SP if d > 0 else SN, 0, 1))]) for s in range(12)])
+        if t or not P["pe0"]:
+            src, dst, gu = lst(t - 1, LL, 0, 2 * V), lst(t - 1, LCL, 0, 2 * V), R("gu", 2 * t, 2 * t + 2)
+            i, c = (0, H - 1) if d > 0 else (15, H + V)
+            p = tile("gu")
+            mm([(R(p, j, j + 1), [(R("cs", e + 16 - i, e + 144 - i), R("tt", c, c + 1))]) for j, e in enumerate((EL, EN))])
+            ts(gu, R(p, 0, 2), 16.0, float(H + V + 16), AL.add, AL.min)
+            up, dn = int(d > 0), int(d < 0)
+            dma("y", [(T.lu[a + up:b + up, dst[1]:dst[2]], T.lu[a + dn:b + dn, src[1]:src[2]]) for a, b in ((0, 112), (112, 127))], [src], [dst], 49152)
+            pr = []
+            for j in range(2):
+                d0, s0, g0 = dst[1] + 96 * j, src[1] + 96 * j, dst[1] + 96 * j + 95 * dn
+                pr += [(T.lu[i:128:16, d0 + up:d0 + up + 95], T.lu[15 - i:128:16, s0 + dn:s0 + dn + 95]), (T.lu[i:128:16, g0:g0 + 1], T.gu[i:128:16, gu[1] + j:gu[1] + j + 1])]
+            ops[dma("y", pr, [src, gu], [dst], 4096)]["cost"] = ("d", 1, 16384)
+            ts(dst, dst, float(d), None, AL.add)
+        p = tile("cur")
+        mm([(R(p, 32 * s, 32 * s + 32), [(blk("tt", s, H), c_(SC, 0, 1))]) for s in range(12)])
+        cp(P["cur"], R("pb", 0, V, 4), R(p, 0, 384))
+        p = tile("dif")
+        mm([(R(p, 32 * s, 32 * s + 32), [(blk("tt", s, H - d), c_(SC, 0, 1)), (blk("tt", s, H), c_(SP if d > 0 else SN, 0, 1))]) for s in range(12)])
+        return p
 
-    thirds = [(0, 512), (512, 1024), (1024, V)]
-
-    staged, ydone = [0], [0]
-
-    def stage():
-        staged[0] += 1
-        return ps(staged[0] % 2, 0, 512)
-
-    def ypart(t, a, b):
-        tm, p = "tm", stage() if t < RO - 1 else ps(2 + ydone[0] % 2, 0, b - a)
+    def ypart(t):
         sc = abs(SCALE[t])
-        act(p, R("ds", a, b), AF.Exp, bias=-math.log(sc * (9.0 if SCALE[t] < 0 else 1.0)), scale=-1.0 / sc)
-        tt(R(tm, a, b), p, R("mf", a, b), AL.mult)
-        ydone[0] += 1
-        if t == RO - 1 or P["y3"]:
-            dma("g" if t else "y", [(T.ye[:, a:b], A(R(tm, a, b)))], [R(tm, a, b)], [R("ye", a, b)], 512 * (b - a), add=t > 0)
-        elif ydone[0] % 3 == 0:
-            dma("g" if t else "y", [(T.ye[:], A(R(tm)))], [R(tm)], [R("ye")], 786432, add=t > 0)
+        for a, b, x in of("yy", t):
+            p = R(tile("y"), 0, b - a)
+            if t == 0 and P["r0"]:
+                mm([(p, [(R("ident"), R("xb", a, b))])])
+                tt(R("mf", a, b), p, R("ds", a, b), AL.mult)
+            else:
+                o = act(p, R("ds", a, b), AF.Exp, bias=-math.log(sc * (9.0 if SCALE[t] < 0 else 1.0)), scale=-1.0 / sc)
+                ops[o]["behind"] += [warm, last[a // 128], last[(b - 1) // 128]]
+                tt(R("mf", a, b), p, R("mf", a, b), AL.mult)
+            if t == RO - 1 or P["y3"]:
+                dma("g" if t else "y", [(T.ye[:, a:b], A(R("mf", a, b)))], [R("mf", a, b)], [R("ye", a, b)], 512 * (b - a), add=t > 0)
+        if t < RO - 1 and not P["y3"]:
+            dma("g" if t else "y", [(T.ye[:], A(R("mf")))], [R("mf")], [R("ye")], 786432, add=t > 0)
 
-    prepare(0)
+    dif = prepare(0)
+    last = {}
     for t in range(RO):
-        z, zc, dr, ma, mb = "z%d" % t, "zc" if t else "xb", "dr%d" % (t % 2), "ma", "mb"
+        z, zc, dr, ma, mb, u = "z%d" % t, "zc" if t else "xb", "dr%d" % (t % 2), "ma", "mb", "u%d" % (t % 2)
+        if t == 0 and P["r0"]:
+            dr = "bm"
 
         def own(a=0, b=V):
             return R(z, ZO + H + a, ZO + H + b)
-        u = "u%d" % (t % 2)
-        pieces = P[("ww", "wwu", "wwu", "wwl")[t]]
-        for a, b in (P["u"] if SCALE[t] < 0 else [x[:2] for x in pieces if x[2] in "vs"]):
-            act(R(u, H + a, H + b), own(a, b), AF.Copy, scale=-9.0)
+        pieces = of("ww", t)
+        for a, b, x in of("u", t) if t >= PM else ():
+            cp("s", R(u, H + a, H + b), own(a, b), scale=-9.0)
         tab, t0 = (z, ZO) if SCALE[t] > 0 else (u, 0)
         if SCALE[t] < 0:
-            act(R(u, 0, H), R(z, ZO, ZO + H), AF.Copy, scale=-9.0)
-        sub = {}
-        for side, d_ in (("R", dr), ("L", "dl")):
-            for what, c0 in (("cur", 0), ("can", V)):
-                lc = {"curR": LR, "curL": LL, "canR": LCR, "canL": LCL}[what + side]
-                for a, b, x in of(what + side, t):
-                    win = rwin(z, ZO + H, Z8, a) if side == "R" else R(z, 0, ZO + H + b)
-                    out = R(d_, c0 + a, c0 + b)
+            cp("s", R(u, 0, H), R(z, ZO, ZO + H), scale=-9.0)
+        one = R("mvf", 128, 256) if t else R("ident")
+        for side, d_, lc in (("R", dr, LR), ("L", "dl", LL)):
+            nn = "n" + side.lower()
+            for k, (a, b) in enumerate(x[:2] for x in of("cur" + side, t)):
+                win = R(z, ZO + H, Z8) if side == "R" else R(z, 0, ZO + H + b)
+                cur, can = lst(t - 1, lc, a, b), lst(t - 1, lc + LCL - LL, a, b)
+                if side == "L" and t < P["prod"]:
+                    x = of("prodL", t)[k]
+                    ne, ce, p = R("g1" if t == 0 else "hg" if x == "v" else "dl", a, b), R("hc" if t else "g2", a, b), R(tile("pr"), 0, b - a)
+                    o = gcp(ne, win, cur, x, -1.0)
+                    gtt(ce, win, can, ne, AL.add)
+                    sums(p, (one, own(a, b)), (R("hk", 128, 256) if ne[0] == "hg" else one, ne), (R("hk", 0, 128) if t else R("bk"), ce), ahead=o)
+                    tt(R(nn, a, b), p, ce, AL.mult)
+                    ts(R(nn, a, b), R(nn, a, b), 0.0, None, AL.is_gt)
+                    continue
+                for what, off in (("cur", cur), ("can", can)):
+                    x = of(what + side, t)[k][2]
+                    out = R(d_, a, b) if what == "cur" else R(d_, V + a, V + b)
+                    keep = what == "cur" or d_ == "bm"
+                    src, p = out, None
                     if x == "p":
-                        got, one = (out, R("mvf", 256, 384)) if t else (R({LR: "g1", LL: "g2", LCL: "wb"}[lc], a, b), R("ident"))
-                        act(got, win, AF.Copy, scale=-1.0, off=lst(t - 1, lc, a // 16, b // 16))
-                        p = ps(4 + len(sub) % 2, 0, b - a)
-                        sub[lc, a] = p
-                        mm([(p, [(one, own(a, b))])], stop=False)
-                        mm([(p, [(one, got)])], start=False)
-                        act(out if what == "cur" else p, p, AF.Abs)
-                        if what == "can":
-                            tt(R("nl", a, b), p, R(d_, a, b), AL.is_lt)
-                        continue
-                    if x == "s":
-                        act(out, win, AF.Copy, scale=-1.0, off=lst(t - 1, lc, a // 16, b // 16))
-                        dma("g", [(A(out), A(own(a, b)))], [own(a, b), out], [out], 512 * (b - a), add=True)
+                        got = out if t or d_ == "bm" else R("g2" if what == "cur" else "wb", a, b)
+                        src = p = R(tile("sub"), 0, b - a)
+                        sums(p, (one, own(a, b)), (one, got), ahead=gcp(got, win, off, "s", -1.0))
+                        if side == "R" and not keep:
+                            cp("s", out, p)
+                    elif x == "s":
+                        gcp(out, win, off, "s", -1.0)
+                        dma("g", [(A(out), A(own(a, b)))], [own(a, b), out], [out], (256 if d_ == "bm" else 512) * (b - a), add=True)
                     else:
-                        gtt(out, win, lst(t - 1, lc, a // 16, b // 16), R(zc, a, b), AL.subtract)
-                    if what == "cur":
-                        act(out, out, AF.Abs)
-        for side, ci in P["seq"].split():
-            a, b = thirds[int(ci)]
-            if side == "Y":
-                if t:
-                    ypart(t - 1, a, b)
-                continue
-            if side == "L" and (LCL, a) in sub:
-                continue
-            d_, p = dr if side == "R" else "dl", stage()
-            act(p, R(d_, V + a, V + b), AF.Abs)
-            tt(R("n" + side.lower(), a, b), p, R(d_, a, b), AL.is_lt)
+                        gtt(out, win, off, R(zc, a, b), AL.subtract)
+                    if keep:
+                        act(out, src, AF.Abs)
+                        p = None
+                    if what == "can":
+                        p = p or R(tile("abs"), 0, b - a)
+                        if keep:
+                            mm([(p, [(one, out)])])
+                        else:
+                            act(p, src, AF.Abs)
+                        tt(R(nn, a, b), p, R(d_, a, b), AL.is_lt)
         ll, lr = "ll%d" % t, "lr%d" % t
         done = {"R": set(), "L": set()}
         late = False
-        for sides, a, b in P["dec"]:
-            mm([(ps(3, 32 * s, 32 * s + 32), [(blk("n" + x.lower(), s), R("cs", QQ + (x == "L"), QQ + (x == "L") + 32)) for x in sides]) for s in range(a, b)])
+        for sides, a, b in of("dec", t):
+            p = tile("cnt")
+            mm([(R(p, 32 * s, 32 * s + 32), [(blk("n" + x.lower(), s), R("cs", QQ + (x == "L"), QQ + (x == "L") + 32)) for x in sides]) for s in range(a, b)])
             j, st = int(sides == "R"), 2 // len(sides)
             dec = R("pb", 128 * a + 4 * j + 2, 128 * b, 4 * st)
-            ts(dec, ps(3, 32 * a + j, 32 * b, st), 8.5, None, AL.is_gt)
-            tt(R("pb", 128 * a + 4 * j + 1, 128 * b, 4 * st), ps(2, 32 * a + j, 32 * b, st), dec, AL.mult)
+            ts(dec, R(p, 32 * a + j, 32 * b, st), 8.5, None, AL.is_gt)
+            tt(R("pb", 128 * a + 4 * j + 1, 128 * b, 4 * st), R(dif, 32 * a + j, 32 * b, st), dec, AL.mult)
             before = {x: set(done[x]) for x in done}
             for x in sides:
                 done[x].update(range(a, b))
@@ -450,159 +533,155 @@ def build(core, T, topo, both=False):
             elif late and 11 in done["L"] and 11 not in before["L"]:
                 exchange([(right, blk("pb", 11), R("lx", 16 * rotr, 16 * rotr + 128), R("lx", 16 * rotl, 16 * rotl + 128))], 32768)
                 if rotl:
-                    sel(R("lx", 0, 16), R("lx", 128, 144), [[0, 16]], AL.is_gt, 1, 0)
+                    wrap("lx", 0, 128, "l")
             if {0, 1} <= done["R"] & done["L"] and not {0, 1} <= before["R"] & before["L"]:
                 exchange([(left, R("pb", 0, H), R(lr, 0, H), R(lr, 0, H))], 65536)
         if rotl:
-            sel(R(ll, 0, 16), R(ll, 128, 144), [[0, 16]], AL.is_gt, 1, 0)
-            sel(R(ll, 128, 144), R(ll, 256, 272), [[0, 16]], AL.is_gt, 1, 0)
+            wrap(ll, 0, 128, "l")
+            wrap(ll, 128, 256, "l")
         if rotr:
-            sel(R(lr, 256, 272), R(lr, 128, 144), [[0, 16]], AL.is_gt, 1, 0)
-            sel(R(lr, 128, 144), R(lr, 0, 16), [[0, 16]], AL.is_gt, 1, 0)
-        o = 16 * rotr
-        byp = []
+            wrap(lr, 256, 128, "r")
+            wrap(lr, 128, 0, "r")
+        HV = [x[:2] for x in of("hv", t)]
         for h, (a, b) in enumerate(HV):
             bs = range(a // 128, b // 128)
-            tr([(blk("pt", s, H), blk("pb", s)) for s in bs])
-            cp(P["t"][1 + h], R("tt", H + a, H + b), R("pt", H + a, H + b))
-            p = ps(4 + h, 128, 128 + (b - a) // 16)
-            ext(p, EL, "tt", H, a // 16, b // 16)
-            cp("v", lst(t, LL, a // 16, b // 16), p, bias=16.0)
-            byp.append((bs, 128 * h - a // 8, 384 - 384 * h - a // 8))
-            if not P["mut"]:
-                mm([(ps(2, byp[h][2] + 16 * s, byp[h][2] + 16 * s + 16), [(blk("tt", s, H), c_(SD, 0, 1, 16))]) for s in bs])
-        mm([(ps(5, 288, 384), terms(ER, "tt", H) + rebase)])
-        ext(ps(5, 384, 480), ED, "tt", H)
-        for a, b in (((0, 96), (96, 192)) if P["ld"] else ((0, 192),)):
-            ts(lst(t, LR, a, b), ps(5, 288 + a, 288 + b), -float(H), None, AL.add)
-        for a, b in P["ds"]:
-            act(R("ds", a, b), R(dr), AF.Abs, off=lst(t, LD, a // 16, b // 16))
-        for h, (a, b) in enumerate(HV):
-            bs, c2, c1 = byp[h]
-            early = H if P["g1e"] and h == 0 else a
-            if early > a:
-                gcp(R("g1", H, b), R("tt", -16, H + b), lst(t, LL, H // 16, b // 16), 0)
-            if h == 0:
-                tr([(blk("pt", s), blk(ll, s)) for s in range(2)])
-                cp(P["t"][0], R("tt", 0, H), R("pt", 0, H), bias=BM)
-            e_ = H if early > a else b
-            gcp(R("g1", a, e_), R("tt", -16, H + e_), lst(t, LL, a // 16, e_ // 16), min(of("g1", t)[h], e_ - a))
-            if P["mut"]:
-                mm([(ps(3, c2 + 16 * s, c2 + 16 * s + 16), [(blk("tt", s, H), c_(SV, 0, 1, 16)), (blk("tt", s, H), c_(SD, 0, 1, 16)), (blk("g1", s), c_(SR, 0, 1, 16))])
-                    for s in bs])
-                ts(R("pa", a, b, 8), ps(3, c2 + a // 8, c2 + b // 8), -2048.0, 2048.0, AL.max, AL.min)
+            p = tile("tt", B)
+            tr([(blk(p, s - bs[0]), blk("pb", s)) for s in bs])
+            cp(P["t"][1 + min(h, 1)], R("tt", H + a, H + b), R(p, 0, b - a))
+            cp("v", lst(t, LL, a, b), ext("ll", EL, "tt", H, a, b), bias=16.0)
+        cp("v", lst(t, LR), ext("lr", ER, "tt", H), bias=-float(H))
+        cp("v", lst(t, LD), ext("ld", ED, "tt", H), bias=-float(H))
+        if t:
+            ypart(t - 1)
+        for a, b, x in of("ds", t):
+            if dr == "bm":
+                ops[act(R("ds", a, b), R(dr), AF.Exp, scale=-1.0, off=lst(t, LD, a, b))]["behind"].append(warm)
             else:
-                mm([(ps(3, c2 + 16 * s, c2 + 16 * s + 16), [(blk("g1", s), c_(SR, 0, 1, 16))]) for s in bs])
-                mut = R("sm", a // 8, b // 8)
-                tt(mut, ps(3, c2 + a // 8, c2 + b // 8), R("v2", 224 + a // 8, 224 + b // 8), AL.is_equal)
-                tt(R("pa", a, b, 8), ps(2, c1 + a // 8, c1 + b // 8), mut, AL.mult)
-            tr([(blk("pt", s, H), blk("pa", s)) for s in bs])
-            cp(P["c"][h], R("a1", H + a, H + b), R("pt", H + a, H + b))
+                act(R("ds", a, b), R(dr), AF.Abs, off=lst(t, LD, a, b))
+        g1, got = of("g1", t), {}
+        for y in ([g1[1], None, g1[0]] + g1[2:] if g1[0][1] == H else [None] + g1):
+            if y is None:
+                p = tile("gl", B)
+                tr([(blk(p, s), blk(ll, s)) for s in range(2)])
+                cp(P["t"][0], R("tt", 0, H), R(p, 0, H), bias=BM)
+                continue
+            a, b, x = y
+            o = gcp(R("g1", a, b), R("tt", -16, H + b), lst(t, LL, a, b), x)
+            got.update((s, o) for s in range(a // 128, b // 128))
+        for h, (a, b) in enumerate(HV):
+            for c in range(a, b, 512):
+                e = min(b, c + 512)
+                p = R(tile("ch"), 0, e - c)
+                sums(p, (R("wk", 0, 128), R("tt", H + c, H + e)), (R("wk", 128, 256), R("g1", c, e)), ahead=got[c // 128])
+                ts(R("a1", H + c, H + e), p, LO, UP, AL.max, AL.min)
         ghosts = False
         for a, b, x in of("g2", t):
             if b > V - H and not ghosts:
-                tr([(blk("pt", s, H + V), blk(lr, s, o)) for s in range(2)])
-                cp(P["t"][3], R("tt", H + V, W), R("pt", H + V, W), bias=BP)
+                p = tile("gr", B)
+                tr([(blk(p, s), blk(lr, s, 16 * rotr)) for s in range(2)])
+                cp(P["t"][3], R("tt", H + V, W), R(p, 0, H), bias=BP)
                 ghosts = True
-            gcp(R("g2", a, b), rwin("tt", H, W, a), lst(t, LR, a // 16, b // 16), b - a if x == "v" else 0)
+            gcp(R("g2", a, b), R("tt", H, W), lst(t, LR, a, b), x)
         if late:
-            tr([(blk("pt", 0), blk("lx", 0))])
-            cp("s", R("tt", H - 1, H), R("pt", 127, 128), bias=BM)
+            p = tile("lx", B)
+            tr([(blk(p, 0), blk("lx", 0))])
+            cp("s", R("tt", H - 1, H), R(p, 127, 128), bias=BM)
         twin(R(z, Z8, Z8 + H), R(z, ZO, ZO + H))
         gh = R(tab, t0, t0 + H)
         if t:
             dma("y", [(A(R(m_, 0, H)), A(gh)) for m_ in (ma, mb)], [gh], [R(ma, 0, H), R(mb, 0, H)], 262144)
         else:
-            cp("s", R(ma, 0, H), gh)
-            twin(R(mb, 0, H), R(ma, 0, H))
+            dma("g", [(A(R(m_, 0, H)), A(gh)) for m_ in (ma, mb)], [gh], [R(ma, 0, H), R(mb, 0, H)], 262144)
         if SCALE[t] < 0:
             twin(R("mc0"), R(u, H, H + V))
         src = [(tab, t0), (ma, 0), (mb, 0), (ma, 0)]
-        dst = [(ma, H), (mb, H), (ma, H), ("mf", 0)]
+        dst = [(ma, H), (mb, H), (ma, H), ("xb" if dr == "bm" else "mf", 0)]
         tabs = [("a1", H), ("a2", H), ("a4", H), ("a8", 0), (z, Z8 + H)]
         for k in range(4):
-            bank = (0, 5, 4, 5)[k]
-            for h, (a, b) in enumerate(HV):
-                p = pair(bank, h) if k else ps(4 + h, 64, 64 + (b - a) // 16)
-                ext(p, EA, tabs[k][0], tabs[k][1], a // 16, b // 16)
-                cp("v", lst(t, LA1 + 96 * k, a // 16, b // 16), p)
-            for h, (a, b) in enumerate(HV):
-                nn, c0 = tabs[k + 1]
-                win = R(tabs[k][0], 0, H + b) if k < 3 else R(z, ZO, ZO + H + b)
-                gcp(R(nn, c0 + a, c0 + b), win, lst(t, LA1 + 96 * k, a // 16, b // 16), of(("a2", "a4", "a8", "z8")[k], t)[h])
-            for h, (a, b) in (enumerate(HV) if P["ls"] > 1 else [(2, (0, V))]):
-                a2, qq, pp, vc = [R(nn, c0 + a // 16, c0 + b // 16) for nn, c0 in (("sm", 192), ("sm", 288), ("sm", 384), ("vw", 96))]
+            def small(a, b):
+                return [R(nn, c0 + a // 16, c0 + b // 16) for nn, c0 in (("sm", 0), ("sm", 96), ("sm", 192), ("vw", 0))]
+            if k == 1:
+                for a, b, x in of("go", t):
+                    act(small(a, b)[1], ext("qq", EL, "g2", 0, a, b, [(R("ident"), R("vn", a // 16, b // 16))]), AF.Abs, bias=KQ, scale=4096.0)
+            for a, b, x in P.get("x%d" % k, of("hv", t)):
+                p = ext("a%d" % k, EA, tabs[k][0], tabs[k][1], a, b)
+                cp("v", lst(t, LA1 + 96 * k, a, b), p)
+                a2, qq, pp, vc = small(a, b)
                 if k == 1:
-                    cp("s", a2, pair(bank, h))
-                    p = ps(5, 192 + a // 16, 192 + b // 16)
-                    mm([(p, terms(EL, "g2", 0, a // 16, b // 16) + [(R("ident"), R("vn", a // 16, b // 16))])])
-                    act(qq, p, AF.Abs, bias=KQ, scale=4096.0)
+                    cp("s", a2, p)
                 if k == 2:
-                    tt(pp, a2, pair(bank, h), AL.subtract)
+                    tt(pp, a2, p, AL.subtract)
+                if k == 3:
+                    tt(a2, p, pp, AL.min)
+                    ts(lst(t, LS, a, b), a2, float(Z8 - ZO), None, AL.add)
+            if k == 2:
+                for a, b, x in of("go", t):
+                    a2, qq, pp, vc = small(a, b)
                     tt(pp, pp, qq, AL.mult)
                     tt(pp, pp, vc, AL.add)
-            if k == 3:
-                for h, (a, b) in (enumerate(HV) if P["ls"] else [(2, (0, V))]):
-                    mv = R("sm", 192 + a // 16, 192 + b // 16)
-                    tt(mv, pair(bank, h), R("sm", 384 + a // 16, 384 + b // 16), AL.min)
-                    ts(lst(t, LS, a // 16, b // 16), mv, float(Z8 - ZO), None, AL.add)
+            nn, c0 = tabs[k + 1]
+            for a, b, x in of(("a2", "a4", "a8", "z8")[k], t):
+                win = R(tabs[k][0], 0, H + b) if k < 3 else R(z, ZO, ZO + H + b)
+                gcp(R(nn, c0 + a, c0 + b), win, lst(t, LA1 + 96 * k, a, b), x)
             sn, s_ = src[k]
             dn, d_ = dst[k]
             cn = zc if k == 0 and SCALE[t] > 0 else "mc%d" % (k % 2)
-            for a, b in P["mcl" if t == RO - 1 else "mc"]:
-                gtt(R(dn, d_ + a, d_ + b), R(sn, s_, s_ + H + b), lst(t, LA1 + 96 * k, a // 16, b // 16), R(cn, a, b), AL.max)
-                if k < 3 and t == RO - 1 and P["twl"][k] == "s":
-                    cp("s", R("mc%d" % (1 - k % 2), a, b), R(dn, d_ + a, d_ + b))
-                elif k < 3:
-                    twin(R("mc%d" % (1 - k % 2), a, b), R(dn, d_ + a, d_ + b))
+            for a, b, x in of("mc", t):
+                o = gtt(R(dn, d_ + a, d_ + b), R(sn, s_, s_ + H + b), lst(t, LA1 + 96 * k, a, b), R(cn, a, b), AL.max)
+                last.update((s, o) for s in range(a // 128, b // 128))
+                if k < 3:
+                    twin(R("mc%d" % (1 - k % 2), a, b), R(dn, d_ + a, d_ + b), of("tw", t)[k])
         if t < RO - 1:
-            prepare(t + 1)
-        nz, mv_, ww = "z%d" % (t + 1), "mvf" if t else "mvb", "ww" if t else "wb"
-
+            dif = prepare(t + 1)
+        nz, mv_ = "z%d" % (t + 1), "mv%d" % t if t < PM else "mvf"
         lo, hi = sorted((0.0, 4.0 * SCALE[t + 1]))
 
-        def move(out, a, b, turn):
+        def move(out, a, b, x, o):
+            p = R(ww, a, b)
             if x in "pq":
-                p = stage()
-                p = (p[0], p[1], p[1] + b - a, 1)
-                mm([(p, [(R(mv_, turn, turn + 128), own(a, b))])], stop=False)
-                mm([(p, [(R(mv_, 256 + turn, 384 + turn), R(ww, a, b))])], start=False)
-            elif turn:
-                p = ps(3, 0, H)
-                mm([(p, [(R(mv_, 256 + turn, 384 + turn), R(ww, a, b))])])
+                p = R(tile("mv"), 0, b - a)
+                sums(p, (R(mv_, 0, 128), own(a, b)), (R("hk", 256, 384) if ww == "hg" else R(mv_, 128, 256), R(ww, a, b)), ahead=o)
+            top = R("col", 8 + t // 2, 9 + t // 2)
+
+            def on_s():
+                first = ops.pop(act(p, p, AF.Relu, bias=top, scale=-1.0))
+                o = act(out, p, AF.Relu, bias=top, scale=-1.0)
+                ops[o].update(first=first["fn"], cost=("e", 2 * cnt(p) + 160))
+                return o
+            if lo < 0:
+                return ts(out, p, lo, hi, AL.max, AL.min)
+            o = either("s" if x == "c" else "v", lambda: ts(out, p, lo, hi, AL.max, AL.min), on_s)
+            ops[o].update(rd=[p, top], wr=[out, p])
+        if lo == 0:
+            ms(R("col", 8 + t // 2, 9 + t // 2), hi)
+        for a, b, x in pieces:
+            win, off, ww = R(z, ZO, Z8 + H + b), lst(t, LS, a, b), "wb" if t == 0 else "hg" if t == 1 < PM and x == "q" else "ww"
+            if x in "pqs":
+                o = gcp(R(ww, a, b), win, off, "v" if x == "q" else "s")
+                if x == "s":
+                    dma("g", [(A(R(ww, a, b)), A(R(u, H + a, H + b)))], [R(u, H + a, H + b), R(ww, a, b)], [R(ww, a, b)], 512 * (b - a), add=True)
             else:
-                p = R(ww, a, b)
-            ts(out, p, lo, hi, AL.max, AL.min)
-        for ci, (a, b, x) in enumerate(pieces):
-            win = R(z, ZO, Z8 + H + (S if b <= S else V))
-            if x in "pq":
-                gcp(R(ww, a, b), win, lst(t, LS, a // 16, b // 16), b - a if x == "q" else 0)
-            elif x == "s":
-                gcp(R(ww, a, b), win, lst(t, LS, a // 16, b // 16), 0)
-                dma("g", [(A(R(ww, a, b)), A(R(u, H + a, H + b)))], [R(u, H + a, H + b), R(ww, a, b)], [R(ww, a, b)], 512 * (b - a), add=True)
-            else:
-                gtt(R(ww, a, b), win, lst(t, LS, a // 16, b // 16), R(u, H + a, H + b), AL.add)
+                o = gtt(R(ww, a, b), win, off, R(u, H + a, H + b), AL.add)
             if t == RO - 1:
-                move(R("z1", a, b), a, b, 0)
+                move(R("z1", a, b), a, b, x, o)
                 dma("y", [(T.xe[:, a:b], A(R("z1", a, b)))], [R("z1", a, b)], [R("xe", a, b)], 512 * (b - a))
                 continue
-            if a == 0 and rotl:
-                move(R("xs", 0, H), 0, H, 16)
-            if b == V and rotr:
-                move(R("xs", H, 2 * H), V - H, V, 112)
-            move(R(nz, ZO + H + a, ZO + H + b), a, b, 0)
-            if P["twin"][ci] == "y":
-                twin(R("zc", a, b), R(nz, ZO + H + a, ZO + H + b))
-            else:
-                cp(P["twin"][ci], R("zc", a, b), R(nz, ZO + H + a, ZO + H + b))
+            first, end = R(nz, ZO + H, ZO + 2 * H), R(nz, ZO + V, ZO + V + H)
+            turn = [("l", 0, 0, 16, first)] * (a == 0 and rotl) + [("r", H, V - H, 112, end)] * (b == V and rotr)
+            move(R(nz, ZO + H + a, ZO + H + b), a, b, x, o)
+            for only[0], c, e, k, new in turn:
+                p = R(tile("xs"), 0, H)
+                mm([(p, [(R("mvf", 128 + k, 256 + k), new)])])
+                cp(of("xs", t), R("xs", c, c + H), p)
+            only[0] = None
+            twin(R("zc", a, b), R(nz, ZO + H + a, ZO + H + b), of("tz", t)[pieces.index((a, b, x))])
             gl_, gr_ = R(nz, ZO, ZO + H), R(nz, ZO + H + V, ZO + W)
             if a == 0:
-                exchange([(left, R("xs", 0, H) if rotl else R(nz, ZO + H, ZO + 2 * H), gr_, gr_)], 131072)
+                exchange([(left, R("xs", 0, H) if rotl else first, gr_, gr_)], 131072, [first])
             if b == V:
-                exchange([(right, R("xs", H, 2 * H) if rotr else R(nz, ZO + V, ZO + V + H), gl_, gl_)], 131072)
-    for a, b in P["mcl"]:
-        ypart(RO - 1, a, b)
-    return ops
+                exchange([(right, R("xs", H, 2 * H) if rotr else end, gl_, gl_)], 131072, [end])
+    ypart(RO - 1)
+    return ops, tiles, place
 
 
 def bits(r):
@@ -611,28 +690,19 @@ def bits(r):
     return int.from_bytes(np.packbits(m).tobytes(), "big")
 
 
-def banks(o):
-    s = set()
-    for r in o["rd"] + o["wr"]:
-        if r[0] == "pt":
-            s.update(("pt", k) for k in range(r[1] // 1024, (r[2] - 1) // 1024 + 1))
-        elif r[0] == "ps":
-            s.update(("ps", k) for k in range(r[1] // 512, (r[2] - 1) // 512 + 1))
-    return s
-
-
 def depend(ops):
     hist = {}
     memo = {}
     deps = []
+    above = []
     for i, o in enumerate(ops):
         d = set(o["after"])
         new = []
         for lst_, w in ((o["rd"], False), (o["wr"], True)):
             for r in lst_:
-                if r not in memo:
-                    memo[r] = bits(r)
-                m = memo[r]
+                if r[1:] not in memo:
+                    memo[r[1:]] = bits(r)
+                m = memo[r[1:]]
                 for j, wj, mj in hist.get(r[0], ()):
                     if (w or wj) and (m & mj):
                         d.add(j)
@@ -643,26 +713,30 @@ def depend(ops):
                 h[:] = [(j, wj, mj & ~m) for j, wj, mj in h if mj & ~m]
             h.append((i, w, m))
         d.discard(i)
-        deps.append(sorted(d))
+        far = 0
+        for j in d:
+            far |= above[j]
+        deps.append(sorted(j for j in d if not far >> j & 1))
+        above.append(far | sum(1 << j for j in d))
     return deps
 
 
 def times(o, m):
-    c = o["cost"]
+    c, x = o["cost"], o["once"]
     if c[0] == "e":
-        x = 0.06 + max(64, c[1]) * m["c"]
+        x += 0.06 + max(64, c[1]) * m["c"]
     elif c[0] == "g":
-        x = 0.06 + c[1] * m["g"] * m["c"]
+        x += 0.06 + c[1] * m["g"] * m["c"]
     elif c[0] == "q":
-        x = 0.17 + 2 * c[1] * m["c"]
+        x += 0.17 + 2 * c[1] * m["c"]
     elif c[0] == "p":
-        x = 0.05 + c[1] * m["pe"]
+        x += 0.05 + c[1] * m["pe"]
     elif c[0] == "d":
-        i = c[1] * (1.0 if o["e"] == "g" else 0.1)
+        i = x + c[1] * (1.0 if o["e"] == "g" else 0.1)
         x = 8 * c[1] * m["row"] + c[2] / 610000.0
         return i, i + 1.7 + x, x
     elif c[0] == "r":
-        return 0.6, 0.6 + m["rem"] * 0.5 + c[1] / 150000.0, 8 * m["row"] + c[1] / 400000.0
+        return x + 0.6, x + 0.6 + m["rem"] * 0.5 + c[1] / 150000.0, 8 * m["row"] + c[1] / 400000.0
     else:
         return 0.0, m["rem"] * 0.5, 0.0
     return x, x, 0.0
@@ -674,15 +748,67 @@ def land(s, d, busy):
     return x + 0.7
 
 
+def facts(ops, tiles):
+    n, deps, ms_ = len(ops), depend(ops), models()
+    num = {x: k for k, x in enumerate(tiles)}
+    tl = [sorted({num[r[0]] for r in o["rd"] + o["wr"] if r[0] in num}) for o in ops]
+    opens, uses = [-1] * n, [0] * len(num)
+    for i in range(n):
+        for x in tl[i]:
+            if not uses[x]:
+                opens[i] = x
+            uses[x] += 1
+    succ, ahead = [[] for o in ops], [[] for o in ops]
+    for i in range(n):
+        for j in deps[i]:
+            succ[j].append(i)
+        for j in ops[i]["behind"]:
+            ahead[j].append(i)
+    return {"n": n, "deps": deps, "succ": succ, "behind": [o["behind"] for o in ops], "ahead": ahead, "tl": tl, "opens": opens, "uses": uses,
+            "pool": [int(tiles[x][1] == B) for x in tiles], "eng": [QUEUES.index(o["e"]) for o in ops],
+            "alt": [o["alt"] and [[times(o["alt"], m)] for m in ms_] for o in ops],
+            "dma": [o["k"] in "ds" for o in ops], "dur": [[times(o, m) for o in ops] for m in ms_], "lat": [m["lat"] for m in ms_], "w": [m["w"] for m in ms_]}
+
+
+def follow(pre, order, mark=None, known=None, marks=None):
+    free, left, bank = [list(range(NF)), list(range(NF, NF + NB))], pre["uses"], [0] * len(pre["uses"])
+    last, tl, opens, eng, pool, deps = [[-1] * 6 for b in range(NF + NB)], pre["tl"], pre["opens"], pre["eng"], pre["pool"], pre["deps"]
+    if mark:
+        free, left, bank, last = mark
+    free, left, bank, last, waits = [list(x) for x in free], list(left), list(bank), [list(x) for x in last], list(known or deps)
+    for p, i in enumerate(order):
+        if marks is not None and p % 16 == 0:
+            marks.append(([list(x) for x in free], list(left), list(bank), [list(x) for x in last]))
+        if tl[i]:
+            x, e, t = [], eng[i], opens[i]
+            if t >= 0:
+                if not free[pool[t]]:
+                    return None, None
+                b = bank[t] = free[pool[t]].pop(0)
+                x = [j for j in last[b] if j >= 0]
+                last[b] = [-1] * 6
+            for t in tl[i]:
+                l = last[bank[t]]
+                x += [j for j in l if j >= 0 and eng[j] != e]
+                l[e] = i
+                left[t] -= 1
+                if not left[t]:
+                    free[pool[t]].append(bank[t])
+            waits[i] = deps[i] + x
+    return waits, bank
+
+
 def plan(pre, pr, slack, back=False):
-    eng, bk, dur, lat, n = pre["eng"], pre["bk"], pre["dur"][0], pre["lat"][0], pre["n"]
-    succ, then, left = (pre["deps"], pre["behind"], list(pre["outs"])) if back else (pre["succ"], pre["ahead"], list(pre["ins"]))
+    eng, dur, lat, n, tl, opens, pool = pre["eng"], pre["dur"][0], pre["lat"][0], pre["n"], pre["tl"], pre["opens"], pre["pool"]
+    succ, then = (pre["deps"], pre["behind"]) if back else (pre["succ"], pre["ahead"])
+    left = [len(pre["succ"][i]) + len(pre["ahead"][i]) if back else len(pre["deps"][i]) + len(pre["behind"][i]) for i in range(n)]
     ready = [[i for i in range(n) if not left[i] and eng[i] == e] for e in range(6)]
     rdy, fin, est, free = [0.0] * n, [0.0] * n, [0.0] * n, [0.0] * 6
-    last = [[-1] * 6 for b in range(8)]
-    order, extra, busy = [], [[]] * n, [0.0]
+    banks, uses, bank = [list(range(NF)), list(range(NF, NF + NB))], list(pre["uses"]), [0] * len(pre["uses"])
+    last = [[0.0] * 6 for b in range(NF + NB)]
+    order, busy = [], [0.0]
     for step in range(n):
-        b0, e0 = 1e9, 0
+        b0, e0 = 1e9, -1
         for e in range(6):
             f = free[e]
             for i in ready[e]:
@@ -690,27 +816,41 @@ def plan(pre, pr, slack, back=False):
                 x = f - dur[i][1] + dur[i][0] if back else f
                 if x > s:
                     s = x
-                for b in bk[i]:
-                    for j in last[b]:
-                        if j >= 0 and eng[j] != e and fin[j] + lat > s:
-                            s = fin[j] + lat
+                if tl[i] and not back:
+                    t = opens[i]
+                    if t >= 0:
+                        if not banks[pool[t]]:
+                            est[i] = 2e9
+                            continue
+                        s = max(s, max(last[banks[pool[t]][0]]))
+                    for y in tl[i]:
+                        if y != t:
+                            for k, x in enumerate(last[bank[y]]):
+                                if x > s and k != e:
+                                    s = x
                 est[i] = s
                 if s < b0:
                     b0, e0 = s, e
+        if e0 < 0:
+            return None, None
         i, p = -1, -1e9
         for j in ready[e0]:
             if est[j] <= b0 + slack[j] and pr[j] > p:
                 i, p = j, pr[j]
-        if bk[i]:
-            extra[i] = [j for b in bk[i] for j in last[b] if j >= 0 and eng[j] != e0]
-            for b in bk[i]:
-                last[b][e0] = i
         if e0:
             free[e0] = est[i] + dur[i][1 if back else 0]
         fin[i] = land(est[i], dur[i], busy) if dur[i][2] and not back else est[i] + dur[i][1]
         order.append(i)
         ready[e0].remove(i)
         x = fin[i] + lat
+        if tl[i] and not back:
+            if opens[i] >= 0:
+                bank[opens[i]] = banks[pool[opens[i]]].pop(0)
+            for y in tl[i]:
+                last[bank[y]][e0] = x
+                uses[y] -= 1
+                if not uses[y]:
+                    banks[pool[y]].append(bank[y])
         for j in succ[i]:
             if x > rdy[j]:
                 rdy[j] = x
@@ -718,197 +858,306 @@ def plan(pre, pr, slack, back=False):
             left[j] -= 1
             if not left[j]:
                 ready[eng[j]].append(j)
-    return order, extra, fin
+    return order, fin
 
 
-def replay(pre, extra, order, k):
-    eng, dur, lat, deps = pre["eng"], pre["dur"][k], pre["lat"][k], pre["deps"]
-    free, fin, busy = [0.0] * 6, [0.0] * pre["n"], [0.0]
-    for i in order:
+def replay(pre, waits, order, k, old=None, a=0):
+    eng, dur, lat = pre["eng"], pre["dur"][k], pre["lat"][k]
+    free, busy = [0.0] * 6, 0.0
+    st, fin = (list(old[0]), list(old[1])) if old else ([0.0] * pre["n"], [0.0] * pre["n"])
+    need = {1, 2, 3, 4, 5, 6}
+    for p in range(a - 1, -1, -1):
+        i = order[p]
+        if eng[i] in need:
+            need.discard(eng[i])
+            free[eng[i]] = st[i] + dur[i][0]
+        if dur[i][2] and 6 in need:
+            need.discard(6)
+            busy = fin[i] - 0.7 - lat
+        if not need:
+            break
+    for i in order[a:]:
         e = eng[i]
-        s = free[e] - lat
-        for j in deps[i] + extra[i]:
+        s = free[e]
+        for j in waits[i]:
             if fin[j] > s:
                 s = fin[j]
-        s += lat
+        st[i] = s
+        q, c, d = dur[i]
         if e:
-            free[e] = s + dur[i][0]
-        fin[i] = land(s, dur[i], busy) if dur[i][2] else s + dur[i][1]
-    return max(fin)
+            free[e] = s + q
+        if d:
+            x = s + c - 0.7 - d
+            busy = (x if x > busy else busy) + d
+            fin[i] = busy + 0.7 + lat
+        else:
+            fin[i] = s + c + lat
+    return st, fin
 
 
-def held(pre, extra, order, k):
-    eng, dur, lat, deps = pre["eng"], pre["dur"][k], pre["lat"][k], pre["deps"]
-    free, fin, last, par, busy = [0.0] * 6, [0.0] * pre["n"], [-1] * 6, [None] * pre["n"], [0.0]
-    for i in order:
-        e = eng[i]
-        s, par[i] = free[e] - lat, (last[e], True)
-        for j in deps[i] + extra[i]:
-            if fin[j] > s:
-                s, par[i] = fin[j], (j, j not in deps[i])
-        s += lat
-        if e:
-            free[e], last[e] = s + dur[i][0], i
-        fin[i] = land(s, dur[i], busy) if dur[i][2] else s + dur[i][1]
+def held(pre, waits, before, times_):
+    st, fin = times_
     i, out = fin.index(max(fin)), []
-    while i >= 0:
-        if par[i][1] and par[i][0] >= 0:
-            out.append((par[i][0], i))
-        i = par[i][0]
+    while st[i] > 0:
+        j = [j for j in waits[i] if fin[j] == st[i]]
+        j = j[0] if j else before[i]
+        if j not in pre["deps"][i]:
+            out.append((j, i))
+        i = j
     return out
 
 
-def follow(pre, order):
-    last, extra, bk, eng = [{} for b in range(8)], [[]] * pre["n"], pre["bk"], pre["eng"]
-    for i in order:
-        if bk[i]:
-            extra[i] = [j for b in bk[i] for e, j in last[b].items() if e != eng[i]]
-            for b in bk[i]:
-                last[b][eng[i]] = i
-    return extra
-
-
-def kind(o):
+def kind(o, tiles):
     r = (o["wr"] or o["rd"])[0]
-    if o["k"] == "s":
-        return (o["e"], o["cost"])
-    if o["k"] == "d" or r[2] == r[1] + 1:
-        return (o["e"], r)
-    if o["e"] == "p" and o["rd"][0][0] in ("mvb", "mvf", "ident"):
-        return (o["e"], o["cost"], o["rd"][0][1], o["rd"][1][0][0], o["rd"][1][1], max(r[1], 1024))
-    if r[0] == "ps" and r[1] < 1024:
-        r = o["rd"][0] if o["e"] == "s" else o["rd"][1]
-    return (o["e"], o["cost"], r[0].rstrip("0123") if r[0][0] in "zudl" else r[0], r[1] % 960 if r[0] == "lu" else r[1] - r[1] % 32 if o["k"] == "a" else r[1])
+    q = (o["rd"] or o["wr"])[-1 if o["e"] == "p" else 0]
+    return (o["e"], o["cost"]) + tuple((tiles[x[0]][0] if x[0] in tiles else x[0].rstrip("0123") if x[0][0] in "zudl" else x[0],
+                                        x[1] % 960 if x[0] == "lu" else x[1]) for x in (r, q))
 
 
-def names_of(ops):
-    seen = {}
-    out = []
-    for o in ops:
-        k = kind(o)
-        seen[k] = seen.get(k, 0) + 1
-        out.append((k, seen[k]))
-    return out
-
-
-def arrange(ops, like=None):
-    full = depend(ops)
-    ms_ = models()
-    n = len(ops)
-    deps, above = [], []
-    for d in full:
-        far = 0
-        for j in d:
-            far |= above[j]
-        deps.append([j for j in d if not far >> j & 1])
-        above.append(far | sum(1 << j for j in d))
-    behind = [o.get("behind", []) for o in ops]
-    succ, ahead = [[] for o in ops], [[] for o in ops]
-    for i in range(n):
-        for j in deps[i]:
-            succ[j].append(i)
-        for j in behind[i]:
-            ahead[j].append(i)
-    pre = {"n": n, "deps": deps, "succ": succ, "behind": behind, "ahead": ahead,
-           "ins": [len(deps[i] + behind[i]) for i in range(n)], "outs": [len(succ[i] + ahead[i]) for i in range(n)],
-           "eng": [[None, "v", "s", "p", "g", "y"].index(o["e"]) for o in ops],
-           "bk": [[k + 6 * (a == "pt") for a, k in sorted(banks(o))] for o in ops],
-           "dur": [[times(o, m) for o in ops] for m in ms_], "lat": [m["lat"] for m in ms_]}
+def arrange(ops, tiles):
+    pre = facts(ops, tiles)
+    n, deps, nm = pre["n"], pre["deps"], len(pre["w"])
     names = {}
-    kinds = np.array([names.setdefault(kind(o), len(names)) for o in ops])
-    rng = np.random.default_rng(7)
+    kinds = np.array([names.setdefault(kind(o, tiles), len(names)) for o in ops])
+    rng = np.random.default_rng(SEED)
     level = [0.0] * n
     for i in range(n - 1, -1, -1):
         level[i] += pre["dur"][0][i][1] + pre["lat"][0]
-        for j in deps[i]:
+        for j in deps[i] + pre["behind"][i]:
             level[j] = max(level[j], level[i])
-    best = fin = None
-    if like:
-        rank = [0.0] * n
-        for i, x in reversed(list(enumerate(names_of(ops)))):
-            rank[i] = max([rank[j] + 0.01 for j in succ[i] + ahead[i]] + [like.get(x, -1e6)])
-        order = sorted(range(n), key=lambda i: -rank[i])
-        extra = follow(pre, order)
-        return deps, [0, order, extra, [replay(pre, extra, order, j) for j in range(len(ms_))]]
+
+    def score(order, cur=None, more=0.0, a=0):
+        marks = cur[6][:a // 16] if a else []
+        waits = follow(pre, order[a - a % 16:], cur[6][a // 16], cur[2], marks)[0] if a else follow(pre, order, None, None, marks)[0]
+        if waits is None:
+            return None
+        ts_, x, all_ = [], 0.0, []
+        for k in range(nm):
+            all_.append(replay(pre, waits, order, k, cur[5][k] if a else None, a))
+            ts_.append(max(all_[k][1]))
+            x += ts_[k] / pre["w"][k]
+            if cur:
+                more -= (ts_[k] - cur[3][k] + SOON * (sum(all_[k][1]) - sum(cur[5][k][1]))) / pre["w"][k]
+                if more + HOPE * (nm - 1 - k) < 0:
+                    return None
+        return [x, order, waits, ts_, None, all_, marks]
+
+    def links(cur):
+        if cur[4] is None:
+            cur[4] = ahead_of(pre, cur)[6]
+        return cur[4][int(rng.integers(len(cur[4])))]
+    best, fin, keep = None, None, None
     for k in range(TRIES):
-        if k < FB:
+        if k < 32 or best is None:
             slack = np.full(n, [0.1, 0.2, 0.35, 0.5][(k // 8) % 4])
-            rank = np.array(level if k % 8 == 0 else plan(pre, fin, slack.tolist(), True)[2])
+            rank = np.array(level if k % 8 == 0 or fin is None else plan(pre, fin, slack.tolist(), True)[1])
         else:
-            rank, slack = best[4].copy(), best[5].copy()
+            rank, slack = keep[0].copy(), keep[1].copy()
             if k % 2:
-                if best[6] is None:
-                    best[6] = [held(pre, best[2], best[1], j) for j in range(len(ms_))]
-                links = best[6][int(rng.integers(len(ms_)))]
-                j, i = links[int(rng.integers(len(links)))]
+                j, i = links(best)
                 gap = max(rank[j] - rank[i], 0.0) + float(rng.choice([0.05, 0.3, 1.0]))
                 up = rng.random() < 0.5
                 who = i if up else j
                 pick = (kinds == kinds[who]) if rng.random() < 0.6 else (np.arange(n) == who)
-                shift = np.full(n, gap if up else -gap)
-                sl = slack.copy()
-                for x in np.nonzero((kinds == kinds[i]) if pick.sum() > 1 else (np.arange(n) == i))[0]:
-                    slack[x] = max(slack[x], float(rng.choice([0.2, 0.5, 1.0])))
-                sl = slack
+                rank[pick] += gap if up else -gap
+                pick = (kinds == kinds[i]) if pick.sum() > 1 else (np.arange(n) == i)
+                slack[pick] = np.maximum(slack[pick], float(rng.choice([0.2, 0.5, 1.0])))
             elif k % 3:
                 pick = np.isin(kinds, rng.choice(kinds[n // 3:], int(rng.choice([1, 2, 4]))))
-                shift = rng.normal(0.0, float(rng.choice([0.5, 1.5, 4.0])), len(names))[kinds]
-                sl = rng.choice([0.05, 0.2, 0.5, 1.0], len(names))[kinds]
+                rank[pick] += rng.normal(0.0, float(rng.choice([0.5, 1.5, 4.0])), len(names))[kinds][pick]
+                slack[pick] = rng.choice([0.05, 0.2, 0.5, 1.0], len(names))[kinds][pick]
             else:
                 pick = (rng.random(n) < 0.3) & (np.abs(np.arange(n) - int(rng.integers(0, n))) < int(rng.choice([5, 20, 60])))
-                shift = rng.normal(0.0, float(rng.choice([0.3, 1.0, 3.0])), n)
-                sl = rng.choice([0.05, 0.2, 0.5, 1.0], n)
-            rank[pick] += shift[pick]
-            slack[pick] = sl[pick]
-        order, extra, fin = plan(pre, rank.tolist(), slack.tolist())
-        ts_ = [max(fin)]
-        if best and ts_[0] > best[3][0] + 2.5:
-            continue
-        ts_ += [replay(pre, extra, order, j) for j in range(1, len(ms_))]
-        score = sum(t / m["w"] for t, m in zip(ts_, ms_))
-        if best is None or score <= best[0]:
-            best = [score, order, extra, ts_, rank, slack, None]
+                rank[pick] += rng.normal(0.0, float(rng.choice([0.3, 1.0, 3.0])), n)[pick]
+                slack[pick] = rng.choice([0.05, 0.2, 0.5, 1.0], n)[pick]
+        order, fin = plan(pre, rank.tolist(), slack.tolist())
+        new = order and score(order, best)
+        if new:
+            best, keep = new, (rank, slack)
     anc = []
     for i in range(n):
         a = 0
-        for j in deps[i] + behind[i]:
+        for j in deps[i] + pre["behind"][i]:
             a |= anc[j] | 1 << j
         anc.append(a)
-    cur = best[:6] + [None]
+    cur, eng, w = best, pre["eng"], pre["w"]
+    aid, taken, kept = ahead_of(pre, cur), 0, list(eng)
+    draw, heat = rng.random((SWAPS, 4)).tolist(), rng.exponential(size=SWAPS).tolist()
     for k in range(SWAPS):
-        if cur[6] is None:
-            cur[6] = [x for j in range(len(ms_)) for x in held(pre, cur[2], cur[1], j)]
-        j, i = cur[6][int(rng.integers(len(cur[6])))]
-        if anc[i] >> j & 1:
-            continue
-        order = cur[1]
-        a, b = order.index(j), order.index(i) + 1
-        if k % 2:
-            go = [x for x in order[a:b] if x == i or anc[i] >> x & 1]
-            order = order[:a] + go + [x for x in order[a:b] if x not in go] + order[b:]
+        if k % 1000 == 0:
+            key = list(cur[5][0][0])
+            for i in cur[1]:
+                key[i] = max([key[i]] + [key[j] for j in pre["behind"][i]])
+            new = score(sorted(cur[1], key=lambda i: key[i]), cur, 0.3)
+            if new:
+                cur, aid = new, ahead_of(pre, new)
+        order, (pos, before, after, marks, succ, tails, pairs), (r0, r1, r2, r3) = cur[1], aid, draw[k]
+        j, i = pairs[int(r0 * len(pairs))]
+        if r1 < NEAR:
+            i = j = order[min(n - 1, max(0, pos[i] + int((r0 * 977 % 1 - 0.5) * 60)))]
+            j = before[i]
+        other = [x for x in (i, j) if x >= 0 and pre["alt"][x]] if r1 * 991 % 1 < FLIP else []
+        if other:
+            other = other[int(r3 * len(other))]
+            flip(pre, other)
+            a = pos[other]
+            b = a + 1
+            part = [other]
         else:
-            go = [x for x in order[a:b] if x == j or anc[x] >> j & 1]
-            order = order[:a] + [x for x in order[a:b] if x not in go] + go + order[b:]
-        extra = follow(pre, order)
-        ts_ = [replay(pre, extra, order, x) for x in range(len(ms_))]
-        score = sum(t / m["w"] for t, m in zip(ts_, ms_))
-        if score <= cur[0] + HEAT * (1.0 - k / SWAPS) * rng.exponential():
-            cur = [score, order, extra, ts_, None, None, None]
-            if score < best[0]:
-                best = cur
-    return deps, best
+            other = -1
+            while r2 < FAR and j >= 0:
+                j, r2 = before[j], r2 / FAR
+            if j < 0 or anc[i] >> j & 1 or pos[j] > pos[i]:
+                continue
+            a, b = pos[j], pos[i] + 1
+            m = anc[i] | 1 << i
+            if r3 < 0.5:
+                part = [x for x in order[a:b] if m >> x & 1] + [x for x in order[a:b] if not m >> x & 1]
+            else:
+                part = [x for x in order[a:b] if x != j and not anc[x] >> j & 1] + [x for x in order[a:b] if x == j or anc[x] >> j & 1]
+        c = min(n, b + REACH)
+        part += order[b:c]
+        a0 = a - a % 16
+        waits = follow(pre, order[a0:a] + part, marks[a0 // 16], cur[2])[0]
+        new = None
+        if waits:
+            more = left = HEAT * (1.0 - k / SWAPS) * heat[k]
+            last, need = [-1] * 6, {eng[x] for x in part} - {0}
+            p = a - 1
+            while need and p >= 0:
+                if eng[order[p]] in need:
+                    need.discard(eng[order[p]])
+                    last[eng[order[p]]] = order[p]
+                p -= 1
+            for y in range(nm):
+                left -= guess(pre, y, cur, aid, waits, part, a, c, last) / w[y]
+                if left + HOPE * (nm - 1 - y) < 0:
+                    break
+            else:
+                new = score(order[:a] + part + order[c:], cur, more, a)
+        if new:
+            taken += 1
+            cur, aid = new, ahead_of(pre, new, aid if taken % LAZY and other < 0 else None)
+            if new[0] < best[0]:
+                best, kept = new, list(eng)
+        elif other >= 0:
+            flip(pre, other)
+    for i in range(n):
+        if eng[i] != kept[i]:
+            flip(pre, i)
+    return pre, best
+
+
+def flip(pre, i):
+    pre["eng"][i] = 3 - pre["eng"][i]
+    for dur, alt in zip(pre["dur"], pre["alt"][i]):
+        dur[i], alt[0] = alt[0], dur[i]
+
+
+def ahead_of(pre, cur, old=None):
+    order, waits, n, eng, marks = cur[1], cur[2], pre["n"], pre["eng"], cur[6]
+    pos, before, last, succ = [0] * n, [-1] * n, [-1] * 6, [[] for i in range(n)]
+    for p, i in enumerate(order):
+        e = eng[i]
+        pos[i], before[i], last[e] = p, last[e], i
+    tails, dmas = [], [i for i in order if pre["dma"][i]]
+    if old:
+        return (pos, before, dmas, marks) + old[4:]
+    for i in order:
+        for j in waits[i]:
+            succ[j].append(i)
+    for k in range(len(pre["w"])):
+        dur, lat = pre["dur"][k], pre["lat"][k]
+        ts_, tf, nxt, dma = [0.0] * n, [0.0] * n, [0.0] * 6, 0.0
+        for i in reversed(order):
+            q, c, d = dur[i]
+            f = tf[i]
+            if d:
+                if dma > f:
+                    f = tf[i] = dma
+                dma = f + d
+            s, e = f + c + lat, eng[i]
+            if e:
+                if nxt[e] + q > s:
+                    s = nxt[e] + q
+                nxt[e] = s
+            ts_[i] = s
+            for j in waits[i]:
+                if s > tf[j]:
+                    tf[j] = s
+        tails.append((ts_, tf))
+    pairs = [x for k in range(len(pre["w"])) for x in held(pre, waits, before, cur[5][k])]
+    return pos, before, dmas, marks, succ, tails, pairs
+
+
+def guess(pre, k, cur, aid, waits, part, a, c, last):
+    pos, before, dmas, marks, succ, tails, pairs = aid
+    eng, dur, lat, (st, old), (ts_, tf), order = pre["eng"], pre["dur"][k], pre["lat"][k], cur[5][k], tails[k], cur[1]
+    free, fin, busy, end, shift = [0.0] * 6, {}, -1.0, 0.0, 0.0
+    for e in range(1, 6):
+        if last[e] >= 0:
+            free[e] = st[last[e]] + dur[last[e]][0]
+    for i in part:
+        e = eng[i]
+        s = free[e]
+        for j in waits[i]:
+            x = fin[j] if j in fin else old[j]
+            if x > s:
+                s = x
+        q, t, d = dur[i]
+        if e:
+            free[e] = s + q
+        if d:
+            if busy < 0:
+                busy = max([old[j] - 0.7 - lat for j in dmas if pos[j] < a][-1:] + [0.0])
+            x = s + t - 0.7 - d
+            busy = (x if x > busy else busy) + d
+            x = busy + 0.7 + lat
+        else:
+            x = s + t + lat
+        fin[i] = x
+        shift += x - old[i]
+        if x > end:
+            end = x
+        for j in succ[i]:
+            if pos[j] >= c and x + ts_[j] > end:
+                end = x + ts_[j]
+    need = {eng[i] for i in part} - {0}
+    for j in order[c:c + 60]:
+        if eng[j] in need:
+            need.discard(eng[j])
+            end = max(end, free[eng[j]] + ts_[j])
+        if busy >= 0 and dur[j][2]:
+            end, busy = max(end, busy + dur[j][2] + 0.7 + lat + tf[j]), -1.0
+    return max(end - cur[3][k], -0.3) + EASE * shift
+
+
+def ordered(core, T, topo):
+    if not PLANS:
+        ops, tiles, place = build(core, T, topo, True)
+        pre, best = arrange(ops, tiles)
+        PLANS["order"], PLANS["only"], PLANS["eng"] = best[1], [o["only"] for o in ops], [QUEUES[e] for e in pre["eng"]]
+    rank = T.rank_of(core)
+    mine = [None] + ["l"] * (rank == 0) + ["r"] * (rank == len(T.cores) - 1)
+    num = {}
+    for i, x in enumerate(PLANS["only"]):
+        if x in mine:
+            num[i] = len(num)
+    order = [num[i] for i in PLANS["order"] if i in num]
+    ops, tiles, place = build(core, T, topo)
+    for i, k in num.items():
+        if ops[k]["e"] != PLANS["eng"][i]:
+            ops[k].update((x, ops[k]["alt"][x]) for x in ("e", "fn", "cost", "first"))
+    waits, bank = follow(facts(ops, tiles), order)
+    for x, b in zip(tiles, bank):
+        place[x] = ("ps", 512 * b) if b < NF else ("pt", 1024 * (b - NF))
+    return ops, order, waits
 
 
 def rank_program(g, core, T, topo):
     if T.rank_of(core) is None:
         return
-    if not PLANS:
-        first = build(core, T, topo, True)
-        names = names_of(first)
-        PLANS.update((names[i], -float(k)) for k, i in enumerate(arrange(first)[1][1]))
-    ops = build(core, T, topo)
-    deps, best = arrange(ops, PLANS)
-    order, extra = best[1], best[2]
+    ops, order, waits = ordered(core, T, topo)
     Q = {"v": g.vector, "s": g.scalar, "p": g.tensor, "g": g, "y": g.sync}
     known = {e: {} for e in Q}
     total = {}
@@ -924,7 +1173,7 @@ def rank_program(g, core, T, topo):
             continue
         kn = known[e]
         need = {}
-        for j in sorted(set(deps[i] + extra[i]), key=lambda j: -len(clock[j])):
+        for j in sorted(set(waits[i]), key=lambda j: -len(clock[j])):
             s, v = tok[j]
             if kn.get(s, 0) < v:
                 need[s] = max(need.get(s, 0), v)
@@ -933,9 +1182,13 @@ def rank_program(g, core, T, topo):
                         kn[s2] = v2
         for s, v in need.items():
             Q[e].wait_ge(T.sem[s], v)
+        s = "e" + e
+        if o["first"]:
+            o["first"](Q[e])[0].then_inc(T.sem[s], 1)
+            total[s] = kn[s] = total.get(s, 0) + 1
+            Q[e].wait_ge(T.sem[s], total[s])
         ins = o["fn"](Q[e])
         if o["k"] == "c":
-            s = "e" + e
             for x in ins:
                 x.then_inc(T.sem[s], 1)
             total[s] = total.get(s, 0) + len(ins)

import math
import numpy as np
from concourse.bass import DstId, RemoteDMATransfer
from concourse.mybir import AluOpType, AxisListType, ActivationFunctionType

AL = AluOpType
AF = ActivationFunctionType
V, H, W, RO = 1536, 256, 2048, 4
ZO, Z8, ZW = 16, 2080, 3872
F, B, G, I, U = "float32", "bfloat16", "float16", "int32", "uint16"
NF, NB = 6, 2
SCRATCH = {
    "xb": ("sbuf", [128, V], B), "xr": ("sbuf", [128, 2 * H], B),
    "lw": ("sbuf", [128, 192], I), "gl": ("sbuf", [128, 100], I),
    "wp": ("sbuf", [128, 400], B), "wb": ("sbuf", [128, V], B),
    "ones": ("sbuf", [128, 256], B), "mv0": ("sbuf", [128, 256], B), "mvf": ("sbuf", [128, 384], F),
    "mv1": ("sbuf", [128, 256], F), "mv2": ("sbuf", [128, 256], F), "mv3": ("sbuf", [128, 256], F),
    "ident": ("sbuf", [128, 128], B), "gsel": ("sbuf", [128, 16], B), "btmp": ("sbuf", [128, 144], B),
    "bk": ("sbuf", [128, 128], B), "hk": ("sbuf", [128, 384], G), "hg": ("sbuf", [128, V], G), "hc": ("sbuf", [128, V], G),
    "sh": ("sbuf", [128, 128], B), "wk": ("sbuf", [128, 256], B),
    "bm": ("sbuf", [128, 2 * V], B), "cs": ("sbuf", [128, 912], B),
    "ki": ("sbuf", [128, 8], I), "col": ("sbuf", [128, 12], F),
    "v2": ("sbuf", [128, 96], F), "vw": ("sbuf", [128, 192], F), "sm": ("sbuf", [128, 288], F),
    "pb": ("sbuf", [128, V], B), "tt": ("sbuf", [128, W + 16], B), "gu": ("sbuf", [128, 8], U),
    "g1": ("sbuf", [128, V], B), "g2": ("sbuf", [128, V], B),
    "a1": ("sbuf", [128, 1792], B), "a2": ("sbuf", [128, 1792], B), "a4": ("sbuf", [128, 1792], B), "a8": ("sbuf", [128, V], B),
    "nl": ("sbuf", [128, V], B), "nr": ("sbuf", [128, V], B),
    "lu": ("sbuf", [128, 5 * 960], U),
    "dl": ("sbuf", [128, 2 * V], F), "ds": ("sbuf", [128, V], F), "ww": ("sbuf", [128, V], F),
    "zc": ("sbuf", [128, V], F), "xs": ("sbuf", [128, 2 * H], F), "mf": ("sbuf", [128, V], F),
    "u0": ("sbuf", [128, 1792], F), "u1": ("sbuf", [128, 1792], F),
    "lx": ("sbuf", [128, 144], B), "vn": ("sbuf", [128, 96], B),
    "pt": ("psum", [128, 1024 * NB], B), "ps": ("psum", [128, 512 * NF], F),
}
for _k in range(4):
    SCRATCH["z%d" % _k] = ("sbuf", [128, ZW], F if _k else B)
    SCRATCH["ll%d" % _k] = ("sbuf", [128, 272], B)
    SCRATCH["lr%d" % _k] = ("sbuf", [128, 272], B)
for _k in range(2):
    SCRATCH["dr%d" % _k] = ("sbuf", [128, 2 * V], F)
    SCRATCH["m" + "ab"[_k]] = ("sbuf", [128, 1792], F)
    SCRATCH["mc%d" % _k] = ("sbuf", [128, V], F)
SEMAPHORES = ["ev", "es", "ep", "eg"] + ["d%d" % k for k in range(110)] + ["%s%d" % (a, k) for a in ("a", "sn") for k in range(18)]

EL, ER, ED, EA, SR, SC, SP, SN, SD, EN, QQ, SV = 0, 144, 288, 432, 576, 608, 640, 672, 704, 720, 864, 592
LL, LR, LD, LCL, LCR, LA1, LA2, LA4, LA8, LS = [96 * k for k in range(10)]
TRIES, SWAPS, HEAT, HOPE, SEED = 300, 100000, 0.3, 0.3, 4
NEAR, FAR, REACH, EASE, SOON, LAZY, FLIP = 0.3, 0.4, 25, 0.003, 0.001, 4, 0.08
QUEUES = [None, "v", "s", "p", "g", "y"]
MODELS = ((1.7, 1.15, 0.55, 0.07, 2.8, 0.03, 1.15), (2.0, 1.4, 0.6, 0.1, 3.2, 0.04, 1.3), (1.25, 1.05, 0.45, 0.06, 2.5, 0.02, 0.95),
          (1.4, 1.15, 0.85, 0.13, 4.4, 0.05, 1.3))
PLANS = {}


def cut(ways, *ends):
    ends = ends or (512, 1024, V)
    return [(a, b, x) for a, b, x in zip((0,) + ends, ends, ways)]


P = {
    "curR": cut("ssv"), "canR": cut("vsv"), "curL": cut("vvp"), "canL": cut("vsv"),
    "curR.0": cut("ppp"), "canR.0": cut("vpv"),
    "prod": 1, "prodL": "sss", "prodL.1": "vvv", "r0": 1,
    "dec": [("R", 8, 12), ("RL", 0, 4), ("RL", 4, 8), ("L", 8, 12)],
    "ww.0": [(0, 512, "p"), (1024, V, "q"), (512, 1024, "p")],
    "ww.3": cut("vvv"),
    "ww": [(0, 512, "v"), (1280, V, "v"), (512, 1024, "v"), (1024, 1280, "v")],
    "pm": 1, "zd": 0, "zg": 1,
    "hv": cut("vv", 512, V), "go": cut("vv", 512, V), "xs": "s", "far": 1, "tw": "yyy", "tw.3": "ggg", "tz": "gyyy",
    "g1": cut("ssss", 256, 512, 1024, V), "a2": cut("sss"), "a4": cut("sss"), "a8": cut("sss"), "z8": cut("sss"),
    "g1.0": cut("sssv", 256, 512, 1024, V), "a2.0": cut("ssv"), "a4.0": cut("ssv"), "a8.0": cut("ssv"), "z8.0": cut("ssv"),
    "g2": cut("sss", 512, 1280, V),
    "mc": cut("vvv"), "ds": cut("sss"), "u": cut("ss", 768, V), "yy": cut("vvv"),
    "y3": 0, "t": "svvs", "cur": "s", "pe0": 1,
}


def of(key, t):
    return P.get("%s.%d" % (key, t), P[key])


def models():
    out = []
    for ga, f, pe, lat, rem, row, w in MODELS:
        out.append({"g": ga, "c": 0.00083 * f, "pe": 0.001 * pe, "lat": lat, "rem": rem, "row": row, "w": w})
    return out


def build(core, T, topo, both=False):
    rank, n = T.rank_of(core), len(T.cores)
    left, right = T.cores[(rank - 1) % n], T.cores[(rank + 1) % n]
    rotr, rotl = both or rank == n - 1, both or rank == 0
    ops, tiles, place = [], {}, {}
    nd, nx, sent, only = [0], [0], [], [None]

    def R(name, a=0, b=None, s=1):
        if b is None:
            b = SCRATCH[name][1][1] if name in SCRATCH else V
        return (name, a + 16, b + 16, s) if name == "tt" else (name, a, b, s)

    def tile(label, dt=F):
        name = "@%d" % len(tiles)
        tiles[name] = (label, dt)
        return name

    def A(r):
        name, c = place[r[0]] if r[0] in tiles else (r[0], 0)
        return T[name][:, c + r[1]:c + r[2]:r[3]] if r[3] != 1 else T[name][:, c + r[1]:c + r[2]]

    def dty(r):
        return tiles[r[0]][1] if r[0] in tiles else SCRATCH[r[0]][2]

    def cnt(r):
        return len(range(r[1], r[2], r[3]))

    def X(x):
        return A(x) if isinstance(x, tuple) else x

    def op(eng, cost, fn, rd, wr, kind="c", sem=None, val=0, after=()):
        ops.append({"e": eng, "cost": cost, "fn": fn, "rd": [r for r in rd if isinstance(r, tuple)], "wr": list(wr), "k": kind,
                    "sem": sem, "val": val, "after": list(after), "behind": [], "only": only[0], "once": 0.0, "alt": None, "first": None})
        return len(ops) - 1

    def either(eng, on_v, on_s):
        (on_s if eng == "v" else on_v)()
        alt = ops.pop()
        o = (on_v if eng == "v" else on_s)()
        ops[o]["alt"] = alt
        return o

    def two(*rs):
        return all(dty(r) in (B, G, U) for r in rs)

    def ts(out, a, s1, s2, o0, o1=None):
        def fn(q):
            if o1 is None:
                return [q.tensor_scalar(A(out), A(a), X(s1), None, o0)]
            return [q.tensor_scalar(A(out), A(a), X(s1), X(s2), o0, o1)]
        return op("v", ("e", cnt(a) * (0.5 if two(out, a) else 1)), fn, [a, s1, s2], [out])

    def tt(out, a, b, o):
        sb = a[0] not in tiles and b[0] not in tiles
        return op("v", ("e", cnt(a) * (2 if sb else 1)), lambda q: [q.tensor_tensor(A(out), A(a), A(b), o)], [a, b], [out])

    def cp(eng, out, a, bias=None, scale=None):
        def on_v():
            if bias is not None or scale is not None:
                return ts(out, a, scale if bias is None else bias, None, AL.mult if bias is None else AL.add)
            return op("v", ("e", cnt(a) * (0.5 if two(out, a) else 1)), lambda q: [q.tensor_copy(A(out), A(a))], [a], [out])
        if {dty(out), dty(a)} - {F, B}:
            return on_v()
        return either(eng, on_v, lambda: act(out, a, AF.Copy if bias is None else AF.Identity, bias=bias, scale=scale))

    def act(out, a, f, bias=None, scale=None, off=None):
        def fn(q):
            kw = {}
            if bias is not None:
                kw["bias"] = X(bias)
            if scale is not None:
                kw["scale"] = X(scale)
            return [q.activation(A(out), A(a).indirect(A(off)) if off else A(a), f, **kw)]
        return op("s", ("g" if off else "e", cnt(out)), fn, [a, bias, scale, off], [out])

    def gtt(out, win, off, b, o):
        return op("v", ("g", cnt(out)), lambda q: [q.tensor_tensor(A(out), A(win).indirect(A(off)), A(b), o)], [win, off, b], [out])

    def gcp(out, win, off, eng, scale=None):
        def on_v():
            if scale:
                return op("v", ("g", cnt(out)), lambda q: [q.tensor_scalar(A(out), A(win).indirect(A(off)), scale, None, AL.mult)], [win, off], [out])
            return op("v", ("g", cnt(out)), lambda q: [q.tensor_copy(A(out), A(win).indirect(A(off)))], [win, off], [out])
        if dty(out) == G:
            return on_v()
        return either(eng, on_v, lambda: act(out, win, AF.Copy, scale=scale, off=off))

    def ms(out, c):
        return op("v", ("e", cnt(out) * (0.5 if two(out) else 1)), lambda q: [q.memset(A(out), c)], [], [out])

    def red(out, a):
        return op("v", ("e", cnt(a)), lambda q: [q.tensor_reduce(A(out), A(a), AxisListType.X, AL.add)], [a], [out])

    def iota(out, pat, base, cm):
        kw = {} if dty(out) == I else {"allow_small_or_imprecise_dtypes": True}
        return op("g", ("q", cnt(out)), lambda q: [q.iota(A(out), pat, base, cm, **kw)], [], [out])

    def sel(out, a, pat, cmpop, base, cm):
        return op("g", ("q", cnt(out)), lambda q: [q.affine_select(A(out), A(a), pat, cmpop, 0.0, base, cm)], [a], [out])

    def mm(groups, start=True, stop=True):
        def fn(q):
            last = []
            for out, terms in groups:
                for k, (l, r) in enumerate(terms):
                    ins = q.matmul(A(out), A(l), A(r), start and k == 0, stop and k == len(terms) - 1)
                last.append(ins)
            return last
        c = sum(max(64, cnt(r)) * (4 if dty(r) == F else 1) for out, terms in groups for l, r in terms)
        return op("p", ("p", c), fn, [x for out, terms in groups for t in terms for x in t], [out for out, terms in groups], val=len(groups))

    def sums(p, *terms, ahead=None):
        for k, x in enumerate(terms):
            o = mm([(p, [x])], start=k == 0, stop=k == len(terms) - 1)
            if k == 0 and ahead is not None:
                ops[o]["behind"].append(ahead)

    def tr(pairs):
        return op("p", ("p", 128 * len(pairs)), lambda q: [q.transpose(A(o), A(a), A(R("ident"))) for o, a in pairs],
                  [a for o, a in pairs] + [R("ident")], [o for o, a in pairs], val=len(pairs))

    gd = []

    def dma(eng, pairs, rd, wr, nbytes, add=False):
        s = "d%d" % nd[0]
        nd[0] += 1

        def fn(q):
            if add:
                return [q.dma_start(o, a, accum_op=AL.add) for o, a in pairs]
            return [q.dma_start(o, a) for o, a in pairs]
        o = op(eng, ("d", len(pairs), nbytes * (2 if add else 1)), fn, rd, wr, kind="d", sem=s, val=16 * len(pairs))
        if eng == "g":
            ops[o]["behind"] += gd[:1]
            ops[o]["once"] = 0.0 if gd else 1.0
            gd.append(o)
        return o

    def twin(dst, src, eng="y"):
        if eng == "g":
            return sel(dst, src, [[0, cnt(src)]], AL.is_gt, 1, 0)
        if eng == "s":
            return cp(eng, dst, src)
        return dma("y", [(A(dst), A(src))], [src], [dst], 512 * cnt(src))

    def exchange(sides, nbytes, also=()):
        k = nx[0]
        nx[0] += len(sides)
        eng = [topo.engines(core, x[0]) for x in sides]
        m = len(eng[0]) // len(sides)

        def fn(q):
            trs = []
            for j, (d, src, there, here) in enumerate(sides):
                rid, pid = topo.addr(d, core)
                mask = sum(1 << e for e in eng[j][j * m:(j + 1) * m])
                trs.append(RemoteDMATransfer(dst_ids=[DstId(rid=rid, pnc=pid)], dma_engine_mask=mask, remote_sem=T.sem["a%d" % (k + j)], src=A(src), dst=A(there)))
            q.remote_dma_fused(trs, local_sem=T.sem["sn%d" % k])
            return []
        o = op("g", ("r", nbytes), fn, [x[1] for x in sides] + list(also), [], kind="s", sem="sn%d" % k, val=m * len(sides))
        ops[o]["behind"] += sent[-1:]
        ops[o]["once"] = 0.0 if sent else 1.5
        sent.append(o)
        for j, x in enumerate(sides):
            op(None, ("a",), None, [], [x[3]], kind="a", sem="a%d" % (k + j), val=m, after=[o])

    def terms(e, tab, first, c0=0, c1=96):
        return [(R("cs", e + 16 - i, e + 144 - i), R(tab, first + 16 * c0 + i, first + 16 * c1 + i - 15, 16)) for i in range(16)]

    def ext(label, e, tab, first, a=0, b=V, more=()):
        p = R(tile(label), 0, (b - a) // 16)
        mm([(p, terms(e, tab, first, a // 16, b // 16) + list(more))])
        return p

    def lst(t, c, a=0, b=V):
        return R("lu", 960 * (t + 1) + c + a // 16, 960 * (t + 1) + c + b // 16)

    def blk(tab, s, first=0):
        return R(tab, first + 128 * s, first + 128 * s + 128)

    def wrap(name, a, b, side):
        only[0] = side
        sel(R(name, a, a + 16), R(name, b, b + 16), [[0, 16]], AL.is_gt, 1, 0)
        only[0] = None

    srcl, srcr = R("xr", 0, H), R("xr", H, 2 * H)
    pr = [(T.xr[16:128, H:], T.x0[0:112, V - H:V]), (T.xr[0:16, H:], T.x0[112:128, V - H:V])] if rotr else [(T.xr[:, H:], T.x0[:, V - H:V])]
    loads = [dma("y", pr, [], [srcr], 65536)]
    pr = [(T.xr[0:112, :H], T.x0[16:128, 0:H]), (T.xr[112:128, :H], T.x0[0:16, 0:H])] if rotl else [(T.xr[:, :H], T.x0[:, 0:H])]
    loads.append(dma("s", pr, [], [srcl], 65536))
    loads.append(dma("s", [(T.lw[:, 0:96], T.lf[:]), (T.lw[:, 96:192], T.rt[:])], [], [R("lw")], 98304))
    loads.append(dma("y", [(T.z0[:, ZO + H:ZO + H + V], T.x0[:])], [], [R("z0", ZO + H, ZO + H + V)], 393216))
    loads.append(dma("y", [(T.xb[:], T.x0[:])], [], [R("xb")], 393216))
    for a, b in zip(loads, loads[1:]):
        ops[b]["behind"].append(a)
    gl_, gr_ = R("z0", ZO, ZO + H), R("z0", ZO + H + V, ZO + W)
    exchange([(left, srcl, gr_, gr_), (right, srcr, gl_, gl_)], 131072)
    exchange([(right, R("lw", 92, 192), R("gl"), R("gl"))], 51200)

    ms(R("ones", 0, 144), 1.0)
    warm = act(R("ones", 144, 256), R("ones", 0, 112), AF.Exp, scale=0.0)
    ops[warm]["once"] = 1.3
    sel(R("ident"), R("ones", 0, 128), [[-1, 128]], AL.is_equal, 0, 1)
    sel(R("btmp"), R("ones", 0, 144), [[-1, 16], [-16, 9]], AL.is_equal, 16, 1)
    ms(R("pb"), 0.0)
    if P["zd"]:
        o = dma("y", [(A(R("bm", a, b)), A(R("pb", 0, b - a))) for a, b in ((0, V), (V, 2416))], [R("pb")], [R("bm", 0, 2416)], 256 * 2416)
        ops[o]["behind"].append(loads[P["zd"]])
    else:
        ms(R("bm", 0, 2416), 0.0)
    cp("s", R("bm", 0, 2304, 16), R("btmp"))

    def zero(r):
        return iota(r, [[0, cnt(r)]], 0, 0) if P["zg"] else ms(r, 0.0)
    ms(R("cs"), 0.0)
    sel(R("gsel", 0, 8), R("ones", 0, 8), [[-16, 8]], AL.is_ge, 0, 1)
    sel(R("gsel", 8, 16), R("gsel", 0, 8), [[16, 8]], AL.is_ge, 15, -1)
    cp("s", R("cs", EA + 16, EA + 144, 16), R("gsel", 8, 16))
    for j in (1, 3):
        cp("s", R("cs", QQ + j, QQ + 33, 4), R("gsel", 8, 16))

    def idn(a, s):
        return R("ident", a, 128, s)

    def c_(base, a, s, w=32):
        return R("cs", base + a, base + w, s)
    el, er, ed = [R("cs", e + 16, e + 144, 16) for e in (EL, ER, ED)]
    tt(c_(SC, 0, 1), idn(0, 4), idn(1, 4), AL.add)
    tt(el, c_(SC, 0, 4), c_(SC, 2, 4), AL.add)
    tt(er, c_(SC, 1, 4), c_(SC, 3, 4), AL.add)
    for base, o_ in ((SP, AL.add), (SN, AL.subtract)):
        act(c_(base, 0, 1), c_(SC, 0, 1), AF.Copy, scale=-1.0)
        for j in (2, 3):
            tt(c_(base, j, 4), c_(base, j, 4), idn(11, 16), o_)
    act(R("gsel", 0, 8), idn(6, 16), AF.Copy, scale=1536.0)
    act(R("btmp", 0, 8), idn(11, 16), AF.Copy, scale=-272.0)
    vv = R("btmp", 16, 24)
    tt(vv, idn(3, 16), idn(7, 16), AL.add)
    tt(ed, vv, R("gsel", 0, 8), AL.add)
    tt(R("cs", EN + 16, EN + 144, 16), er, R("btmp", 0, 8), AL.add)
    KK, ONE, HI, BM, BP, KQ, LO, UP = [R("col", k, k + 1) for k in range(8)]
    iota(R("ki", 0, 1), [[0, 1]], 0, 1)
    ts(R("ki", 4, 5), R("ki", 0, 1), 15, None, AL.bitwise_and)
    cp("v", KK, R("ki", 4, 5))
    red(ONE, idn(11, 16))
    tt(R("btmp", 8, 16), idn(0, 16), idn(4, 16), AL.add)
    red(HI, R("btmp", 8, 16))
    act(BM, HI, AF.Copy, scale=-1536.0)
    act(BP, HI, AF.Copy, scale=1536.0)
    act(KQ, KK, AF.Copy, scale=-4096.0)
    iota(R("v2"), [[128, 12], [0, 8]], 256, 1)

    def w_(k, r):
        return R("wk", 128 * k + r, 128 * k + 128, 16)
    zero(R("wk"))
    for r, x in enumerate((4096.0, -4096.0, -256.0, 256.0)):
        act(w_(1, r), er, AF.Copy, scale=x)
        act(w_(0, r), vv, AF.Copy, scale=-x)
    for r, j, k in ((0, 0, 15), (2, 2, 7)):
        tt(w_(0, r), w_(0, r), c_(SC, j, 4), AL.add)
        tt(w_(0, r), w_(0, r), idn(k, 16), AL.subtract)
    cp("s", w_(0, 4), idn(3, 16))
    cp("s", w_(0, 5), idn(7, 16))
    tt(R("btmp", 24, 32), idn(2, 16), idn(3, 16), AL.add)
    red(UP, R("btmp", 24, 32))
    ts(UP, UP, -1920.0, 2048.0, AL.mult, AL.add)
    act(LO, UP, AF.Copy, scale=-1.0)
    iota(R("vw", 96, 192), [[16, 96]], 256, 0)
    act(R("vn"), R("vw", 96, 192), AF.Copy, scale=-1.0)
    ts(R("vw", 0, 96), R("vw", 96, 192), KK, float(ZO - Z8), AL.add, AL.add)
    ms(R("pb", 11, V, 16), 1.0)
    for c in (3, 15):
        ts(R("pb", c, V, 16), R("v2"), KK, None, AL.subtract)
    act(R("pb", 7, V, 16), R("v2"), AF.Identity, bias=KK, scale=0.0)
    iota(R("a2", 0, H), [[1, H]], 0, 0)
    act(R("a1", 0, H), R("a2", 0, H), AF.Copy, scale=ONE)
    dma("y", [(A(R(a, 0, H)), A(R("a1", 0, H))) for a in ("a2", "a4")], [R("a1", 0, H)], [R("a2", 0, H), R("a4", 0, H)], 131072)
    sel(R("mvf", 128, 384), R("ones"), [[0, 2], [-1, 128]], AL.is_equal, 0, 1)
    PM = P["pm"]
    SCALE = [1.0] * PM + [(-8.0) ** (t - RO) for t in range(PM, RO + 1)]
    for t in range(PM):
        for c, x in ((0, 1.125), (128, -0.125)):
            act(R("mv%d" % t, c, c + 128), R("ident"), AF.Copy, scale=x * SCALE[t + 1] / SCALE[t])
    act(R("mvf", 0, 128), R("ident"), AF.Copy, scale=-9.0)
    if P["prod"]:
        act(R("bk"), R("ident"), AF.Copy, scale=-0.5)
    if P["prod"] > 1:
        ts(R("hk", 0, 128), R("ident"), -0.5, None, AL.mult)
        cp("v", R("hk", 128, 256), R("ident"))
    if PM > 1:
        ts(R("hk", 256, 384), R("ident"), -0.125 * SCALE[2], None, AL.mult)
    zero(R("tt", -16, H - 1))
    zero(R("tt", H + V, W))
    for k in range(RO):
        for c in (0, ZO + W):
            if k < P["far"]:
                ms(R("z%d" % k, c, c + 16), 4096.0)
            else:
                iota(R("z%d" % k, c, c + 16), [[0, 16]], 4096, 0)

    cp("v", lst(-1, LL), R("lw", 0, 96), bias=16.0)
    cp("v", lst(-1, LR), R("lw", 96, 192), bias=-float(H))
    big = 1.5 * 2.0 ** 27
    ts(R("wp", 0, 192), R("lw"), big, big, AL.add, AL.subtract)
    tt(R("wp", 192, 384), R("lw"), R("wp", 0, 192), AL.subtract)
    ts(R("wp", 388, 390), R("gl", 3, 100, 96), big, big, AL.add, AL.subtract)
    ts(R("wp", 384, 386), R("gl", 3, 100, 96), big, big + V, AL.add, AL.subtract)
    tt(R("wp", 386, 388), R("gl", 3, 100, 96), R("wp", 388, 390), AL.subtract)
    parts = [(0, 0), (4, 96), (8, 192), (12, 288)]

    def bv(i, kk):
        return R("bm", 144 * i + 16 - kk, 144 * i + 144 - kk)
    turns = (16, -112) if rotl else (0,)
    if P["pe0"]:
        cp("s", R("sh", 1, 128), R("ident", 0, 127))
        ms(R("sh", 0, 128, 16), 0.0)
        p = tile("c0")
        mm([(R(p, 1, 192), [(R("sh"), R("wp", c + 1, c + 192)) for c in (0, 192)] + [(bv(15, 0), R("wp", c, c + 191)) for c in (0, 192)])])
        cp("v", lst(-1, LCL, 16, V), R(p, 1, 96), bias=17.0)
        cp("v", lst(-1, LCR, 16, V), R(p, 97, 192), bias=1.0 - H)
        p = tile("c1")
        mm([(R(p, 0, 2), [(R("sh"), R("wp", c, c + 192, 96)) for c in (0, 192)] + [(bv(15, k), R("wp", c, c + 2)) for c in (384, 386) for k in turns])])
        cp("v", lst(-1, LCL, 0, 16), R(p, 0, 1), bias=17.0)
        cp("v", lst(-1, LCR, 0, 16), R(p, 1, 2), bias=1.0 - H)
    for k in range(4):
        p = tile("t0")
        mm([(R(p, 96 * j, 96 * j + 96), [(bv(4 * k + j, kk), R("wp", c, c + 96)) for kk, c in parts]) for j in range(4)])
        for j in range(4):
            cp("s", R("tt", H + 4 * k + j, H + V, 16), R(p, 96 * j, 96 * j + 96), bias=ONE)
    p = R(tile("t1"), 0, 1)
    mm([(p, [(bv(15, 4 * j + k), R("wp", 384 + j, 385 + j)) for j in range(4) for k in turns])])
    cp("s", R("tt", H - 1, H), p, bias=ONE)

    def prepare(t):
        d = 1 if t % 2 == 0 else -1
        if t or not P["pe0"]:
            src, dst, gu = lst(t - 1, LL, 0, 2 * V), lst(t - 1, LCL, 0, 2 * V), R("gu", 2 * t, 2 * t + 2)
            i, c = (0, H - 1) if d > 0 else (15, H + V)
            p = tile("gu")
            mm([(R(p, j, j + 1), [(R("cs", e + 16 - i, e + 144 - i), R("tt", c, c + 1))]) for j, e in enumerate((EL, EN))])
            ts(gu, R(p, 0, 2), 16.0, float(H + V + 16), AL.add, AL.min)
            up, dn = int(d > 0), int(d < 0)
            dma("y", [(T.lu[a + up:b + up, dst[1]:dst[2]], T.lu[a + dn:b + dn, src[1]:src[2]]) for a, b in ((0, 112), (112, 127))], [src], [dst], 49152)
            pr = []
            for j in range(2):
                d0, s0, g0 = dst[1] + 96 * j, src[1] + 96 * j, dst[1] + 96 * j + 95 * dn
                pr += [(T.lu[i:128:16, d0 + up:d0 + up + 95], T.lu[15 - i:128:16, s0 + dn:s0 + dn + 95]), (T.lu[i:128:16, g0:g0 + 1], T.gu[i:128:16, gu[1] + j:gu[1] + j + 1])]
            ops[dma("y", pr, [src, gu], [dst], 4096)]["cost"] = ("d", 1, 16384)
            ts(dst, dst, float(d), None, AL.add)
        p = tile("cur")
        mm([(R(p, 32 * s, 32 * s + 32), [(blk("tt", s, H), c_(SC, 0, 1))]) for s in range(12)])
        cp(P["cur"], R("pb", 0, V, 4), R(p, 0, 384))
        p = tile("dif")
        mm([(R(p, 32 * s, 32 * s + 32), [(blk("tt", s, H - d), c_(SC, 0, 1)), (blk("tt", s, H), c_(SP if d > 0 else SN, 0, 1))]) for s in range(12)])
        return p

    def ypart(t):
        sc = abs(SCALE[t])
        for a, b, x in of("yy", t):
            p = R(tile("y"), 0, b - a)
            if t == 0 and P["r0"]:
                mm([(p, [(R("ident"), R("xb", a, b))])])
                tt(R("mf", a, b), p, R("ds", a, b), AL.mult)
            else:
                o = act(p, R("ds", a, b), AF.Exp, bias=-math.log(sc * (9.0 if SCALE[t] < 0 else 1.0)), scale=-1.0 / sc)
                ops[o]["behind"] += [warm, last[a // 128], last[(b - 1) // 128]]
                tt(R("mf", a, b), p, R("mf", a, b), AL.mult)
            if t == RO - 1 or P["y3"]:
                dma("g" if t else "y", [(T.ye[:, a:b], A(R("mf", a, b)))], [R("mf", a, b)], [R("ye", a, b)], 512 * (b - a), add=t > 0)
        if t < RO - 1 and not P["y3"]:
            dma("g" if t else "y", [(T.ye[:], A(R("mf")))], [R("mf")], [R("ye")], 786432, add=t > 0)

    dif = prepare(0)
    last = {}
    for t in range(RO):
        z, zc, dr, ma, mb, u = "z%d" % t, "zc" if t else "xb", "dr%d" % (t % 2), "ma", "mb", "u%d" % (t % 2)
        if t == 0 and P["r0"]:
            dr = "bm"

        def own(a=0, b=V):
            return R(z, ZO + H + a, ZO + H + b)
        pieces = of("ww", t)
        for a, b, x in of("u", t) if t >= PM else ():
            cp("s", R(u, H + a, H + b), own(a, b), scale=-9.0)
        tab, t0 = (z, ZO) if SCALE[t] > 0 else (u, 0)
        if SCALE[t] < 0:
            cp("s", R(u, 0, H), R(z, ZO, ZO + H), scale=-9.0)
        one = R("mvf", 128, 256) if t else R("ident")
        for side, d_, lc in (("R", dr, LR), ("L", "dl", LL)):
            nn = "n" + side.lower()
            for k, (a, b) in enumerate(x[:2] for x in of("cur" + side, t)):
                win = R(z, ZO + H, Z8) if side == "R" else R(z, 0, ZO + H + b)
                cur, can = lst(t - 1, lc, a, b), lst(t - 1, lc + LCL - LL, a, b)
                if side == "L" and t < P["prod"]:
                    x = of("prodL", t)[k]
                    ne, ce, p = R("g1" if t == 0 else "hg" if x == "v" else "dl", a, b), R("hc" if t else "g2", a, b), R(tile("pr"), 0, b - a)
                    o = gcp(ne, win, cur, x, -1.0)
                    gtt(ce, win, can, ne, AL.add)
                    sums(p, (one, own(a, b)), (R("hk", 128, 256) if ne[0] == "hg" else one, ne), (R("hk", 0, 128) if t else R("bk"), ce), ahead=o)
                    tt(R(nn, a, b), p, ce, AL.mult)
                    ts(R(nn, a, b), R(nn, a, b), 0.0, None, AL.is_gt)
                    continue
                for what, off in (("cur", cur), ("can", can)):
                    x = of(what + side, t)[k][2]
                    out = R(d_, a, b) if what == "cur" else R(d_, V + a, V + b)
                    keep = what == "cur" or d_ == "bm"
                    src, p = out, None
                    if x == "p":
                        got = out if t or d_ == "bm" else R("g2" if what == "cur" else "wb", a, b)
                        src = p = R(tile("sub"), 0, b - a)
                        sums(p, (one, own(a, b)), (one, got), ahead=gcp(got, win, off, "s", -1.0))
                        if side == "R" and not keep:
                            cp("s", out, p)
                    elif x == "s":
                        gcp(out, win, off, "s", -1.0)
                        dma("g", [(A(out), A(own(a, b)))], [own(a, b), out], [out], (256 if d_ == "bm" else 512) * (b - a), add=True)
                    else:
                        gtt(out, win, off, R(zc, a, b), AL.subtract)
                    if keep:
                        act(out, src, AF.Abs)
                        p = None
                    if what == "can":
                        p = p or R(tile("abs"), 0, b - a)
                        if keep:
                            mm([(p, [(one, out)])])
                        else:
                            act(p, src, AF.Abs)
                        tt(R(nn, a, b), p, R(d_, a, b), AL.is_lt)
        ll, lr = "ll%d" % t, "lr%d" % t
        done = {"R": set(), "L": set()}
        late = False
        for sides, a, b in of("dec", t):
            p = tile("cnt")
            mm([(R(p, 32 * s, 32 * s + 32), [(blk("n" + x.lower(), s), R("cs", QQ + (x == "L"), QQ + (x == "L") + 32)) for x in sides]) for s in range(a, b)])
            j, st = int(sides == "R"), 2 // len(sides)
            dec = R("pb", 128 * a + 4 * j + 2, 128 * b, 4 * st)
            ts(dec, R(p, 32 * a + j, 32 * b, st), 8.5, None, AL.is_gt)
            tt(R("pb", 128 * a + 4 * j + 1, 128 * b, 4 * st), R(dif, 32 * a + j, 32 * b, st), dec, AL.mult)
            before = {x: set(done[x]) for x in done}
            for x in sides:
                done[x].update(range(a, b))
            if {10, 11} <= done["R"] and not {10, 11} <= before["R"]:
                exchange([(right, R("pb", V - H, V), R(ll, 16 * rotr, 16 * rotr + H), R(ll, 16 * rotl, 16 * rotl + H))], 65536)
                late = t == 1 and 11 not in done["L"]
            elif late and 11 in done["L"] and 11 not in before["L"]:
                exchange([(right, blk("pb", 11), R("lx", 16 * rotr, 16 * rotr + 128), R("lx", 16 * rotl, 16 * rotl + 128))], 32768)
                if rotl:
                    wrap("lx", 0, 128, "l")
            if {0, 1} <= done["R"] & done["L"] and not {0, 1} <= before["R"] & before["L"]:
                exchange([(left, R("pb", 0, H), R(lr, 0, H), R(lr, 0, H))], 65536)
        if rotl:
            wrap(ll, 0, 128, "l")
            wrap(ll, 128, 256, "l")
        if rotr:
            wrap(lr, 256, 128, "r")
            wrap(lr, 128, 0, "r")
        HV = [x[:2] for x in of("hv", t)]
        for h, (a, b) in enumerate(HV):
            bs = range(a // 128, b // 128)
            p = tile("tt", B)
            tr([(blk(p, s - bs[0]), blk("pb", s)) for s in bs])
            cp(P["t"][1 + min(h, 1)], R("tt", H + a, H + b), R(p, 0, b - a))
            cp("v", lst(t, LL, a, b), ext("ll", EL, "tt", H, a, b), bias=16.0)
        cp("v", lst(t, LR), ext("lr", ER, "tt", H), bias=-float(H))
        cp("v", lst(t, LD), ext("ld", ED, "tt", H), bias=-float(H))
        if t:
            ypart(t - 1)
        for a, b, x in of("ds", t):
            if dr == "bm":
                ops[act(R("ds", a, b), R(dr), AF.Exp, scale=-1.0, off=lst(t, LD, a, b))]["behind"].append(warm)
            else:
                act(R("ds", a, b), R(dr), AF.Abs, off=lst(t, LD, a, b))
        g1, got = of("g1", t), {}
        for y in ([g1[1], None, g1[0]] + g1[2:] if g1[0][1] == H else [None] + g1):
            if y is None:
                p = tile("gl", B)
                tr([(blk(p, s), blk(ll, s)) for s in range(2)])
                cp(P["t"][0], R("tt", 0, H), R(p, 0, H), bias=BM)
                continue
            a, b, x = y
            o = gcp(R("g1", a, b), R("tt", -16, H + b), lst(t, LL, a, b), x)
            got.update((s, o) for s in range(a // 128, b // 128))
        for h, (a, b) in enumerate(HV):
            for c in range(a, b, 512):
                e = min(b, c + 512)
                p = R(tile("ch"), 0, e - c)
                sums(p, (R("wk", 0, 128), R("tt", H + c, H + e)), (R("wk", 128, 256), R("g1", c, e)), ahead=got[c // 128])
                ts(R("a1", H + c, H + e), p, LO, UP, AL.max, AL.min)
        ghosts = False
        for a, b, x in of("g2", t):
            if b > V - H and not ghosts:
                p = tile("gr", B)
                tr([(blk(p, s), blk(lr, s, 16 * rotr)) for s in range(2)])
                cp(P["t"][3], R("tt", H + V, W), R(p, 0, H), bias=BP)
                ghosts = True
            gcp(R("g2", a, b), R("tt", H, W), lst(t, LR, a, b), x)
        if late:
            p = tile("lx", B)
            tr([(blk(p, 0), blk("lx", 0))])
            cp("s", R("tt", H - 1, H), R(p, 127, 128), bias=BM)
        twin(R(z, Z8, Z8 + H), R(z, ZO, ZO + H))
        gh = R(tab, t0, t0 + H)
        if t:
            dma("y", [(A(R(m_, 0, H)), A(gh)) for m_ in (ma, mb)], [gh], [R(ma, 0, H), R(mb, 0, H)], 262144)
        else:
            dma("g", [(A(R(m_, 0, H)), A(gh)) for m_ in (ma, mb)], [gh], [R(ma, 0, H), R(mb, 0, H)], 262144)
        if SCALE[t] < 0:
            twin(R("mc0"), R(u, H, H + V))
        src = [(tab, t0), (ma, 0), (mb, 0), (ma, 0)]
        dst = [(ma, H), (mb, H), (ma, H), ("xb" if dr == "bm" else "mf", 0)]
        tabs = [("a1", H), ("a2", H), ("a4", H), ("a8", 0), (z, Z8 + H)]
        for k in range(4):
            def small(a, b):
                return [R(nn, c0 + a // 16, c0 + b // 16) for nn, c0 in (("sm", 0), ("sm", 96), ("sm", 192), ("vw", 0))]
            if k == 1:
                for a, b, x in of("go", t):
                    act(small(a, b)[1], ext("qq", EL, "g2", 0, a, b, [(R("ident"), R("vn", a // 16, b // 16))]), AF.Abs, bias=KQ, scale=4096.0)
            for a, b, x in P.get("x%d" % k, of("hv", t)):
                p = ext("a%d" % k, EA, tabs[k][0], tabs[k][1], a, b)
                cp("v", lst(t, LA1 + 96 * k, a, b), p)
                a2, qq, pp, vc = small(a, b)
                if k == 1:
                    cp("s", a2, p)
                if k == 2:
                    tt(pp, a2, p, AL.subtract)
                if k == 3:
                    tt(a2, p, pp, AL.min)
                    ts(lst(t, LS, a, b), a2, float(Z8 - ZO), None, AL.add)
            if k == 2:
                for a, b, x in of("go", t):
                    a2, qq, pp, vc = small(a, b)
                    tt(pp, pp, qq, AL.mult)
                    tt(pp, pp, vc, AL.add)
            nn, c0 = tabs[k + 1]
            for a, b, x in of(("a2", "a4", "a8", "z8")[k], t):
                win = R(tabs[k][0], 0, H + b) if k < 3 else R(z, ZO, ZO + H + b)
                gcp(R(nn, c0 + a, c0 + b), win, lst(t, LA1 + 96 * k, a, b), x)
            sn, s_ = src[k]
            dn, d_ = dst[k]
            cn = zc if k == 0 and SCALE[t] > 0 else "mc%d" % (k % 2)
            for a, b, x in of("mc", t):
                o = gtt(R(dn, d_ + a, d_ + b), R(sn, s_, s_ + H + b), lst(t, LA1 + 96 * k, a, b), R(cn, a, b), AL.max)
                last.update((s, o) for s in range(a // 128, b // 128))
                if k < 3:
                    twin(R("mc%d" % (1 - k % 2), a, b), R(dn, d_ + a, d_ + b), of("tw", t)[k])
        if t < RO - 1:
            dif = prepare(t + 1)
        nz, mv_ = "z%d" % (t + 1), "mv%d" % t if t < PM else "mvf"
        lo, hi = sorted((0.0, 4.0 * SCALE[t + 1]))

        def move(out, a, b, x, o):
            p = R(ww, a, b)
            if x in "pq":
                p = R(tile("mv"), 0, b - a)
                sums(p, (R(mv_, 0, 128), own(a, b)), (R("hk", 256, 384) if ww == "hg" else R(mv_, 128, 256), R(ww, a, b)), ahead=o)
            top = R("col", 8 + t // 2, 9 + t // 2)

            def on_s():
                first = ops.pop(act(p, p, AF.Relu, bias=top, scale=-1.0))
                o = act(out, p, AF.Relu, bias=top, scale=-1.0)
                ops[o].update(first=first["fn"], cost=("e", 2 * cnt(p) + 160))
                return o
            if lo < 0:
                return ts(out, p, lo, hi, AL.max, AL.min)
            o = either("s" if x == "c" else "v", lambda: ts(out, p, lo, hi, AL.max, AL.min), on_s)
            ops[o].update(rd=[p, top], wr=[out, p])
        if lo == 0:
            ms(R("col", 8 + t // 2, 9 + t // 2), hi)
        for a, b, x in pieces:
            win, off, ww = R(z, ZO, Z8 + H + b), lst(t, LS, a, b), "wb" if t == 0 else "hg" if t == 1 < PM and x == "q" else "ww"
            if x in "pqs":
                o = gcp(R(ww, a, b), win, off, "v" if x == "q" else "s")
                if x == "s":
                    dma("g", [(A(R(ww, a, b)), A(R(u, H + a, H + b)))], [R(u, H + a, H + b), R(ww, a, b)], [R(ww, a, b)], 512 * (b - a), add=True)
            else:
                o = gtt(R(ww, a, b), win, off, R(u, H + a, H + b), AL.add)
            if t == RO - 1:
                move(R("z1", a, b), a, b, x, o)
                dma("y", [(T.xe[:, a:b], A(R("z1", a, b)))], [R("z1", a, b)], [R("xe", a, b)], 512 * (b - a))
                continue
            first, end = R(nz, ZO + H, ZO + 2 * H), R(nz, ZO + V, ZO + V + H)
            turn = [("l", 0, 0, 16, first)] * (a == 0 and rotl) + [("r", H, V - H, 112, end)] * (b == V and rotr)
            move(R(nz, ZO + H + a, ZO + H + b), a, b, x, o)
            for only[0], c, e, k, new in turn:
                p = R(tile("xs"), 0, H)
                mm([(p, [(R("mvf", 128 + k, 256 + k), new)])])
                cp(of("xs", t), R("xs", c, c + H), p)
            only[0] = None
            twin(R("zc", a, b), R(nz, ZO + H + a, ZO + H + b), of("tz", t)[pieces.index((a, b, x))])
            gl_, gr_ = R(nz, ZO, ZO + H), R(nz, ZO + H + V, ZO + W)
            if a == 0:
                exchange([(left, R("xs", 0, H) if rotl else first, gr_, gr_)], 131072, [first])
            if b == V:
                exchange([(right, R("xs", H, 2 * H) if rotr else end, gl_, gl_)], 131072, [end])
    ypart(RO - 1)
    return ops, tiles, place


def bits(r):
    m = np.zeros(4864, np.uint8)
    m[r[1]:r[2]:r[3]] = 1
    return int.from_bytes(np.packbits(m).tobytes(), "big")


def depend(ops):
    hist = {}
    memo = {}
    deps = []
    above = []
    for i, o in enumerate(ops):
        d = set(o["after"])
        new = []
        for lst_, w in ((o["rd"], False), (o["wr"], True)):
            for r in lst_:
                if r[1:] not in memo:
                    memo[r[1:]] = bits(r)
                m = memo[r[1:]]
                for j, wj, mj in hist.get(r[0], ()):
                    if (w or wj) and (m & mj):
                        d.add(j)
                new.append((r[0], w, m))
        for name, w, m in new:
            h = hist.setdefault(name, [])
            if w:
                h[:] = [(j, wj, mj & ~m) for j, wj, mj in h if mj & ~m]
            h.append((i, w, m))
        d.discard(i)
        far = 0
        for j in d:
            far |= above[j]
        deps.append(sorted(j for j in d if not far >> j & 1))
        above.append(far | sum(1 << j for j in d))
    return deps


def times(o, m):
    c, x = o["cost"], o["once"]
    if c[0] == "e":
        x += 0.06 + max(64, c[1]) * m["c"]
    elif c[0] == "g":
        x += 0.06 + c[1] * m["g"] * m["c"]
    elif c[0] == "q":
        x += 0.17 + 2 * c[1] * m["c"]
    elif c[0] == "p":
        x += 0.05 + c[1] * m["pe"]
    elif c[0] == "d":
        i = x + c[1] * (1.0 if o["e"] == "g" else 0.1)
        x = 8 * c[1] * m["row"] + c[2] / 610000.0
        return i, i + 1.7 + x, x
    elif c[0] == "r":
        return x + 0.6, x + 0.6 + m["rem"] * 0.5 + c[1] / 150000.0, 8 * m["row"] + c[1] / 400000.0
    else:
        return 0.0, m["rem"] * 0.5, 0.0
    return x, x, 0.0


def land(s, d, busy):
    x = max(s + d[1] - 0.7 - d[2], busy[0]) + d[2]
    busy[0] = x
    return x + 0.7


def facts(ops, tiles):
    n, deps, ms_ = len(ops), depend(ops), models()
    num = {x: k for k, x in enumerate(tiles)}
    tl = [sorted({num[r[0]] for r in o["rd"] + o["wr"] if r[0] in num}) for o in ops]
    opens, uses = [-1] * n, [0] * len(num)
    for i in range(n):
        for x in tl[i]:
            if not uses[x]:
                opens[i] = x
            uses[x] += 1
    succ, ahead = [[] for o in ops], [[] for o in ops]
    for i in range(n):
        for j in deps[i]:
            succ[j].append(i)
        for j in ops[i]["behind"]:
            ahead[j].append(i)
    return {"n": n, "deps": deps, "succ": succ, "behind": [o["behind"] for o in ops], "ahead": ahead, "tl": tl, "opens": opens, "uses": uses,
            "pool": [int(tiles[x][1] == B) for x in tiles], "eng": [QUEUES.index(o["e"]) for o in ops],
            "alt": [o["alt"] and [[times(o["alt"], m)] for m in ms_] for o in ops],
            "dma": [o["k"] in "ds" for o in ops], "dur": [[times(o, m) for o in ops] for m in ms_], "lat": [m["lat"] for m in ms_], "w": [m["w"] for m in ms_]}


def follow(pre, order, mark=None, known=None, marks=None):
    free, left, bank = [list(range(NF)), list(range(NF, NF + NB))], pre["uses"], [0] * len(pre["uses"])
    last, tl, opens, eng, pool, deps = [[-1] * 6 for b in range(NF + NB)], pre["tl"], pre["opens"], pre["eng"], pre["pool"], pre["deps"]
    if mark:
        free, left, bank, last = mark
    free, left, bank, last, waits = [list(x) for x in free], list(left), list(bank), [list(x) for x in last], list(known or deps)
    for p, i in enumerate(order):
        if marks is not None and p % 16 == 0:
            marks.append(([list(x) for x in free], list(left), list(bank), [list(x) for x in last]))
        if tl[i]:
            x, e, t = [], eng[i], opens[i]
            if t >= 0:
                if not free[pool[t]]:
                    return None, None
                b = bank[t] = free[pool[t]].pop(0)
                x = [j for j in last[b] if j >= 0]
                last[b] = [-1] * 6
            for t in tl[i]:
                l = last[bank[t]]
                x += [j for j in l if j >= 0 and eng[j] != e]
                l[e] = i
                left[t] -= 1
                if not left[t]:
                    free[pool[t]].append(bank[t])
            waits[i] = deps[i] + x
    return waits, bank


def plan(pre, pr, slack, back=False):
    eng, dur, lat, n, tl, opens, pool = pre["eng"], pre["dur"][0], pre["lat"][0], pre["n"], pre["tl"], pre["opens"], pre["pool"]
    succ, then = (pre["deps"], pre["behind"]) if back else (pre["succ"], pre["ahead"])
    left = [len(pre["succ"][i]) + len(pre["ahead"][i]) if back else len(pre["deps"][i]) + len(pre["behind"][i]) for i in range(n)]
    ready = [[i for i in range(n) if not left[i] and eng[i] == e] for e in range(6)]
    rdy, fin, est, free = [0.0] * n, [0.0] * n, [0.0] * n, [0.0] * 6
    banks, uses, bank = [list(range(NF)), list(range(NF, NF + NB))], list(pre["uses"]), [0] * len(pre["uses"])
    last = [[0.0] * 6 for b in range(NF + NB)]
    order, busy = [], [0.0]
    for step in range(n):
        b0, e0 = 1e9, -1
        for e in range(6):
            f = free[e]
            for i in ready[e]:
                s = rdy[i]
                x = f - dur[i][1] + dur[i][0] if back else f
                if x > s:
                    s = x
                if tl[i] and not back:
                    t = opens[i]
                    if t >= 0:
                        if not banks[pool[t]]:
                            est[i] = 2e9
                            continue
                        s = max(s, max(last[banks[pool[t]][0]]))
                    for y in tl[i]:
                        if y != t:
                            for k, x in enumerate(last[bank[y]]):
                                if x > s and k != e:
                                    s = x
                est[i] = s
                if s < b0:
                    b0, e0 = s, e
        if e0 < 0:
            return None, None
        i, p = -1, -1e9
        for j in ready[e0]:
            if est[j] <= b0 + slack[j] and pr[j] > p:
                i, p = j, pr[j]
        if e0:
            free[e0] = est[i] + dur[i][1 if back else 0]
        fin[i] = land(est[i], dur[i], busy) if dur[i][2] and not back else est[i] + dur[i][1]
        order.append(i)
        ready[e0].remove(i)
        x = fin[i] + lat
        if tl[i] and not back:
            if opens[i] >= 0:
                bank[opens[i]] = banks[pool[opens[i]]].pop(0)
            for y in tl[i]:
                last[bank[y]][e0] = x
                uses[y] -= 1
                if not uses[y]:
                    banks[pool[y]].append(bank[y])
        for j in succ[i]:
            if x > rdy[j]:
                rdy[j] = x
        for j in succ[i] + then[i]:
            left[j] -= 1
            if not left[j]:
                ready[eng[j]].append(j)
    return order, fin


def replay(pre, waits, order, k, old=None, a=0):
    eng, dur, lat = pre["eng"], pre["dur"][k], pre["lat"][k]
    free, busy = [0.0] * 6, 0.0
    st, fin = (list(old[0]), list(old[1])) if old else ([0.0] * pre["n"], [0.0] * pre["n"])
    need = {1, 2, 3, 4, 5, 6}
    for p in range(a - 1, -1, -1):
        i = order[p]
        if eng[i] in need:
            need.discard(eng[i])
            free[eng[i]] = st[i] + dur[i][0]
        if dur[i][2] and 6 in need:
            need.discard(6)
            busy = fin[i] - 0.7 - lat
        if not need:
            break
    for i in order[a:]:
        e = eng[i]
        s = free[e]
        for j in waits[i]:
            if fin[j] > s:
                s = fin[j]
        st[i] = s
        q, c, d = dur[i]
        if e:
            free[e] = s + q
        if d:
            x = s + c - 0.7 - d
            busy = (x if x > busy else busy) + d
            fin[i] = busy + 0.7 + lat
        else:
            fin[i] = s + c + lat
    return st, fin


def held(pre, waits, before, times_):
    st, fin = times_
    i, out = fin.index(max(fin)), []
    while st[i] > 0:
        j = [j for j in waits[i] if fin[j] == st[i]]
        j = j[0] if j else before[i]
        if j not in pre["deps"][i]:
            out.append((j, i))
        i = j
    return out


def kind(o, tiles):
    r = (o["wr"] or o["rd"])[0]
    q = (o["rd"] or o["wr"])[-1 if o["e"] == "p" else 0]
    return (o["e"], o["cost"]) + tuple((tiles[x[0]][0] if x[0] in tiles else x[0].rstrip("0123") if x[0][0] in "zudl" else x[0],
                                        x[1] % 960 if x[0] == "lu" else x[1]) for x in (r, q))


def arrange(ops, tiles):
    pre = facts(ops, tiles)
    n, deps, nm = pre["n"], pre["deps"], len(pre["w"])
    names = {}
    kinds = np.array([names.setdefault(kind(o, tiles), len(names)) for o in ops])
    rng = np.random.default_rng(SEED)
    level = [0.0] * n
    for i in range(n - 1, -1, -1):
        level[i] += pre["dur"][0][i][1] + pre["lat"][0]
        for j in deps[i] + pre["behind"][i]:
            level[j] = max(level[j], level[i])

    def score(order, cur=None, more=0.0, a=0):
        marks = cur[6][:a // 16] if a else []
        waits = follow(pre, order[a - a % 16:], cur[6][a // 16], cur[2], marks)[0] if a else follow(pre, order, None, None, marks)[0]
        if waits is None:
            return None
        ts_, x, all_ = [], 0.0, []
        for k in range(nm):
            all_.append(replay(pre, waits, order, k, cur[5][k] if a else None, a))
            ts_.append(max(all_[k][1]))
            x += ts_[k] / pre["w"][k]
            if cur:
                more -= (ts_[k] - cur[3][k] + SOON * (sum(all_[k][1]) - sum(cur[5][k][1]))) / pre["w"][k]
                if more + HOPE * (nm - 1 - k) < 0:
                    return None
        return [x, order, waits, ts_, None, all_, marks]

    def links(cur):
        if cur[4] is None:
            cur[4] = ahead_of(pre, cur)[6]
        return cur[4][int(rng.integers(len(cur[4])))]
    best, fin, keep = None, None, None
    for k in range(TRIES):
        if k < 32 or best is None:
            slack = np.full(n, [0.1, 0.2, 0.35, 0.5][(k // 8) % 4])
            rank = np.array(level if k % 8 == 0 or fin is None else plan(pre, fin, slack.tolist(), True)[1])
        else:
            rank, slack = keep[0].copy(), keep[1].copy()
            if k % 2:
                j, i = links(best)
                gap = max(rank[j] - rank[i], 0.0) + float(rng.choice([0.05, 0.3, 1.0]))
                up = rng.random() < 0.5
                who = i if up else j
                pick = (kinds == kinds[who]) if rng.random() < 0.6 else (np.arange(n) == who)
                rank[pick] += gap if up else -gap
                pick = (kinds == kinds[i]) if pick.sum() > 1 else (np.arange(n) == i)
                slack[pick] = np.maximum(slack[pick], float(rng.choice([0.2, 0.5, 1.0])))
            elif k % 3:
                pick = np.isin(kinds, rng.choice(kinds[n // 3:], int(rng.choice([1, 2, 4]))))
                rank[pick] += rng.normal(0.0, float(rng.choice([0.5, 1.5, 4.0])), len(names))[kinds][pick]
                slack[pick] = rng.choice([0.05, 0.2, 0.5, 1.0], len(names))[kinds][pick]
            else:
                pick = (rng.random(n) < 0.3) & (np.abs(np.arange(n) - int(rng.integers(0, n))) < int(rng.choice([5, 20, 60])))
                rank[pick] += rng.normal(0.0, float(rng.choice([0.3, 1.0, 3.0])), n)[pick]
                slack[pick] = rng.choice([0.05, 0.2, 0.5, 1.0], n)[pick]
        order, fin = plan(pre, rank.tolist(), slack.tolist())
        new = order and score(order, best)
        if new:
            best, keep = new, (rank, slack)
    anc = []
    for i in range(n):
        a = 0
        for j in deps[i] + pre["behind"][i]:
            a |= anc[j] | 1 << j
        anc.append(a)
    cur, eng, w = best, pre["eng"], pre["w"]
    aid, taken, kept = ahead_of(pre, cur), 0, list(eng)
    draw, heat = rng.random((SWAPS, 4)).tolist(), rng.exponential(size=SWAPS).tolist()
    for k in range(SWAPS):
        if k % 1000 == 0:
            key = list(cur[5][0][0])
            for i in cur[1]:
                key[i] = max([key[i]] + [key[j] for j in pre["behind"][i]])
            new = score(sorted(cur[1], key=lambda i: key[i]), cur, 0.3)
            if new:
                cur, aid = new, ahead_of(pre, new)
        order, (pos, before, after, marks, succ, tails, pairs), (r0, r1, r2, r3) = cur[1], aid, draw[k]
        j, i = pairs[int(r0 * len(pairs))]
        if r1 < NEAR:
            i = j = order[min(n - 1, max(0, pos[i] + int((r0 * 977 % 1 - 0.5) * 60)))]
            j = before[i]
        other = [x for x in (i, j) if x >= 0 and pre["alt"][x]] if r1 * 991 % 1 < FLIP else []
        if other:
            other = other[int(r3 * len(other))]
            flip(pre, other)
            a = pos[other]
            b = a + 1
            part = [other]
        else:
            other = -1
            while r2 < FAR and j >= 0:
                j, r2 = before[j], r2 / FAR
            if j < 0 or anc[i] >> j & 1 or pos[j] > pos[i]:
                continue
            a, b = pos[j], pos[i] + 1
            m = anc[i] | 1 << i
            if r3 < 0.5:
                part = [x for x in order[a:b] if m >> x & 1] + [x for x in order[a:b] if not m >> x & 1]
            else:
                part = [x for x in order[a:b] if x != j and not anc[x] >> j & 1] + [x for x in order[a:b] if x == j or anc[x] >> j & 1]
        c = min(n, b + REACH)
        part += order[b:c]
        a0 = a - a % 16
        waits = follow(pre, order[a0:a] + part, marks[a0 // 16], cur[2])[0]
        new = None
        if waits:
            more = left = HEAT * (1.0 - k / SWAPS) * heat[k]
            last, need = [-1] * 6, {eng[x] for x in part} - {0}
            p = a - 1
            while need and p >= 0:
                if eng[order[p]] in need:
                    need.discard(eng[order[p]])
                    last[eng[order[p]]] = order[p]
                p -= 1
            for y in range(nm):
                left -= guess(pre, y, cur, aid, waits, part, a, c, last) / w[y]
                if left + HOPE * (nm - 1 - y) < 0:
                    break
            else:
                new = score(order[:a] + part + order[c:], cur, more, a)
        if new:
            taken += 1
            cur, aid = new, ahead_of(pre, new, aid if taken % LAZY and other < 0 else None)
            if new[0] < best[0]:
                best, kept = new, list(eng)
        elif other >= 0:
            flip(pre, other)
    for i in range(n):
        if eng[i] != kept[i]:
            flip(pre, i)
    return pre, best


def flip(pre, i):
    pre["eng"][i] = 3 - pre["eng"][i]
    for dur, alt in zip(pre["dur"], pre["alt"][i]):
        dur[i], alt[0] = alt[0], dur[i]


def ahead_of(pre, cur, old=None):
    order, waits, n, eng, marks = cur[1], cur[2], pre["n"], pre["eng"], cur[6]
    pos, before, last, succ = [0] * n, [-1] * n, [-1] * 6, [[] for i in range(n)]
    for p, i in enumerate(order):
        e = eng[i]
        pos[i], before[i], last[e] = p, last[e], i
    tails, dmas = [], [i for i in order if pre["dma"][i]]
    if old:
        return (pos, before, dmas, marks) + old[4:]
    for i in order:
        for j in waits[i]:
            succ[j].append(i)
    for k in range(len(pre["w"])):
        dur, lat = pre["dur"][k], pre["lat"][k]
        ts_, tf, nxt, dma = [0.0] * n, [0.0] * n, [0.0] * 6, 0.0
        for i in reversed(order):
            q, c, d = dur[i]
            f = tf[i]
            if d:
                if dma > f:
                    f = tf[i] = dma
                dma = f + d
            s, e = f + c + lat, eng[i]
            if e:
                if nxt[e] + q > s:
                    s = nxt[e] + q
                nxt[e] = s
            ts_[i] = s
            for j in waits[i]:
                if s > tf[j]:
                    tf[j] = s
        tails.append((ts_, tf))
    pairs = [x for k in range(len(pre["w"])) for x in held(pre, waits, before, cur[5][k])]
    return pos, before, dmas, marks, succ, tails, pairs


def guess(pre, k, cur, aid, waits, part, a, c, last):
    pos, before, dmas, marks, succ, tails, pairs = aid
    eng, dur, lat, (st, old), (ts_, tf), order = pre["eng"], pre["dur"][k], pre["lat"][k], cur[5][k], tails[k], cur[1]
    free, fin, busy, end, shift = [0.0] * 6, {}, -1.0, 0.0, 0.0
    for e in range(1, 6):
        if last[e] >= 0:
            free[e] = st[last[e]] + dur[last[e]][0]
    for i in part:
        e = eng[i]
        s = free[e]
        for j in waits[i]:
            x = fin[j] if j in fin else old[j]
            if x > s:
                s = x
        q, t, d = dur[i]
        if e:
            free[e] = s + q
        if d:
            if busy < 0:
                busy = max([old[j] - 0.7 - lat for j in dmas if pos[j] < a][-1:] + [0.0])
            x = s + t - 0.7 - d
            busy = (x if x > busy else busy) + d
            x = busy + 0.7 + lat
        else:
            x = s + t + lat
        fin[i] = x
        shift += x - old[i]
        if x > end:
            end = x
        for j in succ[i]:
            if pos[j] >= c and x + ts_[j] > end:
                end = x + ts_[j]
    need = {eng[i] for i in part} - {0}
    for j in order[c:c + 60]:
        if eng[j] in need:
            need.discard(eng[j])
            end = max(end, free[eng[j]] + ts_[j])
        if busy >= 0 and dur[j][2]:
            end, busy = max(end, busy + dur[j][2] + 0.7 + lat + tf[j]), -1.0
    return max(end - cur[3][k], -0.3) + EASE * shift


def ordered(core, T, topo):
    if not PLANS:
        ops, tiles, place = build(core, T, topo, True)
        pre, best = arrange(ops, tiles)
        PLANS["order"], PLANS["only"], PLANS["eng"] = best[1], [o["only"] for o in ops], [QUEUES[e] for e in pre["eng"]]
    rank = T.rank_of(core)
    mine = [None] + ["l"] * (rank == 0) + ["r"] * (rank == len(T.cores) - 1)
    num = {}
    for i, x in enumerate(PLANS["only"]):
        if x in mine:
            num[i] = len(num)
    order = [num[i] for i in PLANS["order"] if i in num]
    ops, tiles, place = build(core, T, topo)
    for i, k in num.items():
        if ops[k]["e"] != PLANS["eng"][i]:
            ops[k].update((x, ops[k]["alt"][x]) for x in ("e", "fn", "cost", "first"))
    waits, bank = follow(facts(ops, tiles), order)
    for x, b in zip(tiles, bank):
        place[x] = ("ps", 512 * b) if b < NF else ("pt", 1024 * (b - NF))
    return ops, order, waits


def rank_program(g, core, T, topo):
    if T.rank_of(core) is None:
        return
    ops, order, waits = ordered(core, T, topo)
    Q = {"v": g.vector, "s": g.scalar, "p": g.tensor, "g": g, "y": g.sync}
    known = {e: {} for e in Q}
    total = {}
    tok = {}
    clock = {}
    for i in order:
        o = ops[i]
        e = o["e"]
        if o["k"] == "a":
            tok[i] = (o["sem"], o["val"])
            total[o["sem"]] = o["val"]
            clock[i] = {o["sem"]: o["val"]}
            continue
        kn = known[e]
        need = {}
        for j in sorted(set(waits[i]), key=lambda j: -len(clock[j])):
            s, v = tok[j]
            if kn.get(s, 0) < v:
                need[s] = max(need.get(s, 0), v)
                for s2, v2 in clock[j].items():
                    if kn.get(s2, 0) < v2:
                        kn[s2] = v2
        for s, v in need.items():
            Q[e].wait_ge(T.sem[s], v)
        s = "e" + e
        if o["first"]:
            o["first"](Q[e])[0].then_inc(T.sem[s], 1)
            total[s] = kn[s] = total.get(s, 0) + 1
            Q[e].wait_ge(T.sem[s], total[s])
        ins = o["fn"](Q[e])
        if o["k"] == "c":
            for x in ins:
                x.then_inc(T.sem[s], 1)
            total[s] = total.get(s, 0) + len(ins)
            tok[i] = (s, total[s])
        else:
            for x in ins:
                x.then_inc(T.sem[o["sem"]], 16)
            total[o["sem"]] = o["val"]
            tok[i] = (o["sem"], o["val"])
        clock[i] = dict(kn)
        clock[i][tok[i][0]] = tok[i][1]
    for s, v in total.items():
        if known["g"].get(s, 0) < v:
            g.wait_ge(T.sem[s], v)
